import numpy as np, ml_dtypes
CORES = [24,48,72,152,176,200]
N = 6
BF = ml_dtypes.bfloat16
W, L, Q, RO, FU, SB, SC = 2048, 128, 512, 3, 6, 1, 4
def pack(sect, mv, traj, amt, cap):
    return {"sect": np.ascontiguousarray(sect.reshape(N, 128, W)).astype(np.float32).astype(BF), "mv": np.ascontiguousarray(mv.reshape(N, 128, Q)).astype(np.int32),
            "traj": np.ascontiguousarray(traj.reshape(N, 128, L)).astype(np.int32), "amt": np.ascontiguousarray(amt.reshape(N, 128, L)).astype(np.float32).astype(BF),
            "cap": np.ascontiguousarray(cap.reshape(N, 128, 1)).astype(np.int32)}
def parts(rng):
    sect = (rng.random((N, 8, 16, W)) * 256 * rng.choice(np.array([0.5, 0.75, 1.0]), (N, 8, 1, W))).astype(np.int64)
    mv = rng.integers(0, W, (N, 8, 16, Q)); traj = rng.integers(0, W, (N, 8, 16, L))
    amt = (rng.random((N, 8, 16, L)) * rng.choice(np.array([8, 40, 100, 170, 256]), (N, 8, 1, L))).astype(np.int64)
    return sect, mv, traj, amt, rng.integers(230, 331, (N, 8, 16, 1))
def setup_inputs(rng):
    return pack(*parts(rng))
def setup_inputs_spread(rng):
    sect, mv, traj, amt, cap = parts(rng)
    sect = (np.exp2(3 + 5 * rng.random((N, 8, 1, W))) * rng.random((N, 8, 16, W))).astype(np.int64)
    amt = (np.exp2(4 + 4 * rng.random((N, 8, 1, L))) * rng.random((N, 8, 16, L))).astype(np.int64)
    traj = (W * rng.random((N, 8, 16, L)) ** 3).astype(np.int64); mv = (W * rng.random((N, 8, 16, Q)) ** 2).astype(np.int64)
    return pack(sect, mv, traj, amt, rng.integers(160, 401, (N, 8, 16, 1)))
def endmix(rng, n, top):
    k = rng.integers(0, 3, (N, 8, 1, n)); e = rng.integers(0, 2, (N, 8, 16, n))
    return top * np.where(k == 2, e, k)
def setup_inputs_ends(rng):
    sect = endmix(rng, W, 255); amt = endmix(rng, L, 255); mv = endmix(rng, Q, W - 1); traj = (W - 1) * rng.integers(0, 2, (N, 8, 16, L))
    cap = 160 + 240 * rng.integers(0, 2, (N, 8, 16, 1)); cap[:, 0] = 400; cap[:, 6:] = 160
    sect[:, 6, :, 0] = 255; sect[:, 6, :, W - 1] = 255; sect[:, 7, :, 0] = 0; sect[:, 7, :, W - 1] = 255
    amt[:, 6:, :, L - 2:] = 255; amt[:, 6:, :, 0] = 255; amt[:, 6:, :, 1] = 0
    traj[:, 6:, 0, L - 1] = 0; traj[:, 6:, 3, L - 1] = W - 1; traj[:, 6:, 13:, L - 1] = W - 1
    traj[:, 7, :15, L - 2] = 0; traj[:, 7, 15, L - 2] = W - 1; traj[:, 7, :, 1] = 0
    return pack(sect, mv, traj, amt, cap)
def setup_inputs_corners(rng):
    sect, mv, traj, amt, cap = parts(rng)
    c0 = rng.integers(160, 401, (1, 8, 16, 1)); c0[0, 0, 0] = 160; c0[0, 7, 15] = 400
    lo = np.maximum(c0 - 255, 0); hi = np.minimum(c0, 254)
    x0 = lo + (rng.random(c0.shape) * (hi - lo + 1)).astype(np.int64)
    cls = np.arange(W) % 4
    n1 = rng.choice(np.array([FU, FU + 1, 16]), (N, 8, 1, W)); n2 = rng.choice(np.array([0, FU - 1, FU, FU + 1, 16]), (N, 8, 1, W))
    n = np.where(cls == 0, 0, np.where(cls == 1, n1, n2))
    sh = rng.integers(0, 16, (N, 8, 1, W)) * rng.integers(0, 2, (N, 8, 1, W))
    over = (np.arange(16).reshape(1, 1, 16, 1) + sh) % 16 < n
    up = rng.integers(0, 3, (N, 8, 1, W)) * rng.integers(0, 2, (N, 8, 1, W))
    sect = np.where(over, np.minimum(x0 + 1 + up, 255), np.maximum(x0 - up, 0))
    kind = rng.integers(0, 6, (N, 8, 1, L)); kind[..., 0] = 1; kind[..., L - 1] = 2; kind[..., L - 2] = 5
    k = np.arange(16).reshape(1, 1, 16, 1); one = np.ones((N, 8, 16, L), np.int64)
    cl = np.where(kind == 0, 0 * one, np.where(kind == 1, one * (k == 0), np.where(kind == 2, one * (k == 15), np.where(kind == 3, rng.integers(2, 4, one.shape), np.where(kind == 4, rng.integers(0, 4, one.shape), one)))))
    traj = 4 * rng.integers(0, W // 4, (N, 8, 16, L)) + cl
    amt = np.where(kind == 4, amt, c0 - x0)
    mv[..., ::5] = (W - 1) * rng.integers(0, 2, mv[..., ::5].shape)
    return pack(sect, mv, traj, amt, np.broadcast_to(c0, (N, 8, 16, 1)))
def setup_inputs_crowd(rng):
    sect, mv, traj, amt, cap = parts(rng)
    for g in (0, 1, 2):
        sect[:, g] = rng.integers(200, 256, (N, 16, W)); amt[:, g] = rng.integers(170, 256, (N, 16, L))
    cap[:, 1] = rng.integers(300, 331, (N, 16, 1))
    pl = rng.integers(0, W, (N, 8, 1, 1)); pl[0, 0] = W - 1; pl[1, 0] = 0; traj[:, :4] = pl[:, :4]
    few = np.array([0, W - 1, W // 2, 3])
    traj[:, 4] = few[rng.integers(0, 4, (N, 16, L))]; mv[:, 4] = few[rng.integers(0, 4, (N, 16, Q))]
    traj[:, 5] = rng.integers(0, W, (N, 16, 1))
    for q in range(N):
        v = int(rng.integers(0, L)); amt[q, 1, :, v] = 0
        traj[q, 2:4, :, v] = (pl[q, 2:4, 0] + 1 + rng.integers(0, W - 1, (2, 16))) % W
        traj[q, 6] = rng.permutation(W)[:L][None, :]
    return pack(sect, mv, traj, amt, cap)
def setup_inputs_fine(rng):
    sect, mv, traj, amt, cap = parts(rng); o = rng.permutation(8); w4 = W >> 2
    for n, (base, e, share) in enumerate(((215, 20, 0.4), (240, 12, 0.4), (247, 6, 0.1))):
        g = int(o[n]); h = rng.integers(-e, e + 1, (N, 8, W)); x = np.concatenate([base + h, base - h], axis=1)
        x[:, 0] += rng.integers(1, 3, (N, W)) * (rng.random((N, W)) < share)
        x[:, :, :w4] = rng.integers(0, 21, (N, 16, w4))
        sect[:, g] = x; amt[:, g] = rng.integers(250, 256, (N, 16, L)); cap[:, g] = 160
        traj[:, g, 0] = rng.integers(0, w4, (N, L)); traj[:, g, 1:] = rng.integers(w4, W, (N, 15, L))
    for n in (3, 4):
        g = int(o[n]); hot = (rng.permutation(16) < FU).reshape(1, 16, 1)
        sect[:, g] = np.where(hot, rng.integers(200, 256, (N, 16, W)), rng.integers(0, 21, (N, 16, W)))
        amt[:, g] = np.where(hot, rng.integers(120, 256, (N, 16, L)), rng.integers(0, 21, (N, 16, L)))
        cap[:, g] = rng.integers(280, 311, (N, 16, 1))
        for q in range(0, N, 2): amt[q, g, :, int(rng.integers(0, L))] = 0
    for n in (5, 6):
        g = int(o[n]); x = rng.integers(80, 121, (N, 16, W)); x[:, :, 1::2] = rng.integers(0, 21, (N, 16, W >> 1)); sect[:, g] = x
        cap[:, g] = 400; cap[int(rng.integers(0, N)), g] = 160
        traj[:, g] = 2 * rng.integers(0, W >> 1, (N, 16, L))
        for q in range(N):
            traj[q, g, 0] = 2 * rng.permutation(W >> 1)[:L]
            a = rng.integers(100, 119, 16); a[0] += (int(np.sum(a)) + n + 1) & 1
            amt[q, g] = a[np.argsort(rng.random((16, L)), axis=0)]
    return pack(sect, mv, traj, amt, cap)
def check_inputs(d):
    bad = []
    for k, lo, hi in (("sect", 0, 255), ("mv", 0, W - 1), ("traj", 0, W - 1), ("amt", 0, 255), ("cap", 160, 400)):
        v = np.asarray(d[k]).astype(np.float64)
        if not (np.min(v) >= lo and np.max(v) <= hi): bad.append("range of " + k)
        elif not np.all(v == np.floor(v)): bad.append("whole numbers of " + k)
    return bad
def picks(x, ix):
    return np.take_along_axis(x, ix.reshape(8, 1, 16 * L), 2).reshape(8, 16, 16, L)
def full(x, z, c, th):
    return np.add.reduce((x + z[:, :, None, :] > c).astype(np.int64), axis=1) >= th
def reference(sect, mv, traj, amt, cap):
    X = sect.astype(np.float32).astype(np.int64).reshape(N, 8, 16, W); z = amt.astype(np.float32).astype(np.int64).reshape(N, 8, 16, L)
    t = traj.astype(np.int64).reshape(N, 8, 16, L); man = mv.astype(np.int64).reshape(N, 8, 16, Q); cp = cap.astype(np.int64).reshape(N, 8, 16, 1, 1)
    odd = np.zeros((N, 8, 1, 1), np.int64); kk = np.arange(16).reshape(1, 16, 1); shadows = []
    for rnd in range(RO):
        for c, g, s, a in shadows: X[c, g][:, s] = X[c, g][:, s] - a
        shadows = []; th = FU + odd; cut = []; verdict = []
        for r in range(N):
            b = (r + SB) % N; x = picks(X[b], t[r])
            fm = full(np.maximum.accumulate(x, axis=2), z[r], cp[b], th[r])
            j = np.where(np.any(fm, axis=1), np.argmax(fm, axis=1), 16)
            p = np.take_along_axis(t[r], np.minimum(j, 15)[:, None, :], 1)[:, 0]
            lead = np.zeros((8, L), bool)
            for g in range(8):
                i = np.unique(p[g], return_index=True)[1]; lead[g, i] = True
                X[b, g][:, p[g, i]] = np.minimum(X[b, g][:, p[g, i]] + (z[r, g][:, i] >> 2), 255)
            cut.append((j, p, lead))
        for r in range(N):
            c = (r + SC) % N; j, p, lead = cut[r]; y = picks(X[c], t[r])
            fy = full(y, z[r], cp[c], th[r]) & (kk >= j[:, None, :]); refused = np.any(fy, axis=1)
            score = np.add.reduce(np.maximum(y + z[r][:, :, None, :] - cp[c], 0), axis=1)
            m = np.argmax(np.where(fy, score, -1), axis=1)
            tm = np.take_along_axis(t[r], m[:, None, :], 1)
            nn = np.take_along_axis(man[c], tm & (Q - 1), 2)
            ym = np.take_along_axis(y, m[:, None, None, :], 2)[:, :, 0]
            ok = lead & (j < 16) & ~refused
            for g in range(8):
                i = np.flatnonzero(ok[g]); s = p[g, i]; a = z[r, g][:, i] >> 2
                X[c, g][:, s] = np.minimum(X[c, g][:, s] + a, 255); shadows.append((c, g, s, a))
            verdict.append((refused, nn, ym))
        for r in range(N):
            j = cut[r][0]; refused, nn, ym = verdict[r]; rf = refused[:, None, :]
            fw = full(picks(X[r], nn), z[r], cp[r], th[r])
            u = np.add.reduce(z[r], axis=1)[:, None, :]
            t[r] = np.where(rf, np.where((kk >= j[:, None, :]) & ~fw, nn, t[r]), (5 * t[r] + u + 1) & (W - 1))
            z[r] = np.where(rf, (z[r] + ym) >> 1, z[r])
            odd[r] = (np.add.reduce(refused.astype(np.int64), axis=1) & 1).reshape(8, 1, 1)
    return {"ysect": X.reshape(N, 128, W).astype(np.float32).astype(BF), "ytraj": t.reshape(N, 128, L).astype(np.float32), "yamt": z.reshape(N, 128, L).astype(np.float32).astype(BF)}

@@ -1,0 +1,725 @@
+from concourse.mybir import AluOpType as ALU, ActivationFunctionType as ACT
+
+N, W, L, Q, RO, SB, SC = 6, 2048, 128, 512, 3, 1, 4
+H = "float16"
+BF, F32, U16, I32 = "bfloat16", "float32", "uint16", "int32"
+XW = W + L
+XZ = XW + L
+ZW = 272
+S2PE = True
+V2 = (0, 512)
+CH2 = [(512, 1024), (1024, 1536), (1536, 1792), (1792, 2048)]
+CH3 = [(0, 384), (384, 768), (768, 1280), (1280, 1792), (1792, 2048)]
+SGN3 = 768
+CH4 = [(0, 256), (256, 512), (512, 1024), (1024, 1408), (1408, 1664)]
+V4 = 1664
+V4L = 1536
+CH4L = [(0, 256), (256, 512), (512, 1024), (1024, 1280), (1280, 1536)]
+ALLENG = True
+EQS = 2
+TH3EARLY = 3
+EQMID = True
+DDAT = [0, 3, 6, 8, 8]
+THRAT = 1024
+MAGIC = 12582912.0
+
+
+def sb(n, d):
+    return ("sbuf", [128, n], d)
+
+
+SCRATCH = {
+    "X": sb(XZ, BF), "XR": sb(XW, BF), "man": sb(W, I32), "tr32": sb(L, I32), "cap32": sb(1, I32),
+    "Th": sb(L, U16), "Zs": sb(L, BF), "Cs": sb(8, BF), "Ch": sb(8, BF),
+    "Tc": sb(RO * L, U16), "Zc": sb(RO * ZW, BF), "Tj": sb(RO * L, U16), "Zj": sb(4 * ZW, BF), "Zh": sb(2 * ZW, BF),
+    "DDs": sb(RO * L, F32), "DD": sb(RO * L, F32), "NFs": sb(RO * L, BF), "NF": sb(RO * L, BF),
+    "Ous": sb(RO * 8, U16), "Oj": sb(RO * 8, U16), "Orp": sb(RO * 8, U16), "Ofs": sb(RO * 8, F32), "Of": sb(RO * 8, F32),
+    "V2s": sb(RO * 256, BF), "V2": sb(RO * 256, BF), "SVs": sb(RO * 256, BF), "SV": sb(RO * 256, BF),
+    "SOs": sb(RO * 8, U16), "SO": sb(RO * 8, U16), "Vs": sb(RO * L, U16), "Vl": sb(RO * L, U16),
+    "DAs": sb(RO * 256, H), "DA": sb(RO * 256, H),
+    "xs": sb(W, BF), "bb": sb(W, BF), "bo": sb(W, BF), "th3": sb(W, BF), "EC": sb(W, BF),
+    "eq": sb(1024, BF), "ab": sb(256, BF), "SEL": sb(1024, H), "NSEL": sb(1024, H), "Tm": sb(1024, F32),
+    "pi": sb(8, I32), "pf": sb(24, F32), "xr": sb(144, F32), "xq": sb(L, F32), "xm": sb(L, F32),
+    "idb": sb(L, BF), "idf": sb(L, F32), "id4": sb(L, F32), "id5": sb(L, F32), "idq": sb(L, BF), "idp": sb(L, BF), "id16": sb(L, BF),
+    "WB": sb(144, BF), "WS": sb(144, BF), "BO": sb(L, BF), "TRI": sb(L, BF), "mA": sb(L, BF), "ones": sb(L, BF),
+    "Dm": sb(16, F32), "Dm2": sb(16, F32), "C15": sb(512, BF), "rst": sb(L, BF), "cMx": sb(L, F32), "c4k": sb(8, BF),
+    "cTm": sb(8, U16), "cPA": sb(8, U16), "cEx": sb(8, U16), "cPm": sb(8, U16), "cUn": sb(8, U16),
+    "dum": sb(8, F32), "dumm": sb(8, F32), "dumz": sb(8, F32),
+    "capf": sb(8, F32), "F6": sb(8, BF), "fc": sb(8, F32),
+    "thA": sb(L, BF), "thT": sb(L, BF), "thA4": sb(L, BF), "thT4": sb(L, BF),
+    "a1": sb(L, BF), "nc": sb(L, BF), "a1j": sb(L, BF), "nj": sb(L, BF), "s15": sb(L, BF),
+    "FB": sb(144, BF), "ys": sb(L, F32), "PA": sb(L, H), "Pu": sb(8, U16),
+    "ee": sb(L, BF), "rf": sb(L, BF), "KB": sb(144, F32), "ids": sb(L, BF), "ng3": sb(L, BF), "y3": sb(L, F32), "Tmu": sb(8, U16),
+    "Vp": sb(L, I32), "o3": sb(8, F32), "js": sb(L, F32), "w1": sb(8, F32), "w2": sb(8, F32), "Yu": sb(8, U16),
+    "tt": sb(8, F32), "vv": sb(8, F32), "ex": sb(L, BF), "AP2": sb(256, BF), "nn": sb(8, F32), "nq": sb(8, BF), "nf": sb(8, F32),
+    "ymp": sb(L, BF), "ss": sb(L, F32), "hp": sb(L, F32),
+    "TD": sb(256, F32), "qq": sb(L, BF), "TK": sb(256, BF), "Tn": sb(256, H), "To": sb(L, F32),
+    "PT": ("psum", [128, 2048], F32), "PD": ("psum", [128, 1024], F32), "P6": ("psum", [128, 512], F32), "P7": ("psum", [128, 512], F32),
+}
+PER_ROUND = ["fT", "dd", "nf", "v2", "oj", "of", "orp", "sa", "sv", "so", "V", "R", "da", "Z", "Zb"]
+SEMAPHORES = (["qV", "qS", "qP", "qG", "sent", "bulk", "iT", "iZ", "iC", "fZ", "bk0", "bk1"]
+              + ["%s%d" % (m, r) for m in PER_ROUND for r in range(RO)]
+              + ["d%d" % i for i in range(12)])
+
+
+def messages(T):
+    m = {"iZ": (SB, T.Zs[:], T.Zc[:, 0:L], 0), "iT": (SB, T.Th[:], T.Tc[:, 0:L], 1), "iC": (SB, T.Cs[:], T.Ch[:], 1),
+         "fZ": (SC - SB, T.Zc[:, 0:L], T.Zj[:, 0:L], 1),
+         "bk0": (1, T.X[:, 0:W // 2], T.XR[:, 0:W // 2], 2), "bk1": (1, T.X[:, W // 2:W], T.XR[:, W // 2:W], 3)}
+    for r in range(RO):
+        last = r == RO - 1
+        ex = (-SC if last else SB - SC) % N
+        s = lambda n: slice(r * n, (r + 1) * n)
+        m["fT%d" % r] = (SC - SB, T.Tc[:, s(L)], T.Tj[:, s(L)], 1)
+        m["dd%d" % r] = (SC - SB, T.DDs[:, s(L)], T.DD[:, s(L)], 1)
+        m["nf%d" % r] = (SC - SB, T.NFs[:, s(L)], T.NF[:, s(L)], 1)
+        m["oj%d" % r] = (SC - SB, T.Ous[:, s(8)], T.Oj[:, s(8)], 1)
+        m["of%d" % r] = (SC - SB, T.Ofs[:, s(8)], T.Of[:, s(8)], 1)
+        m["V%d" % r] = (ex, T.Vs[:, s(L)], T.Vl[:, s(L)], 0)
+        m["da%d" % r] = (ex, T.DAs[:, s(256)], T.DA[:, s(256)], 1)
+        zn = (r + 1) * ZW
+        zsrc, rsrc = T.Zj[:, zn:zn + 136], T.Zj[:, zn + 144:zn + ZW]
+        if last:
+            m["Z%d" % r] = (ex, zsrc, T.Zh[:, ZW:ZW + 136], 0)
+            m["R%d" % r] = (ex, rsrc, T.Zh[:, ZW + 144:2 * ZW], 0)
+        else:
+            m["Z%d" % r] = (ex, zsrc, T.Zc[:, zn:zn + 136], 0)
+            m["R%d" % r] = (ex, rsrc, T.Zc[:, zn + 144:zn + ZW], 0)
+            m["v2%d" % r] = (1, T.V2s[:, s(256)], T.V2[:, s(256)], 1)
+            m["orp%d" % r] = (1, T.Ous[:, s(8)], T.Orp[:, s(8)], 1)
+            m["sv%d" % r] = (1, T.SVs[:, r * 256:r * 256 + L], T.SV[:, r * 256:r * 256 + L], 1)
+            m["sa%d" % r] = (1, T.SVs[:, r * 256 + L:r * 256 + 256], T.SV[:, r * 256 + L:r * 256 + 256], 1)
+            m["so%d" % r] = (1, T.SOs[:, s(8)], T.SO[:, s(8)], 0)
+        if r == RO - 2:
+            m["Zb%d" % r] = (-SC % N, T.Zj[:, (r + 1) * ZW:(r + 1) * ZW + 136], T.Zh[:, 0:136], 1)
+    return m
+
+
+def order_of_sends():
+    o = ["iZ", "iT", "iC", "bk0", "bk1", "fZ"]
+    for r in range(RO):
+        o += ["%s%d" % (x, r) for x in ("fT", "dd", "v2", "oj", "of", "orp", "nf", "sa", "sv", "so", "V", "R")]
+        o += ["%s%d" % (x, r) for x in (("da", "Z") if r == RO - 1 else ("Z", "da", "Zb"))]
+    return o
+
+
+def first_hop(T, topo, rank, step, lane):
+    src, dst = T.cores[rank], T.cores[(rank + step) % N]
+    if lane < 2 and topo.may_write(src, dst):
+        return dst
+    able = [c for c in topo.cores_of(src) if c != src and all(topo.may_write(c, d) for d in T.cores)]
+    near = [c for c in able if topo.die(c) == topo.die(src)]
+    far = [c for c in able if topo.die(c) != topo.die(src)]
+    return (near + far)[lane]
+
+
+def small_mask(topo, src, dst, name):
+    e = topo.engines(src, dst)
+    if name[:2] == "bk":
+        e = e[-8:]
+    elif name[0] == "i" or name in ("fZ", "fT0") or not ALLENG:
+        e = e[:8]
+    return sum(1 << x for x in e), len(e)
+
+
+def helper_program(g, core, T, topo):
+    msgs, sent = messages(T), 0
+    for rank in range(N):
+        if core not in topo.cores_of(T.cores[rank]):
+            continue
+        for name in order_of_sends():
+            if name not in msgs:
+                continue
+            step, _, land, lane = msgs[name]
+            if first_hop(T, topo, rank, step, lane) != core:
+                continue
+            dst = T.cores[(rank + step) % N]
+            g.wait_ge(T.sem[name], small_mask(topo, T.cores[rank], core, name)[1])
+            mask, n = small_mask(topo, core, dst, name)
+            rid, pid = topo.addr(dst, core)
+            g.remote_dma(land, land, T.sem[name], T.sem.sent, pid, rid, mask)
+            sent += n
+    if sent:
+        g.wait_ge(T.sem.sent, sent)
+
+
+def rank_program(g, core, T, topo):
+    rank = T.rank_of(core)
+    if rank is None:
+        helper_program(g, core, T, topo)
+        return
+    msgs = messages(T)
+    ops, lastw, readers = [], {}, {}
+    V, S, P = g.vector, g.scalar, g.tensor
+    eng = {"V": V, "S": S, "P": P, "G": g, "Y": g.sync}
+
+    def op(q, fn, r=(), w=(), ext=None):
+        i, deps = len(ops), set()
+        for k in r:
+            if k in lastw:
+                deps.add(lastw[k])
+            if k[0] == "B":
+                deps.update(x for x in readers.get(k, []) if ops[x]["q"] != q)
+        for k in w:
+            for x in readers.get(k, []) + ([lastw[k]] if k in lastw else []):
+                if ops[x]["q"] != q or ops[x]["ext"]:
+                    deps.add(x)
+        ops.append({"q": q, "fn": fn, "deps": deps, "ext": ext})
+        for k in w:
+            lastw[k], readers[k] = i, []
+        for k in r:
+            if k not in w:
+                readers.setdefault(k, []).append(i)
+
+    def arrive(name, keys):
+        step = msgs[name][0]
+        src = (rank - step) % N
+        via = first_hop(T, topo, src, step, msgs[name][3])
+        n = small_mask(topo, T.cores[src] if via == core else via, core, name)[1]
+        op("X", None, (), keys, (name, n))
+
+    total = {"sent": 0, "bulk": 0}
+
+    def send(name, keys):
+        step, src, land, lane = msgs[name]
+        to = first_hop(T, topo, rank, step, lane)
+        mask, n = small_mask(topo, core, to, name)
+        rid, pid = topo.addr(to, core)
+        loc = "bulk" if lane >= 2 else "sent"
+        total[loc] += n
+        op("G", lambda: g.remote_dma(land, src, T.sem[name], T.sem[loc], pid, rid, mask), keys, (), ("-", 0))
+
+    ndma = [0]
+
+    def dma(q, out, in_, r, w):
+        s = "d%d" % ndma[0]
+        ndma[0] += 1
+        op(q, lambda: eng[q].dma_start(out, in_), r, w, (s, 16))
+
+    def ts(out, in0, s1, o0, r, w, s2=None, o1=None):
+        if o1 is None:
+            op("V", lambda: V.tensor_scalar(out, in0, s1, None, o0), r, w)
+        else:
+            op("V", lambda: V.tensor_scalar(out, in0, s1, s2, o0, o1), r, w)
+
+    def tt(out, a, b, o, r, w):
+        op("V", lambda: V.tensor_tensor(out, a, b, o), r, w)
+
+    def cp(out, a, r, w):
+        op("V", lambda: V.tensor_copy(out, a), r, w)
+
+    def scan(out, d0, d1, o0, o1, r, w):
+        op("V", lambda: V.tensor_tensor_scan(out, d0, d1, 0.0, o0, o1), r, w)
+
+    def ms(ap, c, w, r=()):
+        op("V", lambda: V.memset(ap, c), r, w)
+
+    def act(out, in_, f, r, w, bias=0.0, scale=1.0, acc=None):
+        op("S", lambda: S.activation(out, in_, f, bias=bias, scale=scale, accum_out=acc), r, w)
+
+    def mm(out, lhsT, rhs, start, stop, r, w):
+        op("P", lambda: P.matmul(out, lhsT, rhs, start, stop), r, w)
+
+    def iota(out, pat, w):
+        op("G", lambda: g.iota(out, pat, 0, 0, allow_small_or_imprecise_dtypes=True), (), w)
+
+    def cols(name, a, b):
+        return ["%s%d" % (name, x) for x in range(a // L, (b - 1) // L + 1)]
+
+    def bank(a):
+        return "B%d" % (a // 512)
+
+    ID, RELU, SIGN, ABS = ACT.Identity, ACT.Relu, ACT.Sign, ACT.Abs
+    Xw, XRw = T.X[:, 0:XW], T.XR[:, 0:XW]
+    XK = ["X", "Xd"]
+
+    dma("Y", T.Zs[:], T.amt[:], (), ["zs"])
+    dma("S", T.tr32[:], T.traj[:], (), ["tr32"])
+    dma("Y", T.cap32[:], T.cap[:], (), ["cap32"])
+    dma("S", T.X[:, 0:W], T.sect[:], (), ["X"])
+    op("G", lambda: g.iota(T.pi[:, 0:1], [[0, 1]], 0, 1), (), ["pi0"])
+    iota(T.xr[:], [[1, 144]], ["xr"])
+    iota(T.xq[:], [[16, 8], [0, 16]], ["xq"])
+    iota(T.xm[:], [[1, 16], [0, 8]], ["xm"])
+    ms(T.Cs[:], 0.0, ["cs"])
+    ts(T.pi[:, 1:2], T.pi[:, 0:1], 15, ALU.bitwise_and, ["pi0"], ["pi1"])
+    ts(T.pi[:, 2:3], T.pi[:, 0:1], 112, ALU.bitwise_and, ["pi0"], ["pi2"])
+    ts(T.pi[:, 3:4], T.pi[:, 0:1], 7, ALU.bitwise_and, ["pi0"], ["pi3"])
+    ts(T.pi[:, 4:5], T.pi[:, 0:1], 3, ALU.logical_shift_right, ["pi0"], ["pi4"], 1, ALU.bitwise_and)
+    cp(T.pf[:, 0:5], T.pi[:, 0:5], ["pi0", "pi1", "pi2", "pi3", "pi4"], ["pf"])
+    pc, kc, gc_, a8, ah = (T.pf[:, i:i + 1] for i in range(5))
+    ts(T.idb[:], T.xr[:, 0:L], pc, ALU.is_equal, ["xr", "pf"], ["idb"])
+    for k in range(16):
+        act(T.EC[:, k::16], T.idb[:], ID, ["idb"], ["EC%d" % k])
+    ECK = ["EC%d" % k for k in range(16)]
+    ts(T.pf[:, 5:6], gc_, 8.0, ALU.mult, ["pf"], ["pf5"], kc, ALU.add)
+    ts(T.pf[:, 6:7], a8, 16.0, ALU.mult, ["pf"], ["pf6"], 15.0, ALU.add)
+    ts(T.pf[:, 7:8], kc, 8.0, ALU.mult, ["pf"], ["pf7"])
+    ts(T.pf[:, 8:9], a8, 16.0, ALU.mult, ["pf"], ["pf8"], ah, ALU.add)
+    ts(T.pf[:, 9:10], kc, -1.0, ALU.mult, ["pf"], ["pf9"], 8.0, ALU.add)
+    ts(T.pf[:, 10:11], kc, SGN3 / L - 0.5, ALU.is_lt, ["pf"], ["pf10"], -16.0, ALU.mult)
+    ts(T.BO[:], T.xq[:], gc_, ALU.is_equal, ["xq", "pf"], ["cBO"])
+    ms(T.ones[:], 1.0, ["ones"])
+    ts(T.WB[:], T.xr[:], -15.0, ALU.add, ["xr", "pf"], ["WB"], gc_, ALU.is_equal)
+    ts(T.pf[:, 11:12], T.pf[:, 10:11], 2048.0, ALU.add, ["pf10"], ["pf11"])
+    send("iZ", ["zs"])
+    cp(T.Th[:], T.tr32[:], ["tr32"], ["Th"])
+    send("iT", ["Th"])
+    ts(T.Cs[:, 0:1], T.cap32[:], -200.0, ALU.add, ["cap32", "cs"], ["cs"])
+    send("iC", ["cs"])
+
+    def fill(out, n, c, w):
+        op("G", lambda: g.iota(out, [[0, n]], c, 0, allow_small_or_imprecise_dtypes=True), (), w)
+    fill(T.X[:, W:XW], L, 0, ["Xd"])
+    fill(T.FB[:, 0:8], 8, 0, ["FB"])
+    fill(T.F6[:], 8, 6, ["F6"])
+    fill(T.c4k[:], 8, 4096, ["c4k"])
+    fill(T.ids[:], L, 1 if S2PE else -1, ["ids"])
+    send("bk0", ["X"])
+    send("bk1", ["X"])
+    op("X", None, (), ["Xsent"], ("bulk", total["bulk"]))
+    for i in range(W // Q):
+        dma("Y", T.man[:, i * Q:(i + 1) * Q], T.mv[:], ["X"], ["man%d" % i])
+    MAN = ["man%d" % i for i in range(W // Q)]
+    x8 = T.xr[:, 0:8]
+    sg2 = -1.0 if S2PE else 1.0
+    ts(T.capf[:, 0:1], T.cap32[:], -200.0, ALU.add, ["cap32"], ["capm"])
+    ts(T.capf[:, 1:2], T.cap32[:], 1.0, ALU.add, ["cap32"], ["capp"])
+    ts(T.capf[:, 2:3], T.cap32[:], -200.0, ALU.add, ["cap32"], ["cap2"], sg2, ALU.mult)
+    ts(T.cTm[:], x8, 16.0, ALU.mult, ["xr", "pf5"], ["cTm"], T.pf[:, 5:6], ALU.add)
+    ms(T.C15[:], 1.0, ["C15"])
+    ts(T.Dm[:], T.xr[:, 0:16], kc, ALU.is_equal, ["xr", "pf"], ["Dm"])
+    ts(T.Dm2[:], T.xr[:, 1:17], kc, ALU.is_equal, ["xr", "pf"], ["Dm2"])
+    ms(T.C15[:, 15::16], 0.0, ["C15"], ["C15"])
+    tt(T.Dm[:], T.Dm[:], T.Dm2[:], ALU.subtract, ["Dm", "Dm2"], ["Dm"])
+    ts(T.cPA[:], x8, 0.0, ALU.mult, ["xr", "pf6"], ["cPA"], T.pf[:, 6:7], ALU.add)
+    ts(T.cEx[:], x8, 0.0, ALU.mult, ["xr", "pf"], ["cEx"], a8, ALU.add)
+    ts(T.cPm[:], x8, T.pf[:, 7:8], ALU.add, ["xr", "pf7"], ["cPm"])
+    ts(T.dum[:], x8, T.pf[:, 7:8], ALU.add, ["xr", "pf7"], ["dum"], float(W), ALU.add)
+    ts(T.dumm[:], x8, T.pf[:, 7:8], ALU.add, ["xr", "pf7"], ["dumm"])
+    ts(T.dumz[:], x8, T.pf[:, 7:8], ALU.add, ["xr", "pf7"], ["dumz"], float(XW), ALU.add)
+    ts(T.cUn[:], x8, 2.0, ALU.mult, ["xr", "pf8"], ["cUn"], T.pf[:, 8:9], ALU.add)
+    ts(T.mA[:], T.xm[:], kc, ALU.is_equal, ["xm", "pf"], ["mA"])
+    ts(T.TRI[:], T.xr[:, 0:L], pc, ALU.is_le, ["xr", "pf"], ["TRI"], 4096.0, ALU.mult)
+    for gg in range(8):
+        ts(T.SEL[:, gg * L:(gg + 1) * L], T.ones[:], T.BO[:, 16 * gg:16 * gg + 1], ALU.mult, ["ones", "cBO"], ["SEL%d" % gg])
+    SELK = ["SEL%d" % gg for gg in range(8)]
+    ts(T.NSEL[:], T.SEL[:], -1.0, ALU.mult, SELK, ["NSEL"])
+    op("G", lambda: g.affine_select(T.ids[:], T.ids[:], [[-1, L]], ALU.is_equal, 0.0, 0, 1), ["ids"], ["ids"])
+    act(T.Tm[:], T.EC[:, 0:1024], ID, ECK, ["Tm"], scale=0.0)
+    act(T.idf[:], T.idb[:], ID, ["idb"], ["idf"])
+    act(T.idp[:], T.idb[:], ID, ["idb"], ["idp"], scale=2048.0)
+    act(T.idq[:], T.idb[:], ID, ["idb"], ["idq"], scale=-2048.0)
+    act(T.WS[:], T.WB[:], ID, ["WB"], ["WS"], scale=2048.0)
+    act(T.id4[:], T.idb[:], ID, ["idb"], ["id4"], scale=4.0)
+    act(T.id5[:], T.idb[:], ID, ["idb"], ["id5"], scale=5.0)
+
+    def late_constants():
+        fill(T.KB[:, 0:8], 8, 0, ["KB"])
+        fill(T.cMx[:], L, 16000000, ["cMx"])
+        op("G", lambda: g.affine_select(T.rst[:], T.ones[:], [[0, 8], [1, 16]], ALU.is_gt, 0.0, 0, 0), ["ones"], ["rst"])
+        op("G", lambda: g.affine_select(T.cMx[:], T.cMx[:], [[0, 8], [1, 16]], ALU.is_gt, -1.0, 0, 0), ["cMx"], ["cMx"])
+        fill(T.XR[:, W:XW], L, 0, ["XRd"])
+        for n in range(1, RO + 1):
+            fill(T.Zj[:, n * ZW + L:n * ZW + 144], 16, 0, ["zjF%d" % n])
+        fill(T.TK[:], 256, 0, ["TK"])
+        fill(T.AP2[:], 256, 0, ["AP0", "ap"])
+
+    def wband(buf, k):
+        return buf[:, 15 - k:143 - k]
+
+    def thr_transposed(A, TT, ka, kt, z, zk, capcol, capk, sign, tmp, tk, on="S"):
+        if on == "S":
+            act(A[:], z, ID, zk + capk, [ka], bias=capcol, scale=-sign)
+        else:
+            ts(A[:], z, -sign, ALU.mult, zk + capk, [ka], capcol, ALU.add)
+        mm(tmp, A[:], T.idb[:], True, True, [ka, "idb"], [tk])
+        if on == "S":
+            act(TT[:], tmp, ID, [tk], [kt])
+        else:
+            cp(TT[:], tmp, [tk], [kt])
+
+    def thr_bank(TT, kt, b, stop):
+        mm(T.PT[:, 512 * b:512 * b + 512], TT[:], T.EC[:, 512 * b:512 * b + 512], True, stop, [kt] + ECK, ["B%d" % b])
+
+    def quarters(z, zk, a1, a, ak, n, tag):
+        act(a1[:], z.indirect(T.cPm[:]), ID, zk + ["cPm"], ["a1" + tag], bias=128.625, scale=0.25)
+        act(n[:], a1[:], ID, ["a1" + tag], ["n" + tag], bias=384.0, scale=-1.0)
+        act(a, a1[:], ID, ["a1" + tag], [ak], bias=-129.0)
+
+    nv = 8 - EQS
+    half = (nv + 1) // 2
+
+    def dpos(gg, n=1):
+        if gg >= nv:
+            c = (gg - nv) * L
+            return T.PT[:, c:c + n * L], "B0"
+        h = gg // half
+        c = 512 * h + (gg - h * half) * L
+        return T.PD[:, c:c + n * L], "B%d" % (4 + h)
+    runs = [(0, half), (half, nv)] + ([(nv, 8)] if EQS else [])
+
+    def tri(a, b):
+        for gg in range(a, b):
+            o, bk = dpos(gg)
+            mm(o, T.idb[:], T.TRI[:], gg == a, False, ["idb", "TRI"], [bk])
+
+    def th3_piece(k, zj, zjk):
+        act(T.th3[:, k::16], zj, RELU, [zjk, "capp"], ["th3_%d" % k], bias=T.capf[:, 1:2], scale=-1.0)
+    TH3 = ["th3_%d" % k for k in range(16)]
+    B2ORDER = [1, 0, 2, 3]
+
+    tri(*runs[0])
+    tri(*runs[1])
+    arrive("iZ", ["zc0"])
+    arrive("iT", ["tc0"])
+    arrive("iC", ["caph"])
+    send("fZ", ["zc0"])
+    arrive("fZ", ["zj0"])
+    arrive("bk0", ["XR0"])
+    arrive("bk1", ["XR1"])
+    thr_transposed(T.thA, T.thT, "thA", "thT", T.Zc[:, 0:L], ["zc0"], T.capf[:, 2:3], ["cap2"], sg2, T.P6[:, 0:L], "B6", "V")
+    for b in B2ORDER:
+        thr_bank(T.thT, "thT", b, not S2PE)
+
+    for r in range(RO):
+        last = r == RO - 1
+        s = lambda n: slice(r * n, (r + 1) * n)
+        rs, ns, zn = str(r), str(r + 1), (r + 1) * ZW
+        tck, tjk = "tc" + rs, "tj" + rs
+        zc, zck = T.Zc[:, r * ZW:r * ZW + L], "zc" + rs
+        zj, zjk = T.Zj[:, r * ZW:r * ZW + L], "zj" + rs
+        Fc, Fck = (T.F6[:, 0:1], "F6") if r == 0 else (T.Zc[:, r * ZW + L:r * ZW + L + 1], zck)
+        Fj, Fjk = (T.F6[:, 0:1], "F6") if r == 0 else (T.Zj[:, r * ZW + L:r * ZW + L + 1], "zjF" + rs)
+        mn2, a2 = T.V2s[:, r * 256:r * 256 + L], T.V2s[:, r * 256 + L:r * 256 + 256]
+        mn3, a3 = T.SVs[:, r * 256:r * 256 + L], T.SVs[:, r * 256 + L:r * 256 + 256]
+        send("fT" + rs, [tck])
+        arrive("fT" + rs, [tjk])
+        if r == 0:
+            late_constants()
+
+        def off2(a, b):
+            return Xw.indirect(T.Tc[:, r * L + a // 16:r * L + b // 16])
+        if r == 0:
+            cp(T.To[:], T.Tc[:, 0:L], [tck], ["To"])
+            cp(T.Tm[:].indirect(T.cTm[:]), T.To[:], ["To", "cTm", "Tm"], ["Tm"])
+        else:
+            cp(T.Tm[:].indirect(T.cTm[:]), T.Tn[:, 1::2], ["Tn", "cTm", "Tm"], ["Tm"])
+        ts(T.xs[:, V2[0]:V2[1]], off2(*V2), -200.0, ALU.add, XK + [tck], cols("xs", *V2))
+        for a, b in CH2:
+            act(T.xs[:, a:b], off2(a, b), ID, XK + [tck], cols("xs", a, b), bias=-200.0)
+        quarters(zc, [zck], T.a1, a2, "a2" + rs, T.nc, "c")
+        act(T.fc[:, 0:1], Fc, ID, [Fck], ["fc0"], bias=-0.5)
+        act(T.fc[:, 1:2], Fc, ID, [Fck], ["fc1"], bias=-8.5)
+
+        def xacc(bk):
+            for a, b in [V2] + CH2:
+                if a // 512 == bk:
+                    mm(T.PT[:, a:b], T.idb[:], T.xs[:, a:b], False, b % 512 == 0, ["idb"] + cols("xs", a, b), [bank(a)])
+
+        def marks(bk):
+            a, b = 512 * bk, 512 * bk + 512
+            if S2PE:
+                scan(T.bo[:, a:b], T.PT[:, a:b], T.C15[:], ALU.max, ALU.min, [bank(a), "C15"], cols("bo", a, b))
+            else:
+                tt(T.bb[:, a:b], T.xs[:, a:b], T.PT[:, a:b], ALU.is_gt, cols("xs", a, b) + [bank(a)], cols("bb", a, b))
+                scan(T.bo[:, a:b], T.bb[:, a:b], T.C15[:], ALU.max, ALU.min, cols("bb", a, b) + ["C15"], cols("bo", a, b))
+
+        def counts(n):
+            bk = B2ORDER[n]
+            for mu in range(4 * bk, 4 * bk + 4):
+                mm(T.P7[:, 0:L], wband(T.WB, mu), T.bo[:, mu * L:(mu + 1) * L], n == 0 and mu % 4 == 0, n == 3 and mu % 4 == 3,
+                   ["WB", "bo%d" % mu], ["B7"])
+        def diffs(a, b):
+            for lam in range(a, b):
+                mm(T.P6[:, 16 * lam:16 * lam + 16], T.Tm[:, lam::8], T.Dm[:], True, True, ["Tm", "Dm"], ["B6"])
+        for n, bk in enumerate(B2ORDER):
+            diffs(DDAT[n], DDAT[n + 1])
+            if S2PE:
+                xacc(bk)
+            marks(bk)
+            if n >= 2:
+                counts(n - 2)
+        counts(2)
+        if EQS:
+            tri(*runs[2])
+        counts(3)
+        act(T.DDs[:, s(L)], T.P6[:, 0:L], ID, ["B6"], ["dds" + rs])
+        send("dd" + rs, ["dds" + rs])
+        todo3 = list(range(0 if r == 0 else TH3EARLY, 16))
+        if r == 0:
+            quarters(zj, [zjk], T.a1j, a3, "a3" + rs, T.nj, "j")
+        for k in todo3[:4]:
+            th3_piece(k, zj, zjk)
+        todo3 = todo3[4:]
+        if r == 1:
+            cp(XRw.indirect(T.SO[:, 0:8]), T.SV[:, 0:L], ["so0", "sv0", "XR"], ["XR"])
+        ts(T.FB[:, 1:129], T.P7[:, 0:L], Fc, ALU.is_ge, ["B7", Fck, "FB"], ["FB"])
+        scan(T.ys[:], T.FB[:, 0:L], T.DDs[:, s(L)], ALU.mult, ALU.add, ["FB", "dds" + rs], ["ys"])
+        act(T.NFs[:, s(L)], T.P7[:, 0:L], SIGN, ["B7", "fc0"], ["nfs" + rs], bias=T.fc[:, 0:1], scale=-1.0)
+        tt(T.PA[:], T.ys[:].indirect(T.cPA[:]), T.mA[:], ALU.mult, ["ys", "cPA", "mA"], ["PA"])
+        for k in todo3[:5]:
+            th3_piece(k, zj, zjk)
+        for a, b in ([runs[0]] + runs[2:] + [runs[1]] if EQMID else runs):
+            for gg in range(a, b):
+                o, bk = dpos(gg)
+                mm(o, T.NSEL[:, gg * L:(gg + 1) * L], T.PA[:], False, False, ["NSEL", "PA"], [bk])
+            o, bk = dpos(a, b - a)
+            mm(o, T.PA[:], T.SEL[:, a * L:b * L], False, True, SELK + ["PA"], [bk])
+        cp(T.Pu[:], T.ys[:, 15::16], ["ys"], ["Pu"])
+        tt(mn2, Xw.indirect(T.Pu[:]), T.nc[:], ALU.min, XK + ["Pu", "nc"], ["mn2" + rs])
+        if not last:
+            send("v2" + rs, ["mn2" + rs, "a2" + rs])
+        for n, (a, b) in enumerate(runs):
+            o, bk = dpos(a, b - a)
+            if n < 2:
+                ts(T.eq[:, a * L:b * L], o, 0.0, ALU.is_equal, [bk], ["eq%d" % n])
+            else:
+                act(T.ab[:, 0:EQS * L], o, ABS, [bk], ["ab"])
+                act(T.eq[:, a * L:b * L], T.ab[:, 0:EQS * L], RELU, ["ab"], ["eq2"], bias=1.0, scale=-1.0)
+        mm(T.PT[:, 1024:1032], T.idf[:], T.ys[:, 15::16], True, False, ["idf", "ys"], ["B2"])
+        mm(T.PT[:, 512:640], T.idb[:], T.xs[:, 15::16], True, False, ["idb"] + cols("xs", 0, W), ["B1"])
+        mm(T.PT[:, 512:640], T.idp[:], T.bo[:, 14::16], False, False, ["idp"] + cols("bo", 0, W), ["B1"])
+        mm(T.PT[:, 512:640], T.ids[:], T.thA[:], False, True, ["ids", "thA"], ["B1"])
+        act(T.s15[:], T.PT[:, 512:640], SIGN, ["B1"], ["s15"], bias=-0.5)
+        for c in range(8):
+            mm(T.PT[:, 1024 + c:1025 + c], T.eq[:, c::8], T.c4k[:, 0:1], False, c == 7, ["eq0", "eq1", "eq2", "c4k"], ["B2"])
+        cp(T.TD[:, 1::2], T.Tj[:, s(L)], [tjk], ["Tf"])
+        tt(T.Ofs[:, s(8)], T.PT[:, 1024:1032], T.dum[:], ALU.min, ["B2", "dum"], ["ofs" + rs])
+        cp(T.Ous[:, s(8)], T.Ofs[:, s(8)], ["ofs" + rs], ["ous" + rs])
+        tt(Xw.indirect(T.Ous[:, s(8)]), mn2, a2, ALU.add, ["ous" + rs, "mn2" + rs, "a2" + rs, "Xsent"] + XK, ["X"])
+        send("oj" + rs, ["ous" + rs])
+        send("of" + rs, ["ofs" + rs])
+        if not last:
+            send("orp" + rs, ["ous" + rs])
+        for k in todo3[5:]:
+            th3_piece(k, zj, zjk)
+        for mu in range(16):
+            mm(T.PT[:, 1536:1544], wband(T.WB, mu), T.s15[:, 8 * mu:8 * mu + 8], mu == 0, mu == 15, ["WB", "s15"], ["B3"])
+        act(T.fc[:, 2:3], Fj, ID, [Fjk, "pf11"], ["fc2"], bias=T.pf[:, 11:12], scale=2.0)
+        act(T.NFs[:, r * L + 15:(r + 1) * L:16], T.PT[:, 1536:1544], SIGN, ["B3", "fc1", "nfs" + rs], ["nfs" + rs], bias=T.fc[:, 1:2], scale=-0.5)
+        send("nf" + rs, ["nfs" + rs])
+        if not last:
+            send("sa" + rs, ["a3" + rs])
+        mm(T.PD[:, 0:L], T.BO[:], zj, True, False, ["cBO", zjk], ["B4"])
+        mm(T.PD[:, 0:L], T.id5[:], T.TD[:, 1::2], False, True, ["id5", "Tf"], ["B4"])
+        mm(T.PD[:, 512:640], T.BO[:], zj, True, False, ["cBO", zjk], ["B5"])
+        mm(T.PD[:, 512:640], T.id4[:], T.TD[:, 1::2], False, False, ["id4", "Tf"], ["B5"])
+        act(T.qq[:], T.PD[:, 0:L], ID, ["B4"], ["qq"], bias=128.500732421875, scale=1.0 / 2048)
+        for nm in ("dd", "nf", "oj", "of"):
+            arrive(nm + rs, [nm + rs])
+        NF = T.NF[:, s(L)]
+        for n, (a, b) in enumerate(CH3):
+            tt(T.xs[:, a:b], Xw.indirect(T.Tj[:, r * L + a // 16:r * L + b // 16]), T.th3[:, a:b], ALU.subtract,
+               XK + [tjk] + TH3, cols("xs", a, b))
+            act(T.bo[:, a:b], T.xs[:, a:b], RELU, cols("xs", a, b), cols("bo", a, b), bias=1.0)
+            if b <= SGN3:
+                act(T.bb[:, a:b], T.xs[:, a:b], SIGN, cols("xs", a, b), cols("bb", a, b), bias=0.5)
+            else:
+                ts(T.bb[:, a:b], T.xs[:, a:b], 0.0, ALU.is_ge, cols("xs", a, b), cols("bb", a, b), 2.0, ALU.mult)
+            for which in ((0, 1) if b <= SGN3 else (1, 0)):
+                for mu in range(a // L, b // L):
+                    if which == 0:
+                        mm(T.P6[:, 0:L], wband(T.WS, mu), T.bo[:, mu * L:(mu + 1) * L], mu == 0, mu == 15, ["WS", "bo%d" % mu], ["B6"])
+                    else:
+                        mm(T.P7[:, 0:L], wband(T.WB, mu), T.bb[:, mu * L:(mu + 1) * L], mu == 0, mu == 15, ["WB", "bb%d" % mu], ["B7"])
+            if n == 0:
+                mm(T.PD[:, 512:640], T.idq[:], T.qq[:], False, True, ["idq", "qq"], ["B5"])
+            if n == len(CH3) - 2:
+                mm(T.P7[:, 0:L], T.idq[:], NF, False, False, ["idq", "nf" + rs], ["B7"])
+                act(T.TD[:, 0::2], T.PD[:, 512:640], ID, ["B5"], ["dT"], bias=264193.0)
+
+        def shadow_values():
+            tt(mn3, Xw.indirect(T.Oj[:, s(8)]), T.nj[:], ALU.min, XK + ["oj" + rs, "nj"], ["mn3" + rs])
+        shadow_values()
+        if not last:
+            send("sv" + rs, ["mn3" + rs])
+        if r == 0:
+            act(T.id16[:], T.idb[:], ID, ["idb"], ["id16"], scale=16.0)
+        ts(T.ee[:], T.P7[:, 0:L], T.fc[:, 2:3], ALU.is_ge, ["B7", "fc2"], ["ee"])
+
+        def refused():
+            scan(T.rf[:], T.rst[:], T.ee[:], ALU.mult, ALU.max, ["rst", "ee"], ["rf"])
+            mm(T.PD[:, 0:8], T.idf[:], T.Of[:, s(8)], True, False, ["idf", "of" + rs], ["B4"])
+            mm(T.PD[:, 0:8], T.idp[:], T.NF[:, r * L + 15:(r + 1) * L:16], False, False, ["idp", "nf" + rs], ["B4"])
+            for n in range(2):
+                mm(T.PD[:, 0:8], T.idp[:], T.rf[:, 15::16], False, n == 1, ["idp", "rf"], ["B4"])
+            for n in range(2):
+                mm(T.PD[:, 512:520], T.idp[:], T.rf[:, 15::16], n == 0, n == 1, ["idp", "rf"], ["B5"])
+
+        def shadow_offsets():
+            tt(T.o3[:], T.PD[:, 0:8], T.dumm[:], ALU.min, ["B4", "dumm"], ["o3"])
+            ts(T.SOs[:, s(8)], T.o3[:], float(W), ALU.add, ["o3"], ["sos" + rs])
+        if not last:
+            refused()
+        tt(T.KB[:, 1:129], T.ee[:], T.P6[:, 0:L], ALU.mult, ["ee", "B6", "KB"], ["KB"])
+        if not last:
+            shadow_offsets()
+            send("so" + rs, ["sos" + rs])
+        scan(T.P6[:, L:2 * L], T.KB[:, 0:L], T.cMx[:], ALU.max, ALU.min, ["KB", "cMx"], ["B6"])
+        if last:
+            z4, z4k, F4, F4k, cap4, cap4k = T.Zh[:, 0:L], "zh0", T.Zh[:, L:L + 1], "zh0", T.capf[:, 0:1], "capm"
+        else:
+            z4, z4k, F4, F4k, cap4, cap4k = zc, zck, Fc, Fck, T.Ch[:, 0:1], "caph"
+        act(T.X[:, XW:XZ], zj, ID, [zjk], ["Xz"])
+        thr_transposed(T.thA4, T.thT4, "thA4", "thT4", z4, [z4k], cap4, [cap4k], 1.0, T.P7[:, 0:L], "B7")
+        tt(T.ng3[:], T.KB[:, 1:129], T.P6[:, L:2 * L], ALU.is_le, ["KB", "B6"], ["ng3"])
+        scan(T.y3[:], T.ng3[:], T.DD[:, s(L)], ALU.mult, ALU.add, ["ng3", "dd" + rs], ["y3"])
+        cp(T.Tmu[:], T.y3[:, 15::16], ["y3"], ["Tmu"])
+        cp(T.Vp[:], T.man[:].indirect(T.Tmu[:]), MAN + ["Tmu"], ["Vp"])
+        cp(T.Vs[:, s(L)], T.Vp[:].indirect(T.cUn[:]), ["Vp", "cUn"], ["vs" + rs])
+        send("V" + rs, ["vs" + rs])
+        for b in range(2 if last else 4):
+            thr_bank(T.thT4, "thT4", b, True)
+        if last:
+            refused()
+        act(T.tt[:], T.rf[:, 15::16], ID, ["rf"], ["tt"], bias=16.0, scale=-64.0)
+        v4 = V4L if last else V4
+        if not last:
+            act(T.th3[:, v4:W], T.PT[:, v4:W], ID, ["B3"], TH3, bias=200.0)
+        scan(T.js[:], T.rst[:], NF, ALU.mult, ALU.add, ["rst", "nf" + rs], ["js"])
+        tt(T.w1[:], T.dumz[:], T.PD[:, 512:520], ALU.subtract, ["dumz", "B5"], ["w1"])
+        tt(T.vv[:], T.tt[:], T.js[:, 15::16], ALU.max, ["tt", "js"], ["vv"])
+        tt(T.w2[:], T.w1[:], T.y3[:, 15::16], ALU.max, ["w1", "y3"], ["w2"])
+        tt(T.ex[:], T.vv[:].indirect(T.cEx[:]), T.mA[:], ALU.mult, ["vv", "cEx", "mA"], ["ex"])
+        cp(T.Yu[:], T.w2[:], ["w2"], ["Yu"])
+        mm(T.P7[:, 0:L], T.BO[:], T.ex[:], True, True, ["cBO", "ex"], ["B7"])
+        if last:
+            for b in (3, 2):
+                thr_bank(T.thT4, "thT4", b, True)
+        act(T.ymp[:], T.X[:, 0:XZ].indirect(T.Yu[:]), ID, XK + ["Xz", "Yu"], ["ymp"])
+        act(T.AP2[:, 1::2], T.P7[:, 0:L], RELU, ["B7"], ["ap", "nn"], bias=-7.0, scale=0.5, acc=T.nn[:, 0:1])
+        act(T.Zj[:, zn + 144:zn + ZW], T.P7[:, 0:L], RELU, ["B7", "pf9"], ["zjR" + ns], bias=T.pf[:, 9:10], scale=0.5)
+        send("R" + rs, ["zjR" + ns])
+
+        def new_points():
+            scan(T.DAs[:, s(256)], T.AP2[:], T.TD[:], ALU.mult, ALU.add, ["AP0", "ap", "Tf", "dT"], ["aa" + rs])
+            tt(T.DAs[:, r * 256:(r + 1) * 256:2], T.Vp[:].indirect(T.cUn[:]), T.TD[:, 1::2], ALU.subtract,
+               ["Vp", "cUn", "Tf", "aa" + rs], ["aa" + rs])
+            send("da" + rs, ["aa" + rs])
+        if last:
+            shadow_offsets()
+            new_points()
+        else:
+            for nm in ("v2", "orp", "sa", "sv", "so"):
+                arrive(nm + rs, [nm + rs])
+            tt(XRw.indirect(T.Orp[:, s(8)]), T.V2[:, r * 256:r * 256 + L], T.V2[:, r * 256 + L:r * 256 + 256], ALU.add,
+               ["orp" + rs, "v2" + rs, "XR0", "XR1", "XRd", "XR"], ["XR"])
+        tt(T.ss[:], T.ymp[:].indirect(T.cUn[:]), zj, ALU.add, ["ymp", "cUn", zjk], ["ss"])
+        if not last:
+            act(T.nq[:, 0:1], T.nn[:, 0:1], ID, ["nn"], ["nq"], bias=128.75, scale=0.5)
+        act(T.hp[:], T.ss[:], ID, ["ss"], ["hp"], bias=MAGIC, scale=0.4999)
+        if not last:
+            act(T.nf[:, 0:1], T.nq[:, 0:1], ID, ["nq", "nn"], ["nf"], bias=T.nn[:, 0:1], scale=-2.0)
+        act(T.Zj[:, zn:zn + L], T.hp[:], ID, ["hp"], ["zj" + ns], bias=-MAGIC)
+        if not last:
+            act(T.Zj[:, zn + L:zn + L + 1], T.nf[:, 0:1], ID, ["nf", "zjF" + ns], ["zjF" + ns], bias=264.0)
+        send("Z" + rs, ["zj" + ns, "zjF" + ns])
+        if last:
+            tt(Xw.indirect(T.SOs[:, s(8)]), mn3, a3, ALU.add, ["sos" + rs, "mn3" + rs, "a3" + rs] + XK, ["X"])
+            dma("Y", T.ysect[:], T.X[:, 0:W], ["X"], ["ysect"])
+            act(T.th3[:, v4:W], T.PT[:, v4:W], ID, ["B3"], TH3, bias=200.0)
+        else:
+            tt(XRw.indirect(T.SO[:, s(8)]), T.SV[:, r * 256:r * 256 + L], T.SV[:, r * 256 + L:r * 256 + 256], ALU.add,
+               ["so" + rs, "sv" + rs, "sa" + rs, "XR"], ["XR"])
+            new_points()
+        if r == RO - 2:
+            send("Zb" + rs, ["zj" + ns, "zjF" + ns])
+            arrive("Zb" + rs, ["zh0"])
+        arrive("V" + rs, ["vl" + rs])
+        arrive("da" + rs, ["da" + rs])
+        arrive("R" + rs, ["R" + rs])
+        if last:
+            arrive("Z" + rs, ["zh1"])
+            dma("Y", T.yamt[:], T.Zh[:, ZW:ZW + L], ["zh1"], ["yamt"])
+            win, wk, R, Rk = Xw, XK, T.Zh[:, ZW + 144:2 * ZW], "R" + rs
+        else:
+            arrive("Z" + rs, ["zc" + ns])
+            win, wk, R, Rk = XRw, ["XR"], T.Zc[:, zn + 144:zn + ZW], "R" + rs
+            tri(*runs[0])
+            tri(*runs[1])
+
+        def off4(a, b):
+            return win.indirect(T.Vl[:, r * L + a // 16:r * L + b // 16])
+        ch4 = CH4L if last else CH4
+        for a, b in ch4:
+            act(T.xs[:, a:b], off4(a, b), ID, wk + ["vl" + rs], cols("xs", a, b), bias=-200.0)
+        tt(T.bb[:, v4:W], off4(v4, W), T.th3[:, v4:W], ALU.is_gt, wk + ["vl" + rs] + TH3, cols("bb", v4, W))
+        if not last:
+            act(T.thA[:], T.Zc[:, zn:zn + L], ID, ["zc" + ns, "cap2"], ["thA"], bias=T.capf[:, 2:3], scale=-sg2)
+        for a, b in ch4:
+            tt(T.bb[:, a:b], T.xs[:, a:b], T.PT[:, a:b], ALU.is_gt, cols("xs", a, b) + [bank(a), bank(b - 1)], cols("bb", a, b))
+            if b == ch4[-1][1]:
+                b = W
+                if not last:
+                    mm(T.P6[:, 0:L], T.thA[:], T.idb[:], True, True, ["thA", "idb"], ["B6"])
+                    act(T.thT[:], T.P6[:, 0:L], ID, ["B6"], ["thT"])
+                    quarters(T.Zj[:, zn:zn + L], ["zj" + ns], T.a1j, T.SVs[:, (r + 1) * 256 + L:(r + 2) * 256], "a3" + ns, T.nj, "j")
+                    for k in range(TH3EARLY):
+                        th3_piece(k, T.Zj[:, zn:zn + L], "zj" + ns)
+            if b % 1024 == 0:
+                h = b // 1024 - 1
+                if h == 1:
+                    for hh in range(2):
+                        mm(T.P7[:, 64 * hh:64 * hh + 64], T.id16[:], R[:, 64 * hh:64 * hh + 64], False, False, ["id16", Rk], ["B7"])
+                for k in range(16):
+                    mm(T.P7[:, 64 * h:64 * h + 64], wband(T.WB, k), T.bb[:, 1024 * h + k:1024 * h + 1024:16], h == 0 and k == 0,
+                       h == 1 and k == 15, ["WB"] + cols("bb", b - 1024, b), ["B7"])
+        if not last:
+            cp(Xw.indirect(T.SOs[:, s(8)]), mn3, ["sos" + rs, "mn3" + rs] + XK, ["X"])
+        ts(T.TK[:, 1::2], T.P7[:, 0:L], F4, ALU.is_lt, ["B7", F4k, "TK"], ["TK"])
+        scan(T.Tn[:], T.TK[:], T.DA[:, s(256)], ALU.mult, ALU.add, ["TK", "da" + rs], ["Tn"])
+        if last:
+            cp(T.To[:], T.Tn[:, 1::2], ["Tn"], ["To"])
+            dma("Y", T.ytraj[:], T.To[:], ["To"], ["ytraj"])
+        else:
+            cp(T.Tc[:, (r + 1) * L:(r + 2) * L], T.Tn[:, 1::2], ["Tn"], ["tc" + ns])
+            for b in B2ORDER:
+                thr_bank(T.thT, "thT", b, not S2PE)
+    op("Y", None, ["ysect", "yamt", "ytraj"], ())
+
+    def token(i):
+        o = ops[i]
+        return o["ext"] if o["ext"] else ("q" + o["q"], o["n"])
+
+    known = {q: {} for q in eng}
+    rankof, plan = {q: 0 for q in eng}, []
+    for i, o in enumerate(ops):
+        if o["q"] == "X":
+            o["know"] = {}
+            continue
+        if not o["ext"]:
+            rankof[o["q"]] += 1
+            o["n"] = rankof[o["q"]]
+        kn, need = known[o["q"]], []
+        for d in sorted(o["deps"], reverse=True):
+            sem, n = token(d)
+            if sem == "-" or kn.get(sem, 0) >= n:
+                continue
+            need.append(d)
+            kn[sem] = n
+            for k2, v2 in ops[d]["know"].items():
+                if kn.get(k2, 0) < v2:
+                    kn[k2] = v2
+        o["know"] = dict(kn)
+        plan.append((i, need))
+    wanted = set(d for _, need in plan for d in need)
+    count, val = {q: 0 for q in eng}, {}
+    for i, need in plan:
+        o = ops[i]
+        for d in need:
+            if ops[d]["ext"]:
+                eng[o["q"]].wait_ge(T.sem[ops[d]["ext"][0]], ops[d]["ext"][1])
+            else:
+                eng[o["q"]].wait_ge(T.sem["q" + ops[d]["q"]], val[d])
+        if o["fn"] is None:
+            continue
+        ins = o["fn"]()
+        if o["ext"]:
+            if o["ext"][0] != "-":
+                ins.then_inc(T.sem[o["ext"][0]], o["ext"][1])
+        elif i in wanted:
+            count[o["q"]] += 1
+            val[i] = count[o["q"]]
+            ins.then_inc(T.sem["q" + o["q"]], 1)
+    g.wait_ge(T.sem.sent, total["sent"])

@@ -3,25 +3,23 @@ from concourse.mybir import AluOpType as ALU, ActivationFunctionType as ACT
 N, W, L, Q, RO, SB, SC = 6, 2048, 128, 512, 3, 1, 4
 H = "float16"
 BF, F32, U16, I32 = "bfloat16", "float32", "uint16", "int32"
-XW = W + L
-XZ = XW + L
+SP = W + L
+XW = SP + 2 * L
 ZW = 272
-S2PE = True
-V2 = (0, 512)
-CH2 = [(512, 1024), (1024, 1536), (1536, 1792), (1792, 2048)]
-CH3 = [(0, 384), (384, 768), (768, 1280), (1280, 1792), (1792, 2048)]
-SGN3 = 768
-CH4 = [(0, 256), (256, 512), (512, 1024), (1024, 1408), (1408, 1664)]
-V4 = 1664
-V4L = 1536
-CH4L = [(0, 256), (256, 512), (512, 1024), (1024, 1280), (1280, 1536)]
-ALLENG = True
+ZT, ZR = 144, 272
+LATE_ENGINES = ("bk", "iZ", "iC", "v2", "or", "sv", "Zb")
+UNIT = 2560.0
+S0 = 1280
+S3 = [(1280, 1792), (1792, 2048)]
+V3 = [(0, 512), (512, 1024), (1024, 1280)]
+S4 = [(1280, 1792), (1792, 2048)]
+V4 = [(0, 512), (512, 1024), (1024, 1280)]
+FIRST2 = "V0:512 S512:1024 S1024:1536 S1536:1792 S1792:2048"
+NEXT2 = "S0:512 V512:1024 S1024:1536 S1536:2048"
 EQS = 2
-TH3EARLY = 3
-EQMID = True
-DDAT = [0, 3, 6, 8, 8]
-THRAT = 1024
 MAGIC = 12582912.0
+CYC, PEC, LINK, HOP, ISSUE, FIXV, FIXS, GATHER, SCATTER = 0.83, 0.42, 170, 1600, 300, 30, 40, 1.56, 3.8
+LOAD = 1300
 
 
 def sb(n, d):
@@ -29,78 +27,70 @@ def sb(n, d):
 
 
 SCRATCH = {
-    "X": sb(XZ, BF), "XR": sb(XW, BF), "man": sb(W, I32), "tr32": sb(L, I32), "cap32": sb(1, I32),
-    "Th": sb(L, U16), "Zs": sb(L, BF), "Cs": sb(8, BF), "Ch": sb(8, BF),
-    "Tc": sb(RO * L, U16), "Zc": sb(RO * ZW, BF), "Tj": sb(RO * L, U16), "Zj": sb(4 * ZW, BF), "Zh": sb(2 * ZW, BF),
-    "DDs": sb(RO * L, F32), "DD": sb(RO * L, F32), "NFs": sb(RO * L, BF), "NF": sb(RO * L, BF),
-    "Ous": sb(RO * 8, U16), "Oj": sb(RO * 8, U16), "Orp": sb(RO * 8, U16), "Ofs": sb(RO * 8, F32), "Of": sb(RO * 8, F32),
-    "V2s": sb(RO * 256, BF), "V2": sb(RO * 256, BF), "SVs": sb(RO * 256, BF), "SV": sb(RO * 256, BF),
+    "X": sb(XW, BF), "XR": sb(XW, BF), "man": sb(W, F32), "mv32": sb(Q, I32), "tr32": sb(L, I32), "Th": sb(L, U16),
+    "cap32": sb(1, I32), "mn2": sb(L, BF), "a2": sb(L, BF), "Rm": sb(256, BF), "cIn": sb(8, U16),
+    "Zs": sb(L, BF), "Cs": sb(8, BF), "Ch": sb(8, BF),
+    "Tc": sb(RO * 256, U16), "Zc": sb(RO * ZW, BF), "Tj": sb(RO * 256, U16), "Zj": sb(4 * ZW, BF), "Zh": sb(2 * ZW, BF),
+    "DDs": sb(RO * L, F32), "DD": sb(RO * L, F32), "NFs": sb(RO * L, BF), "NF": sb(RO * L, BF), "NFm": sb(L, BF),
+    "Ous": sb(RO * 8, U16), "Oj": sb(RO * 8, U16), "Orp": sb(RO * 8, U16), "Ofs": sb(16, F32),
+    "V2s": sb(RO * L, BF), "V2": sb(RO * L, BF), "SVs": sb(RO * 256, BF), "SV": sb(RO * 256, BF),
     "SOs": sb(RO * 8, U16), "SO": sb(RO * 8, U16), "Vs": sb(RO * L, U16), "Vl": sb(RO * L, U16),
     "DAs": sb(RO * 256, H), "DA": sb(RO * 256, H),
-    "xs": sb(W, BF), "bb": sb(W, BF), "bo": sb(W, BF), "th3": sb(W, BF), "EC": sb(W, BF),
-    "eq": sb(1024, BF), "ab": sb(256, BF), "SEL": sb(1024, H), "NSEL": sb(1024, H), "Tm": sb(1024, F32),
-    "pi": sb(8, I32), "pf": sb(24, F32), "xr": sb(144, F32), "xq": sb(L, F32), "xm": sb(L, F32),
-    "idb": sb(L, BF), "idf": sb(L, F32), "id4": sb(L, F32), "id5": sb(L, F32), "idq": sb(L, BF), "idp": sb(L, BF), "id16": sb(L, BF),
-    "WB": sb(144, BF), "WS": sb(144, BF), "BO": sb(L, BF), "TRI": sb(L, BF), "mA": sb(L, BF), "ones": sb(L, BF),
-    "Dm": sb(16, F32), "Dm2": sb(16, F32), "C15": sb(512, BF), "rst": sb(L, BF), "cMx": sb(L, F32), "c4k": sb(8, BF),
-    "cTm": sb(8, U16), "cPA": sb(8, U16), "cEx": sb(8, U16), "cPm": sb(8, U16), "cUn": sb(8, U16),
-    "dum": sb(8, F32), "dumm": sb(8, F32), "dumz": sb(8, F32),
-    "capf": sb(8, F32), "F6": sb(8, BF), "fc": sb(8, F32),
-    "thA": sb(L, BF), "thT": sb(L, BF), "thA4": sb(L, BF), "thT4": sb(L, BF),
+    "xs": sb(W, BF), "bb": sb(W, BF), "bo": sb(W, BF), "th": sb(W, BF), "ECp": sb(W, BF), "ECn": sb(W - S0, BF),
+    "eq": sb(1024, BF), "ab": sb(512, BF), "SEL": sb(1024, H), "NSEL": sb(1024, H), "Tm": sb(1024, F32),
+    "pi": sb(8, I32), "pf": sb(24, F32), "xr": sb(144, F32), "xq": sb(L, F32), "xm": sb(L, F32), "xk": sb(L, F32),
+    "lc": sb(L, F32), "lx": sb(L, F32), "x8": sb(24, F32),
+    "idb": sb(L, BF), "idc": sb(L, BF), "idf": sb(L, F32), "id4": sb(L, F32), "id5": sb(L, F32), "idq": sb(L, BF), "idp": sb(L, BF),
+    "idu": sb(L, BF),
+    "WB": sb(144, BF), "WS": sb(144, BF), "WU": sb(144, BF), "BO": sb(L, BF), "TRI": sb(L, BF), "mA": sb(L, BF), "mK": sb(L, BF),
+    "ones": sb(L, BF), "Dm": sb(32, F32), "C15": sb(512, BF), "rst": sb(L, BF), "rs2": sb(256, BF),
+    "cMx": sb(L, F32), "c4k": sb(8, BF), "spT": sb(L, F32),
+    "cTm": sb(8, U16), "cPA": sb(8, U16), "cEx": sb(8, U16), "cP0": sb(8, U16), "cP1": sb(8, U16),
+    "dum": sb(16, F32), "capf": sb(8, F32), "F6": sb(8, BF), "fc": sb(16, F32),
+    "t3": sb(L, BF), "t3T": sb(L, BF), "off": sb(L, BF),
     "a1": sb(L, BF), "nc": sb(L, BF), "a1j": sb(L, BF), "nj": sb(L, BF), "s15": sb(L, BF),
     "FB": sb(144, BF), "ys": sb(L, F32), "PA": sb(L, H), "Pu": sb(8, U16),
-    "ee": sb(L, BF), "rf": sb(L, BF), "KB": sb(144, F32), "ids": sb(L, BF), "ng3": sb(L, BF), "y3": sb(L, F32), "Tmu": sb(8, U16),
-    "Vp": sb(L, I32), "o3": sb(8, F32), "js": sb(L, F32), "w1": sb(8, F32), "w2": sb(8, F32), "Yu": sb(8, U16),
-    "tt": sb(8, F32), "vv": sb(8, F32), "ex": sb(L, BF), "AP2": sb(256, BF), "nn": sb(8, F32), "nq": sb(8, BF), "nf": sb(8, F32),
-    "ymp": sb(L, BF), "ss": sb(L, F32), "hp": sb(L, F32),
-    "TD": sb(256, F32), "qq": sb(L, BF), "TK": sb(256, BF), "Tn": sb(256, H), "To": sb(L, F32),
+    "E": sb(256, H), "Es": sb(256, H), "rq": sb(L, F32), "KB": sb(144, F32), "ng3": sb(L, BF), "y3": sb(L, F32), "Tmu": sb(8, U16),
+    "js": sb(L, F32), "ww": sb(24, F32), "Yu": sb(8, U16),
+    "vv": sb(8, F32), "ex": sb(L, BF), "AP2": sb(256, BF), "nn": sb(8, F32), "nq": sb(8, BF),
+    "ymp": sb(L, BF), "hp": sb(256, F32),
+    "TD": sb(256, F32), "qq": sb(L, BF), "TK": sb(256, BF), "Tn": sb(256, F32), "To": sb(L, F32),
     "PT": ("psum", [128, 2048], F32), "PD": ("psum", [128, 1024], F32), "P6": ("psum", [128, 512], F32), "P7": ("psum", [128, 512], F32),
 }
-PER_ROUND = ["fT", "dd", "nf", "v2", "oj", "of", "orp", "sa", "sv", "so", "V", "R", "da", "Z", "Zb"]
+PER_ROUND = ["fT", "dd", "nf", "v2", "oj", "orp", "sv", "so", "V", "da", "Z", "Zb"]
 SEMAPHORES = (["qV", "qS", "qP", "qG", "sent", "bulk", "iT", "iZ", "iC", "fZ", "bk0", "bk1"]
               + ["%s%d" % (m, r) for m in PER_ROUND for r in range(RO)]
               + ["d%d" % i for i in range(12)])
+PASSES, ORDER_END = 1, []
+ORDER, SENDS = [], []
 
 
 def messages(T):
-    m = {"iZ": (SB, T.Zs[:], T.Zc[:, 0:L], 0), "iT": (SB, T.Th[:], T.Tc[:, 0:L], 1), "iC": (SB, T.Cs[:], T.Ch[:], 1),
+    m = {"iT": (SB, T.Th[:], T.Tc[:, 0:L], 0), "iZ": (SB, T.Zs[:], T.Zc[:, 0:L], 1), "iC": (SB, T.Cs[:], T.Ch[:], 1),
          "fZ": (SC - SB, T.Zc[:, 0:L], T.Zj[:, 0:L], 1),
          "bk0": (1, T.X[:, 0:W // 2], T.XR[:, 0:W // 2], 2), "bk1": (1, T.X[:, W // 2:W], T.XR[:, W // 2:W], 3)}
     for r in range(RO):
         last = r == RO - 1
         ex = (-SC if last else SB - SC) % N
         s = lambda n: slice(r * n, (r + 1) * n)
-        m["fT%d" % r] = (SC - SB, T.Tc[:, s(L)], T.Tj[:, s(L)], 1)
+        m["fT%d" % r] = (SC - SB, T.Tc[:, s(256)], T.Tj[:, s(256)], 1)
         m["dd%d" % r] = (SC - SB, T.DDs[:, s(L)], T.DD[:, s(L)], 1)
         m["nf%d" % r] = (SC - SB, T.NFs[:, s(L)], T.NF[:, s(L)], 1)
         m["oj%d" % r] = (SC - SB, T.Ous[:, s(8)], T.Oj[:, s(8)], 1)
-        m["of%d" % r] = (SC - SB, T.Ofs[:, s(8)], T.Of[:, s(8)], 1)
         m["V%d" % r] = (ex, T.Vs[:, s(L)], T.Vl[:, s(L)], 0)
         m["da%d" % r] = (ex, T.DAs[:, s(256)], T.DA[:, s(256)], 1)
         zn = (r + 1) * ZW
-        zsrc, rsrc = T.Zj[:, zn:zn + 136], T.Zj[:, zn + 144:zn + ZW]
         if last:
-            m["Z%d" % r] = (ex, zsrc, T.Zh[:, ZW:ZW + 136], 0)
-            m["R%d" % r] = (ex, rsrc, T.Zh[:, ZW + 144:2 * ZW], 0)
+            m["Z%d" % r] = (ex, T.Zj[:, zn:zn + L], T.Zh[:, ZW:ZW + L], 0)
         else:
-            m["Z%d" % r] = (ex, zsrc, T.Zc[:, zn:zn + 136], 0)
-            m["R%d" % r] = (ex, rsrc, T.Zc[:, zn + 144:zn + ZW], 0)
-            m["v2%d" % r] = (1, T.V2s[:, s(256)], T.V2[:, s(256)], 1)
+            m["Z%d" % r] = (ex, T.Zj[:, zn:zn + ZW], T.Zc[:, zn:zn + ZW], 0)
+            m["v2%d" % r] = (1, T.V2s[:, s(L)], T.V2[:, s(L)], 1)
             m["orp%d" % r] = (1, T.Ous[:, s(8)], T.Orp[:, s(8)], 1)
-            m["sv%d" % r] = (1, T.SVs[:, r * 256:r * 256 + L], T.SV[:, r * 256:r * 256 + L], 1)
-            m["sa%d" % r] = (1, T.SVs[:, r * 256 + L:r * 256 + 256], T.SV[:, r * 256 + L:r * 256 + 256], 1)
+            m["sv%d" % r] = (1, T.SVs[:, s(256)], T.SV[:, s(256)], 1)
             m["so%d" % r] = (1, T.SOs[:, s(8)], T.SO[:, s(8)], 0)
         if r == RO - 2:
-            m["Zb%d" % r] = (-SC % N, T.Zj[:, (r + 1) * ZW:(r + 1) * ZW + 136], T.Zh[:, 0:136], 1)
+            m["Zb%d" % r] = (-SC % N, T.Zj[:, zn:zn + ZW], T.Zh[:, 0:ZW], 1)
     return m
-
-
-def order_of_sends():
-    o = ["iZ", "iT", "iC", "bk0", "bk1", "fZ"]
-    for r in range(RO):
-        o += ["%s%d" % (x, r) for x in ("fT", "dd", "v2", "oj", "of", "orp", "nf", "sa", "sv", "so", "V", "R")]
-        o += ["%s%d" % (x, r) for x in (("da", "Z") if r == RO - 1 else ("Z", "da", "Zb"))]
-    return o
 
 
 def first_hop(T, topo, rank, step, lane):
@@ -115,21 +105,22 @@ def first_hop(T, topo, rank, step, lane):
 
 def small_mask(topo, src, dst, name):
     e = topo.engines(src, dst)
-    if name[:2] == "bk":
+    if name[:2] in LATE_ENGINES:
         e = e[-8:]
-    elif name[0] == "i" or name in ("fZ", "fT0") or not ALLENG:
+    elif name[0] == "i":
         e = e[:8]
     return sum(1 << x for x in e), len(e)
 
 
 def helper_program(g, core, T, topo):
-    msgs, sent = messages(T), 0
+    sent = 0
     for rank in range(N):
         if core not in topo.cores_of(T.cores[rank]):
             continue
-        for name in order_of_sends():
-            if name not in msgs:
-                continue
+        msgs = messages(T)
+        if not SENDS:
+            lay_out(record(None, T.cores[rank], T, topo)[0])
+        for name in SENDS:
             step, _, land, lane = msgs[name]
             if first_hop(T, topo, rank, step, lane) != core:
                 continue
@@ -143,40 +134,91 @@ def helper_program(g, core, T, topo):
         g.wait_ge(T.sem.sent, sent)
 
 
-def rank_program(g, core, T, topo):
-    rank = T.rank_of(core)
-    if rank is None:
-        helper_program(g, core, T, topo)
-        return
-    msgs = messages(T)
-    ops, lastw, readers = [], {}, {}
-    V, S, P = g.vector, g.scalar, g.tensor
-    eng = {"V": V, "S": S, "P": P, "G": g, "Y": g.sync}
+def lay_out(ops):
+    if ORDER:
+        return ORDER
+    n = len(ops)
+    after = [[] for _ in ops]
+    before = [dict(o["soft"]) for o in ops]
+    for i, o in enumerate(ops):
+        for d in o["deps"]:
+            before[i][d] = max(before[i].get(d, 0), ops[d]["lat"])
+        for d, lat in before[i].items():
+            after[d].append((i, lat))
+    tail = [0.0] * n
+    for i in range(n - 1, -1, -1):
+        tail[i] = ops[i]["cost"] + max([lat + tail[j] for j, lat in after[i]] + [0.0])
 
-    def op(q, fn, r=(), w=(), ext=None):
-        i, deps = len(ops), set()
+
+    def place(turn, nxt):
+        at, busy, end = [0.0] * n, {}, [0.0] * n
+        for i in turn:
+            t, c, line = at[i], ops[i]["cost"], busy.setdefault(ops[i]["q"], [])
+            k = 0
+            if ops[i]["q"] != "X":
+                while k < len(line) and line[k][0] < t + c:
+                    t = max(t, line[k][1])
+                    k += 1
+                line.insert(k, (t, t + c))
+            end[i] = t + c
+            for j, lat in nxt[i]:
+                at[j] = max(at[j], t + c + lat)
+        return end
+    back = [list(b.items()) for b in before]
+    end = place(sorted(range(n), key=lambda i: (-tail[i], i)), after)
+    for _ in range(PASSES):
+        late = place(sorted(range(n), key=lambda i: (-end[i], -i)), back)
+        again = place(sorted(range(n), key=lambda i: (-late[i], i)), after)
+        if max(again) <= max(end):
+            end = again
+    ORDER.extend(sorted(range(n), key=lambda i: (end[i] - ops[i]["cost"], end[i], i)))
+    ORDER_END.append(max(end))
+    SENDS.extend(ops[i]["send"] for i in ORDER if ops[i]["send"])
+    return ORDER
+
+
+def record(g, core, T, topo):
+    rank = T.rank_of(core)
+    msgs = messages(T)
+    ops, lastw, readers, opened, sent_at = [], {}, {}, {}, {}
+    eng = {"V": g.vector, "S": g.scalar, "P": g.tensor, "G": g, "Y": g.sync} if g else {}
+
+    def op(q, fn, r=(), w=(), ext=None, cost=0.0, lat=LINK, send=None, soft=()):
+        i, deps, soft = len(ops), set(), dict(soft)
+        group = None
         for k in r:
-            if k in lastw:
-                deps.add(lastw[k])
+            deps.update(lastw.get(k, []))
+            opened.pop(k, None)
             if k[0] == "B":
                 deps.update(x for x in readers.get(k, []) if ops[x]["q"] != q)
         for k in w:
-            for x in readers.get(k, []) + ([lastw[k]] if k in lastw else []):
+            if q == "P" and k in opened:
+                group, old = opened[k]
+            else:
+                old = readers.get(k, []) + lastw.get(k, [])
+                opened.pop(k, None)
+                lastw[k], readers[k] = [], []
+                if q == "P":
+                    group = i
+                    opened[k] = (group, old)
+            for x in old:
                 if ops[x]["q"] != q or ops[x]["ext"]:
                     deps.add(x)
-        ops.append({"q": q, "fn": fn, "deps": deps, "ext": ext})
-        for k in w:
-            lastw[k], readers[k] = i, []
+                else:
+                    soft[x] = 0
+            lastw[k].append(i)
+        ops.append({"q": q, "fn": fn, "deps": deps, "soft": soft, "ext": ext, "cost": cost, "lat": lat, "send": send, "group": group})
         for k in r:
             if k not in w:
                 readers.setdefault(k, []).append(i)
 
     def arrive(name, keys):
-        step = msgs[name][0]
+        step, _, land, lane = msgs[name]
         src = (rank - step) % N
-        via = first_hop(T, topo, src, step, msgs[name][3])
+        via = first_hop(T, topo, src, step, lane)
         n = small_mask(topo, T.cores[src] if via == core else via, core, name)[1]
-        op("X", None, (), keys, (name, n))
+        hops = max(1 if first_hop(T, topo, x, step, lane) in T.cores else 2 for x in range(N))
+        op("X", None, (), keys, (name, n), lat=0, soft={sent_at[name]: hops * (HOP + land.shape[1])})
 
     total = {"sent": 0, "bulk": 0}
 
@@ -187,163 +229,191 @@ def rank_program(g, core, T, topo):
         rid, pid = topo.addr(to, core)
         loc = "bulk" if lane >= 2 else "sent"
         total[loc] += n
-        op("G", lambda: g.remote_dma(land, src, T.sem[name], T.sem[loc], pid, rid, mask), keys, (), ("-", 0))
+        sent_at[name] = len(ops)
+        op("G", lambda: g.remote_dma(land, src, T.sem[name], T.sem[loc], pid, rid, mask), keys, (), ("-", 0), ISSUE, send=name)
 
     ndma = [0]
 
-    def dma(q, out, in_, r, w):
+    def dma(q, out, in_, r, w, lat):
         s = "d%d" % ndma[0]
         ndma[0] += 1
-        op(q, lambda: eng[q].dma_start(out, in_), r, w, (s, 16))
+        op(q, lambda: eng[q].dma_start(T[out][:] if isinstance(out, str) else out, T[in_][:] if isinstance(in_, str) else in_),
+           r, w, (s, 16), 50, lat)
+
+    def view(x):
+        return x[0].indirect(x[1]) if isinstance(x, tuple) else x
+
+    def narrow(*xs):
+        return all(SCRATCH[x.name][2] in (BF, H, U16) for x in xs)
+
+    def price(fix, out, a, rate):
+        if isinstance(out, tuple):
+            return 50 + a.shape[1] * SCATTER * CYC
+        if isinstance(a, tuple):
+            return 50 + out.shape[1] * GATHER * CYC
+        return fix + max(64, out.shape[1] * rate) * CYC
+
+    def half_rate(out, *xs):
+        return 1.0 if isinstance(out, tuple) or isinstance(xs[0], tuple) or not narrow(out, *xs) else 0.5
 
     def ts(out, in0, s1, o0, r, w, s2=None, o1=None):
+        c = price(FIXV, out, in0, half_rate(out, in0))
         if o1 is None:
-            op("V", lambda: V.tensor_scalar(out, in0, s1, None, o0), r, w)
+            op("V", lambda: g.vector.tensor_scalar(out, view(in0), s1, None, o0), r, w, cost=c)
         else:
-            op("V", lambda: V.tensor_scalar(out, in0, s1, s2, o0, o1), r, w)
+            op("V", lambda: g.vector.tensor_scalar(out, view(in0), s1, s2, o0, o1), r, w, cost=c)
 
     def tt(out, a, b, o, r, w):
-        op("V", lambda: V.tensor_tensor(out, a, b, o), r, w)
+        op("V", lambda: g.vector.tensor_tensor(view(out), view(a), b, o), r, w, cost=price(FIXV, out, a, 1.0))
 
     def cp(out, a, r, w):
-        op("V", lambda: V.tensor_copy(out, a), r, w)
+        op("V", lambda: g.vector.tensor_copy(view(out), view(a)), r, w, cost=price(FIXV, out, a, half_rate(out, a)))
 
     def scan(out, d0, d1, o0, o1, r, w):
-        op("V", lambda: V.tensor_tensor_scan(out, d0, d1, 0.0, o0, o1), r, w)
+        op("V", lambda: g.vector.tensor_tensor_scan(out, d0, d1, 0.0, o0, o1), r, w, cost=price(FIXV, out, d0, half_rate(out, d0, d1)))
 
     def ms(ap, c, w, r=()):
-        op("V", lambda: V.memset(ap, c), r, w)
+        op("V", lambda: g.vector.memset(ap, c), r, w, cost=price(FIXV, ap, ap, half_rate(ap, ap)))
 
     def act(out, in_, f, r, w, bias=0.0, scale=1.0, acc=None):
-        op("S", lambda: S.activation(out, in_, f, bias=bias, scale=scale, accum_out=acc), r, w)
+        op("S", lambda: g.scalar.activation(out, view(in_), f, bias=bias, scale=scale, accum_out=acc), r, w, cost=price(FIXS, out, in_, 1.0))
 
-    def mm(out, lhsT, rhs, start, stop, r, w):
-        op("P", lambda: P.matmul(out, lhsT, rhs, start, stop), r, w)
+    def mm(out, lhsT, rhs, r, w):
+        op("P", lambda first, final: g.tensor.matmul(out, lhsT, rhs, first, final), r, [w],
+           cost=max(64, rhs.shape[1]) * PEC * (1 if narrow(rhs) else 4))
 
-    def iota(out, pat, w):
-        op("G", lambda: g.iota(out, pat, 0, 0, allow_small_or_imprecise_dtypes=True), (), w)
+    def iota(out, pat, w, base=0, step=0):
+        op("G", lambda: g.iota(out, pat, base, step, allow_small_or_imprecise_dtypes=True), (), w, cost=130 + 2 * CYC * out.shape[1])
 
     def cols(name, a, b):
-        return ["%s%d" % (name, x) for x in range(a // L, (b - 1) // L + 1)]
-
-    def bank(a):
-        return "B%d" % (a // 512)
+        return ["%s%d" % (name, x) for x in range(a // 64, (b - 1) // 64 + 1)]
 
     ID, RELU, SIGN, ABS = ACT.Identity, ACT.Relu, ACT.Sign, ACT.Abs
-    Xw, XRw = T.X[:, 0:XW], T.XR[:, 0:XW]
-    XK = ["X", "Xd"]
+    Xl, Xw, XRl, XRw = T.X[:, 0:W], T.X[:], T.XR[:, 0:W], T.XR[:]
+    XK = ["X", "Xz", "Xd"]
 
-    dma("Y", T.Zs[:], T.amt[:], (), ["zs"])
-    dma("S", T.tr32[:], T.traj[:], (), ["tr32"])
-    dma("Y", T.cap32[:], T.cap[:], (), ["cap32"])
-    dma("S", T.X[:, 0:W], T.sect[:], (), ["X"])
-    op("G", lambda: g.iota(T.pi[:, 0:1], [[0, 1]], 0, 1), (), ["pi0"])
+    dma("S", T.tr32[:], "traj", (), ["tr32"], LOAD)
+    dma("Y", T.Zs[:], "amt", (), ["zs"], LOAD)
+    dma("Y", T.cap32[:], "cap", (), ["cap32"], LOAD)
+    dma("S", T.X[:, 0:W], "sect", (), ["X"], 2 * LOAD)
+    op("G", lambda: g.iota(T.pi[:, 0:1], [[0, 1]], 0, 1), (), ["pi0"], cost=130)
+    iota(T.lc[:], [[64, 2], [1, 16], [16, 4]], ["lc"])
     iota(T.xr[:], [[1, 144]], ["xr"])
+    iota(T.x8[:, 0:8], [[64, 2], [4, 4]], ["x8a"])
+    iota(T.x8[:, 8:16], [[1, 8]], ["x8b"], 0, 8)
+    iota(T.x8[:, 16:24], [[64, 2], [1, 4]], ["x8c"])
     iota(T.xq[:], [[16, 8], [0, 16]], ["xq"])
     iota(T.xm[:], [[1, 16], [0, 8]], ["xm"])
-    ms(T.Cs[:], 0.0, ["cs"])
+    iota(T.lx[:], [[1, 16], [16, 8]], ["lx"])
+    iota(T.xk[:], [[0, 8], [1, 16]], ["xk"])
+    ms(T.ones[:], 1.0, ["ones"])
+    ms(T.X[:, W:XW], 0.0, ["Xz", "Xd"])
+    ms(T.XR[:, W:XW], 0.0, ["XRd"])
+    ms(T.C15[:], 1.0, ["C15"])
+    ms(T.C15[:, 15::16], 0.0, ["C15"], ["C15"])
+    ms(T.rs2[:], 1.0, ["rs2"])
+    ms(T.rs2[:, 0::32], 0.0, ["rs2"], ["rs2"])
+    ms(T.FB[:, 0:8], 0.0, ["FB"])
+    ms(T.F6[:], 6.0, ["F6"])
+    ms(T.c4k[:], 4096.0, ["c4k"])
+    ms(T.fc[:, 8:9], -0.5, ["fb0"])
+    ms(T.fc[:, 9:10], -8.5, ["fb1"])
+    ms(T.KB[:, 0:8], 0.0, ["KB"])
+    ms(T.E[:], 0.0, ["E0", "E1"])
+    ms(T.TK[:], 0.0, ["TK0", "TK1"])
+    ms(T.AP2[:], 0.0, ["AP0", "ap"])
+    ms(T.off[:], 0.0, ["off"])
+    for n in range(1, RO):
+        ms(T.Zj[:, n * ZW + L:n * ZW + ZT], 0.0, ["zjF%d" % n])
     ts(T.pi[:, 1:2], T.pi[:, 0:1], 15, ALU.bitwise_and, ["pi0"], ["pi1"])
     ts(T.pi[:, 2:3], T.pi[:, 0:1], 112, ALU.bitwise_and, ["pi0"], ["pi2"])
     ts(T.pi[:, 3:4], T.pi[:, 0:1], 7, ALU.bitwise_and, ["pi0"], ["pi3"])
-    ts(T.pi[:, 4:5], T.pi[:, 0:1], 3, ALU.logical_shift_right, ["pi0"], ["pi4"], 1, ALU.bitwise_and)
-    cp(T.pf[:, 0:5], T.pi[:, 0:5], ["pi0", "pi1", "pi2", "pi3", "pi4"], ["pf"])
-    pc, kc, gc_, a8, ah = (T.pf[:, i:i + 1] for i in range(5))
+    ts(T.pi[:, 4:5], T.pi[:, 0:1], 3, ALU.logical_shift_right, ["pi0"], ["pi4"])
+    ts(T.pi[:, 5:6], T.pi[:, 0:1], 2, ALU.logical_shift_right, ["pi0"], ["pi5"], 3, ALU.bitwise_and)
+    ts(T.pi[:, 6:7], T.pi[:, 0:1], 3, ALU.bitwise_and, ["pi0"], ["pi6"])
+    cp(T.pf[:, 0:7], T.pi[:, 0:7], ["pi%d" % i for i in range(7)], ["pf"])
+    pc, kc, gc_, a8, p8, p4, p3 = (T.pf[:, i:i + 1] for i in range(7))
+    ts(T.idc[:], T.lc[:], pc, ALU.is_equal, ["lc", "pf"], ["idc"])
     ts(T.idb[:], T.xr[:, 0:L], pc, ALU.is_equal, ["xr", "pf"], ["idb"])
-    for k in range(16):
-        act(T.EC[:, k::16], T.idb[:], ID, ["idb"], ["EC%d" % k])
-    ECK = ["EC%d" % k for k in range(16)]
-    ts(T.pf[:, 5:6], gc_, 8.0, ALU.mult, ["pf"], ["pf5"], kc, ALU.add)
-    ts(T.pf[:, 6:7], a8, 16.0, ALU.mult, ["pf"], ["pf6"], 15.0, ALU.add)
-    ts(T.pf[:, 7:8], kc, 8.0, ALU.mult, ["pf"], ["pf7"])
-    ts(T.pf[:, 8:9], a8, 16.0, ALU.mult, ["pf"], ["pf8"], ah, ALU.add)
-    ts(T.pf[:, 9:10], kc, -1.0, ALU.mult, ["pf"], ["pf9"], 8.0, ALU.add)
-    ts(T.pf[:, 10:11], kc, SGN3 / L - 0.5, ALU.is_lt, ["pf"], ["pf10"], -16.0, ALU.mult)
-    ts(T.BO[:], T.xq[:], gc_, ALU.is_equal, ["xq", "pf"], ["cBO"])
-    ms(T.ones[:], 1.0, ["ones"])
-    ts(T.WB[:], T.xr[:], -15.0, ALU.add, ["xr", "pf"], ["WB"], gc_, ALU.is_equal)
-    ts(T.pf[:, 11:12], T.pf[:, 10:11], 2048.0, ALU.add, ["pf10"], ["pf11"])
-    send("iZ", ["zs"])
-    cp(T.Th[:], T.tr32[:], ["tr32"], ["Th"])
+    ts(T.pf[:, 8:9], p3, 16.0, ALU.mult, ["pf"], ["pf8"], p4, ALU.add)
+    ts(T.pf[:, 9:10], a8, 16.0, ALU.mult, ["pf"], ["pf9"], 15.0, ALU.add)
+    ts(T.pf[:, 10:11], a8, 16.0, ALU.mult, ["pf"], ["pf10"], p8, ALU.add)
+    ts(T.pf[:, 11:12], kc, -1.0, ALU.mult, ["pf"], ["pf11"], 8.0, ALU.add)
+    ts(T.pf[:, 12:13], kc, 2.0, ALU.mult, ["pf"], ["pf12"], float(SP), ALU.add)
+    ts(T.pf[:, 13:14], kc, float(W), ALU.add, ["pf"], ["pf13"])
+    ts(T.pf[:, 14:15], T.pf[:, 8:9], 2.0, ALU.mult, ["pf8"], ["pf14"], 1.0, ALU.add)
+    ts(T.pf[:, 15:16], kc, 4.0, ALU.mult, ["pf"], ["pf15"])
+    ts(T.cP0[:], T.x8[:, 0:8], T.pf[:, 8:9], ALU.add, ["x8a", "pf8"], ["cP0"])
+    ts(T.cIn[:], T.x8[:, 16:24], T.pf[:, 15:16], ALU.add, ["x8c", "pf15"], ["cIn"])
+    cp(T.Th[:], (T.tr32[:], T.cP0[:]), ["tr32", "cP0"], ["Th"])
     send("iT", ["Th"])
+    send("iZ", ["zs"])
+    ms(T.Cs[:], 0.0, ["cs"])
     ts(T.Cs[:, 0:1], T.cap32[:], -200.0, ALU.add, ["cap32", "cs"], ["cs"])
     send("iC", ["cs"])
-
-    def fill(out, n, c, w):
-        op("G", lambda: g.iota(out, [[0, n]], c, 0, allow_small_or_imprecise_dtypes=True), (), w)
-    fill(T.X[:, W:XW], L, 0, ["Xd"])
-    fill(T.FB[:, 0:8], 8, 0, ["FB"])
-    fill(T.F6[:], 8, 6, ["F6"])
-    fill(T.c4k[:], 8, 4096, ["c4k"])
-    fill(T.ids[:], L, 1 if S2PE else -1, ["ids"])
     send("bk0", ["X"])
     send("bk1", ["X"])
-    op("X", None, (), ["Xsent"], ("bulk", total["bulk"]))
-    for i in range(W // Q):
-        dma("Y", T.man[:, i * Q:(i + 1) * Q], T.mv[:], ["X"], ["man%d" % i])
+    op("X", None, (), ["Xsent"], ("bulk", total["bulk"]), lat=0, soft={sent_at["bk0"]: 3000, sent_at["bk1"]: 3000})
+    arrive("iT", ["tc00", "tc01"])
+    arrive("iZ", ["zc0"])
+    arrive("iC", ["caph"])
+    send("fZ", ["zc0"])
+    arrive("fZ", ["zj0"])
+    arrive("bk0", ["XR0"])
+    arrive("bk1", ["XR1"])
+    dma("Y", T.mv32[:], "mv", ["zc0"], ["mv32"], 2 * LOAD)
+    cp(T.man[:, 0:Q], T.mv32[:], ["mv32"], ["man0"])
+    for i in range(1, W // Q):
+        act(T.man[:, i * Q:(i + 1) * Q], T.man[:, 0:Q], ID, ["man0"], ["man%d" % i])
     MAN = ["man%d" % i for i in range(W // Q)]
-    x8 = T.xr[:, 0:8]
-    sg2 = -1.0 if S2PE else 1.0
-    ts(T.capf[:, 0:1], T.cap32[:], -200.0, ALU.add, ["cap32"], ["capm"])
+    ts(T.WB[:], T.xr[:], -15.0, ALU.add, ["xr", "pf"], ["WB"], gc_, ALU.is_equal)
+    for k in range(16):
+        if k % 2:
+            act(T.ECp[:, k::16], T.idc[:], ID, ["idc"], ["ECp%d" % k])
+        else:
+            cp(T.ECp[:, k::16], T.idc[:], ["idc"], ["ECp%d" % k])
+        act(T.ECn[:, k::16], T.idb[:, S0 // 16:L], ID, ["idb"], ["ECn%d" % k])
+    ECP = ["ECp%d" % k for k in range(16)]
+    ECN = ["ECn%d" % k for k in range(16)]
+    ts(T.capf[:, 0:1], T.cap32[:], -1.0, ALU.mult, ["cap32"], ["capb"], 150.0, ALU.add)
     ts(T.capf[:, 1:2], T.cap32[:], 1.0, ALU.add, ["cap32"], ["capp"])
-    ts(T.capf[:, 2:3], T.cap32[:], -200.0, ALU.add, ["cap32"], ["cap2"], sg2, ALU.mult)
-    ts(T.cTm[:], x8, 16.0, ALU.mult, ["xr", "pf5"], ["cTm"], T.pf[:, 5:6], ALU.add)
-    ms(T.C15[:], 1.0, ["C15"])
-    ts(T.Dm[:], T.xr[:, 0:16], kc, ALU.is_equal, ["xr", "pf"], ["Dm"])
-    ts(T.Dm2[:], T.xr[:, 1:17], kc, ALU.is_equal, ["xr", "pf"], ["Dm2"])
-    ms(T.C15[:, 15::16], 0.0, ["C15"], ["C15"])
-    tt(T.Dm[:], T.Dm[:], T.Dm2[:], ALU.subtract, ["Dm", "Dm2"], ["Dm"])
-    ts(T.cPA[:], x8, 0.0, ALU.mult, ["xr", "pf6"], ["cPA"], T.pf[:, 6:7], ALU.add)
-    ts(T.cEx[:], x8, 0.0, ALU.mult, ["xr", "pf"], ["cEx"], a8, ALU.add)
-    ts(T.cPm[:], x8, T.pf[:, 7:8], ALU.add, ["xr", "pf7"], ["cPm"])
-    ts(T.dum[:], x8, T.pf[:, 7:8], ALU.add, ["xr", "pf7"], ["dum"], float(W), ALU.add)
-    ts(T.dumm[:], x8, T.pf[:, 7:8], ALU.add, ["xr", "pf7"], ["dumm"])
-    ts(T.dumz[:], x8, T.pf[:, 7:8], ALU.add, ["xr", "pf7"], ["dumz"], float(XW), ALU.add)
-    ts(T.cUn[:], x8, 2.0, ALU.mult, ["xr", "pf8"], ["cUn"], T.pf[:, 8:9], ALU.add)
+    ts(T.capf[:, 2:3], T.cap32[:], 0.0, ALU.add, ["cap32"], ["capo"])
+    act(T.capf[:, 3:4], T.Ch[:, 0:1], ID, ["caph"], ["capH"], bias=200.0)
+    act(T.capf[:, 4:5], T.Ch[:, 0:1], ID, ["caph"], ["capJ"], bias=-50.0, scale=-1.0)
+    x8 = T.xr[:, 0:8]
+    ts(T.cP1[:], x8, 8.0, ALU.mult, ["xr", "pf14"], ["cP1"], T.pf[:, 14:15], ALU.add)
+    cp(T.cTm[:], T.x8[:, 8:16], ["x8b"], ["cTm"])
+    ts(T.cPA[:], x8, 0.0, ALU.mult, ["xr", "pf9"], ["cPA"], T.pf[:, 9:10], ALU.add)
+    cp(T.cEx[:], x8, ["xr"], ["cEx"])
+    ts(T.Dm[:, 0:16], T.xr[:, 0:16], kc, ALU.is_equal, ["xr", "pf"], ["Dm"])
+    ts(T.Dm[:, 16:32], T.xr[:, 1:17], kc, ALU.is_equal, ["xr", "pf"], ["Dm2"])
+    tt(T.Dm[:, 0:16], T.Dm[:, 0:16], T.Dm[:, 16:32], ALU.subtract, ["Dm", "Dm2"], ["Dm"])
+    dum, dumz = T.dum[:, 0:8], T.dum[:, 8:16]
+    ts(dum, x8, 32.0, ALU.mult, ["xr", "pf12"], ["dum"], T.pf[:, 12:13], ALU.add)
+    ts(dumz, x8, 16.0, ALU.mult, ["xr", "pf13"], ["dumz"], T.pf[:, 13:14], ALU.add)
+    ts(T.BO[:], T.xq[:], gc_, ALU.is_equal, ["xq", "pf"], ["cBO"])
     ts(T.mA[:], T.xm[:], kc, ALU.is_equal, ["xm", "pf"], ["mA"])
-    ts(T.TRI[:], T.xr[:, 0:L], pc, ALU.is_le, ["xr", "pf"], ["TRI"], 4096.0, ALU.mult)
+    ts(T.mK[:], T.xk[:], kc, ALU.is_equal, ["xk", "pf"], ["mK"])
+    ts(T.TRI[:], T.lx[:], T.pf[:, 10:11], ALU.is_le, ["lx", "pf10"], ["TRI"], 4096.0, ALU.mult)
     for gg in range(8):
         ts(T.SEL[:, gg * L:(gg + 1) * L], T.ones[:], T.BO[:, 16 * gg:16 * gg + 1], ALU.mult, ["ones", "cBO"], ["SEL%d" % gg])
     SELK = ["SEL%d" % gg for gg in range(8)]
     ts(T.NSEL[:], T.SEL[:], -1.0, ALU.mult, SELK, ["NSEL"])
-    op("G", lambda: g.affine_select(T.ids[:], T.ids[:], [[-1, L]], ALU.is_equal, 0.0, 0, 1), ["ids"], ["ids"])
-    act(T.Tm[:], T.EC[:, 0:1024], ID, ECK, ["Tm"], scale=0.0)
-    act(T.idf[:], T.idb[:], ID, ["idb"], ["idf"])
-    act(T.idp[:], T.idb[:], ID, ["idb"], ["idp"], scale=2048.0)
-    act(T.idq[:], T.idb[:], ID, ["idb"], ["idq"], scale=-2048.0)
-    act(T.WS[:], T.WB[:], ID, ["WB"], ["WS"], scale=2048.0)
-    act(T.id4[:], T.idb[:], ID, ["idb"], ["id4"], scale=4.0)
-    act(T.id5[:], T.idb[:], ID, ["idb"], ["id5"], scale=5.0)
-
-    def late_constants():
-        fill(T.KB[:, 0:8], 8, 0, ["KB"])
-        fill(T.cMx[:], L, 16000000, ["cMx"])
-        op("G", lambda: g.affine_select(T.rst[:], T.ones[:], [[0, 8], [1, 16]], ALU.is_gt, 0.0, 0, 0), ["ones"], ["rst"])
-        op("G", lambda: g.affine_select(T.cMx[:], T.cMx[:], [[0, 8], [1, 16]], ALU.is_gt, -1.0, 0, 0), ["cMx"], ["cMx"])
-        fill(T.XR[:, W:XW], L, 0, ["XRd"])
-        for n in range(1, RO + 1):
-            fill(T.Zj[:, n * ZW + L:n * ZW + 144], 16, 0, ["zjF%d" % n])
-        fill(T.TK[:], 256, 0, ["TK"])
-        fill(T.AP2[:], 256, 0, ["AP0", "ap"])
+    ts(T.rst[:], T.xk[:], 0.0, ALU.is_gt, ["xk"], ["rst"])
+    ts(T.cMx[:], T.xk[:], 0.0, ALU.is_gt, ["xk"], ["cMx"], 17000000.0, ALU.mult)
+    ts(T.cMx[:], T.cMx[:], -1000000.0, ALU.add, ["cMx"], ["cMx"])
+    ts(T.spT[:], T.xq[:], 2.0, ALU.mult, ["xq", "pf12"], ["spT"], T.pf[:, 12:13], ALU.add)
+    act(T.Tm[:], T.ECp[:, 0:1024], ID, ECP, ["Tm"], scale=0.0)
+    for buf, c in ((T.idf, 1.0), (T.idp, 2048.0), (T.idq, -2048.0), (T.idu, UNIT), (T.id4, 4.0), (T.id5, 5.0)):
+        act(buf[:], T.idb[:], ID, ["idb"], [buf.name], scale=c)
+    act(T.WS[:], T.WB[:], ID, ["WB"], ["WS"], scale=0.25)
+    act(T.WU[:], T.WB[:], ID, ["WB"], ["WU"], scale=UNIT)
 
     def wband(buf, k):
         return buf[:, 15 - k:143 - k]
 
-    def thr_transposed(A, TT, ka, kt, z, zk, capcol, capk, sign, tmp, tk, on="S"):
-        if on == "S":
-            act(A[:], z, ID, zk + capk, [ka], bias=capcol, scale=-sign)
-        else:
-            ts(A[:], z, -sign, ALU.mult, zk + capk, [ka], capcol, ALU.add)
-        mm(tmp, A[:], T.idb[:], True, True, [ka, "idb"], [tk])
-        if on == "S":
-            act(TT[:], tmp, ID, [tk], [kt])
-        else:
-            cp(TT[:], tmp, [tk], [kt])
-
-    def thr_bank(TT, kt, b, stop):
-        mm(T.PT[:, 512 * b:512 * b + 512], TT[:], T.EC[:, 512 * b:512 * b + 512], True, stop, [kt] + ECK, ["B%d" % b])
-
     def quarters(z, zk, a1, a, ak, n, tag):
-        act(a1[:], z.indirect(T.cPm[:]), ID, zk + ["cPm"], ["a1" + tag], bias=128.625, scale=0.25)
+        act(a1[:], z, ID, zk, ["a1" + tag], bias=128.625, scale=0.25)
         act(n[:], a1[:], ID, ["a1" + tag], ["n" + tag], bias=384.0, scale=-1.0)
         act(a, a1[:], ID, ["a1" + tag], [ak], bias=-129.0)
 
@@ -352,347 +422,285 @@ def rank_program(g, core, T, topo):
 
     def dpos(gg, n=1):
         if gg >= nv:
-            c = (gg - nv) * L
-            return T.PT[:, c:c + n * L], "B0"
+            c = 1024 + (gg - nv) * L
+            return T.PT[:, c:c + n * L], "B2"
         h = gg // half
         c = 512 * h + (gg - h * half) * L
         return T.PD[:, c:c + n * L], "B%d" % (4 + h)
     runs = [(0, half), (half, nv)] + ([(nv, 8)] if EQS else [])
+    TH = ["th%d" % k for k in range(16)]
 
-    def tri(a, b):
-        for gg in range(a, b):
-            o, bk = dpos(gg)
-            mm(o, T.idb[:], T.TRI[:], gg == a, False, ["idb", "TRI"], [bk])
+    def bank2(a, b):
+        c = (a + 1024) % W
+        return T.PT[:, c:c + b - a], "B%d" % (c // 512)
 
-    def th3_piece(k, zj, zjk):
-        act(T.th3[:, k::16], zj, RELU, [zjk, "capp"], ["th3_%d" % k], bias=T.capf[:, 1:2], scale=-1.0)
-    TH3 = ["th3_%d" % k for k in range(16)]
-    B2ORDER = [1, 0, 2, 3]
+    def spread(lhs, lk, pieces):
+        for n, (a, b) in enumerate(pieces):
+            mm(T.PT[:, 512 * n:512 * n + b - a], lhs, T.ECn[:, a - S0:b - S0], [lk] + ECN, "B%d" % n)
 
-    tri(*runs[0])
-    tri(*runs[1])
-    arrive("iZ", ["zc0"])
-    arrive("iT", ["tc0"])
-    arrive("iC", ["caph"])
-    send("fZ", ["zc0"])
-    arrive("fZ", ["zj0"])
-    arrive("bk0", ["XR0"])
-    arrive("bk1", ["XR1"])
-    thr_transposed(T.thA, T.thT, "thA", "thT", T.Zc[:, 0:L], ["zc0"], T.capf[:, 2:3], ["cap2"], sg2, T.P6[:, 0:L], "B6", "V")
-    for b in B2ORDER:
-        thr_bank(T.thT, "thT", b, not S2PE)
+    cp(T.hp[:, 0:L], T.Tc[:, 0:L], ["tc00", "tc01"], ["hp"])
+    cp(T.To[:], (T.hp[:, 0:L], T.cIn[:]), ["hp", "cIn"], ["To"])
+    mm(T.P7[:, 0:L], T.Zc[:, 0:L], T.idb[:], ["zc0", "idb"], "B7")
+    act(T.Zc[:, ZT:ZR], T.P7[:, 0:L], ID, ["B7"], ["zt0"], bias=-150.0)
+    quarters(T.Zj[:, 0:L], ["zj0"], T.a1j, T.SVs[:, L:256], "a30", T.nj, "j")
 
     for r in range(RO):
         last = r == RO - 1
         s = lambda n: slice(r * n, (r + 1) * n)
         rs, ns, zn = str(r), str(r + 1), (r + 1) * ZW
-        tck, tjk = "tc" + rs, "tj" + rs
+        tjk = "tj" + rs
         zc, zck = T.Zc[:, r * ZW:r * ZW + L], "zc" + rs
+        zt, ztk = T.Zc[:, r * ZW + ZT:r * ZW + ZR], ("zt0" if r == 0 else zck)
         zj, zjk = T.Zj[:, r * ZW:r * ZW + L], "zj" + rs
         Fc, Fck = (T.F6[:, 0:1], "F6") if r == 0 else (T.Zc[:, r * ZW + L:r * ZW + L + 1], zck)
         Fj, Fjk = (T.F6[:, 0:1], "F6") if r == 0 else (T.Zj[:, r * ZW + L:r * ZW + L + 1], "zjF" + rs)
-        mn2, a2 = T.V2s[:, r * 256:r * 256 + L], T.V2s[:, r * 256 + L:r * 256 + 256]
+        mn2, a2 = T.mn2[:], T.a2[:]
         mn3, a3 = T.SVs[:, r * 256:r * 256 + L], T.SVs[:, r * 256 + L:r * 256 + 256]
-        send("fT" + rs, [tck])
+        tsrc, tsk = (T.To[:], ["To"]) if r == 0 else (T.Tn[:, 1::2], ["Tn0", "Tn1"])
+        cp((T.Tm[:], T.cTm[:]), tsrc, tsk + ["cTm", "Tm"], ["Tm"])
+        cp(T.Tc[:, r * 256 + L:r * 256 + 256], tsrc, tsk, ["tn" + rs])
+        send("fT" + rs, ["tc%d0" % r, "tc%d1" % r, "tn" + rs])
         arrive("fT" + rs, [tjk])
-        if r == 0:
-            late_constants()
-
-        def off2(a, b):
-            return Xw.indirect(T.Tc[:, r * L + a // 16:r * L + b // 16])
-        if r == 0:
-            cp(T.To[:], T.Tc[:, 0:L], [tck], ["To"])
-            cp(T.Tm[:].indirect(T.cTm[:]), T.To[:], ["To", "cTm", "Tm"], ["Tm"])
-        else:
-            cp(T.Tm[:].indirect(T.cTm[:]), T.Tn[:, 1::2], ["Tn", "cTm", "Tm"], ["Tm"])
-        ts(T.xs[:, V2[0]:V2[1]], off2(*V2), -200.0, ALU.add, XK + [tck], cols("xs", *V2))
-        for a, b in CH2:
-            act(T.xs[:, a:b], off2(a, b), ID, XK + [tck], cols("xs", a, b), bias=-200.0)
-        quarters(zc, [zck], T.a1, a2, "a2" + rs, T.nc, "c")
-        act(T.fc[:, 0:1], Fc, ID, [Fck], ["fc0"], bias=-0.5)
-        act(T.fc[:, 1:2], Fc, ID, [Fck], ["fc1"], bias=-8.5)
-
-        def xacc(bk):
-            for a, b in [V2] + CH2:
-                if a // 512 == bk:
-                    mm(T.PT[:, a:b], T.idb[:], T.xs[:, a:b], False, b % 512 == 0, ["idb"] + cols("xs", a, b), [bank(a)])
-
-        def marks(bk):
-            a, b = 512 * bk, 512 * bk + 512
-            if S2PE:
-                scan(T.bo[:, a:b], T.PT[:, a:b], T.C15[:], ALU.max, ALU.min, [bank(a), "C15"], cols("bo", a, b))
-            else:
-                tt(T.bb[:, a:b], T.xs[:, a:b], T.PT[:, a:b], ALU.is_gt, cols("xs", a, b) + [bank(a)], cols("bb", a, b))
-                scan(T.bo[:, a:b], T.bb[:, a:b], T.C15[:], ALU.max, ALU.min, cols("bb", a, b) + ["C15"], cols("bo", a, b))
-
-        def counts(n):
-            bk = B2ORDER[n]
-            for mu in range(4 * bk, 4 * bk + 4):
-                mm(T.P7[:, 0:L], wband(T.WB, mu), T.bo[:, mu * L:(mu + 1) * L], n == 0 and mu % 4 == 0, n == 3 and mu % 4 == 3,
-                   ["WB", "bo%d" % mu], ["B7"])
-        def diffs(a, b):
-            for lam in range(a, b):
-                mm(T.P6[:, 16 * lam:16 * lam + 16], T.Tm[:, lam::8], T.Dm[:], True, True, ["Tm", "Dm"], ["B6"])
-        for n, bk in enumerate(B2ORDER):
-            diffs(DDAT[n], DDAT[n + 1])
-            if S2PE:
-                xacc(bk)
-            marks(bk)
-            if n >= 2:
-                counts(n - 2)
-        counts(2)
-        if EQS:
-            tri(*runs[2])
-        counts(3)
-        act(T.DDs[:, s(L)], T.P6[:, 0:L], ID, ["B6"], ["dds" + rs])
+        for lam in range(8):
+            mm(T.P7[:, 16 * lam:16 * lam + 16], T.Tm[:, lam::8], T.Dm[:, 0:16], ["Tm", "Dm"], "B7")
+        act(T.DDs[:, s(L)], T.P7[:, 0:L], ID, ["B7"], ["dds" + rs])
         send("dd" + rs, ["dds" + rs])
-        todo3 = list(range(0 if r == 0 else TH3EARLY, 16))
-        if r == 0:
-            quarters(zj, [zjk], T.a1j, a3, "a3" + rs, T.nj, "j")
-        for k in todo3[:4]:
-            th3_piece(k, zj, zjk)
-        todo3 = todo3[4:]
+        for n in range(4):
+            o, bk = bank2(512 * n, 512 * n + 512)
+            mm(o, zt, T.ECp[:, 512 * n:512 * n + 512], [ztk] + ECP, bk)
+        for word in (NEXT2 if r else FIRST2).split():
+            a, b = (int(x) for x in word[1:].split(":"))
+            src = (Xl, T.Tc[:, r * 256 + a // 16:r * 256 + b // 16])
+            rk = ["X", "capb", "tc%d%d" % (r, a // 1024)]
+            if word[0] == "V":
+                ts(T.xs[:, a:b], src, T.capf[:, 0:1], ALU.add, rk, cols("xs", a, b))
+            else:
+                act(T.xs[:, a:b], src, ID, rk, cols("xs", a, b), bias=T.capf[:, 0:1])
+            o, bk = bank2(a, b)
+            mm(o, T.idb[:], T.xs[:, a:b], ["idb"] + cols("xs", a, b), bk)
+        for a in range(0, W, 512):
+            o, bk = bank2(a, a + 512)
+            scan(T.bo[:, a:a + 512], o, T.C15[:], ALU.max, ALU.min, [bk, "C15"], cols("bo", a, a + 512))
+        for u in range(32):
+            mm(T.P6[:, 64 * (u // 16):64 * (u // 16) + 64], wband(T.WB, u % 16), T.bo[:, 64 * u:64 * u + 64], ["WB", "bo%d" % u], "B6")
+        quarters(zc, [zck], T.a1, a2, "a2", T.nc, "c")
+        act(T.fc[:, 0:2], T.fc[:, 8:10], ID, [Fck, "fb0", "fb1"], ["fc0"], bias=Fc)
         if r == 1:
-            cp(XRw.indirect(T.SO[:, 0:8]), T.SV[:, 0:L], ["so0", "sv0", "XR"], ["XR"])
-        ts(T.FB[:, 1:129], T.P7[:, 0:L], Fc, ALU.is_ge, ["B7", Fck, "FB"], ["FB"])
+            cp((XRw, T.SO[:, 0:8]), T.SV[:, 0:L], ["so0", "sv0", "XR"], ["XR"])
+        ts(T.FB[:, 1:129], T.P6[:, 0:L], Fc, ALU.is_ge, ["B6", Fck, "FB"], ["FB"])
+        act(T.NFs[:, s(L)], T.P6[:, 0:L], SIGN, ["B6", "fc0"], ["nfs" + rs], bias=T.fc[:, 0:1], scale=-1.0)
         scan(T.ys[:], T.FB[:, 0:L], T.DDs[:, s(L)], ALU.mult, ALU.add, ["FB", "dds" + rs], ["ys"])
-        act(T.NFs[:, s(L)], T.P7[:, 0:L], SIGN, ["B7", "fc0"], ["nfs" + rs], bias=T.fc[:, 0:1], scale=-1.0)
-        tt(T.PA[:], T.ys[:].indirect(T.cPA[:]), T.mA[:], ALU.mult, ["ys", "cPA", "mA"], ["PA"])
-        for k in todo3[:5]:
-            th3_piece(k, zj, zjk)
-        for a, b in ([runs[0]] + runs[2:] + [runs[1]] if EQMID else runs):
+        tt(T.PA[:], (T.ys[:], T.cPA[:]), T.mA[:], ALU.mult, ["ys", "cPA", "mA"], ["PA"])
+        cp(T.Pu[:], T.ys[:, 15::16], ["ys"], ["Pu"])
+        tt(mn2, (Xl, T.Pu[:]), T.nc[:], ALU.min, ["X", "Pu", "nc"], ["mn2"])
+        if not last:
+            tt(T.V2s[:, s(L)], mn2, a2, ALU.add, ["mn2", "a2"], ["v2s" + rs])
+        for n, (a, b) in enumerate(runs):
             for gg in range(a, b):
                 o, bk = dpos(gg)
-                mm(o, T.NSEL[:, gg * L:(gg + 1) * L], T.PA[:], False, False, ["NSEL", "PA"], [bk])
+                mm(o, T.idb[:], T.TRI[:], ["idb", "TRI"], bk)
+                mm(o, T.NSEL[:, gg * L:(gg + 1) * L], T.PA[:], ["NSEL", "PA"], bk)
             o, bk = dpos(a, b - a)
-            mm(o, T.PA[:], T.SEL[:, a * L:b * L], False, True, SELK + ["PA"], [bk])
-        cp(T.Pu[:], T.ys[:, 15::16], ["ys"], ["Pu"])
-        tt(mn2, Xw.indirect(T.Pu[:]), T.nc[:], ALU.min, XK + ["Pu", "nc"], ["mn2" + rs])
-        if not last:
-            send("v2" + rs, ["mn2" + rs, "a2" + rs])
-        for n, (a, b) in enumerate(runs):
-            o, bk = dpos(a, b - a)
+            mm(o, T.PA[:], T.SEL[:, a * L:b * L], SELK + ["PA"], bk)
             if n < 2:
                 ts(T.eq[:, a * L:b * L], o, 0.0, ALU.is_equal, [bk], ["eq%d" % n])
             else:
                 act(T.ab[:, 0:EQS * L], o, ABS, [bk], ["ab"])
                 act(T.eq[:, a * L:b * L], T.ab[:, 0:EQS * L], RELU, ["ab"], ["eq2"], bias=1.0, scale=-1.0)
-        mm(T.PT[:, 1024:1032], T.idf[:], T.ys[:, 15::16], True, False, ["idf", "ys"], ["B2"])
-        mm(T.PT[:, 512:640], T.idb[:], T.xs[:, 15::16], True, False, ["idb"] + cols("xs", 0, W), ["B1"])
-        mm(T.PT[:, 512:640], T.idp[:], T.bo[:, 14::16], False, False, ["idp"] + cols("bo", 0, W), ["B1"])
-        mm(T.PT[:, 512:640], T.ids[:], T.thA[:], False, True, ["ids", "thA"], ["B1"])
-        act(T.s15[:], T.PT[:, 512:640], SIGN, ["B1"], ["s15"], bias=-0.5)
+        mm(T.PT[:, 1536:1544], T.idf[:], T.ys[:, 15::16], ["idf", "ys"], "B3")
         for c in range(8):
-            mm(T.PT[:, 1024 + c:1025 + c], T.eq[:, c::8], T.c4k[:, 0:1], False, c == 7, ["eq0", "eq1", "eq2", "c4k"], ["B2"])
-        cp(T.TD[:, 1::2], T.Tj[:, s(L)], [tjk], ["Tf"])
-        tt(T.Ofs[:, s(8)], T.PT[:, 1024:1032], T.dum[:], ALU.min, ["B2", "dum"], ["ofs" + rs])
-        cp(T.Ous[:, s(8)], T.Ofs[:, s(8)], ["ofs" + rs], ["ous" + rs])
-        tt(Xw.indirect(T.Ous[:, s(8)]), mn2, a2, ALU.add, ["ous" + rs, "mn2" + rs, "a2" + rs, "Xsent"] + XK, ["X"])
+            mm(T.PT[:, 1536 + c:1537 + c], T.eq[:, c::8], T.c4k[:, 0:1], ["eq0", "eq1", "eq2", "c4k"], "B3")
+        tt(T.Ofs[:, 0:8], T.PT[:, 1536:1544], dum, ALU.min, ["B3", "dum"], ["ofs"])
+        cp(T.Ous[:, s(8)], T.Ofs[:, 0:8], ["ofs"], ["ous" + rs])
+        tt((Xw, T.Ous[:, s(8)]), mn2, a2, ALU.add, ["ous" + rs, "mn2", "a2", "Xsent"] + XK, XK)
         send("oj" + rs, ["ous" + rs])
-        send("of" + rs, ["ofs" + rs])
         if not last:
+            send("v2" + rs, ["v2s" + rs])
             send("orp" + rs, ["ous" + rs])
-        for k in todo3[5:]:
-            th3_piece(k, zj, zjk)
+        o15 = T.PT[:, 0:L]
+        mm(o15, T.idb[:], T.xs[:, 15::16], ["idb"] + cols("xs", 0, W), "B0")
+        mm(o15, T.idp[:], T.bo[:, 14::16], ["idp"] + cols("bo", 0, W), "B0")
+        mm(o15, zt, T.idc[:], [ztk, "idc"], "B0")
+        for h in range(2):
+            act(T.s15[:, h::2], T.PT[:, 64 * h:64 * h + 64], SIGN, ["B0"], ["s15%d" % h], bias=-0.5)
         for mu in range(16):
-            mm(T.PT[:, 1536:1544], wband(T.WB, mu), T.s15[:, 8 * mu:8 * mu + 8], mu == 0, mu == 15, ["WB", "s15"], ["B3"])
-        act(T.fc[:, 2:3], Fj, ID, [Fjk, "pf11"], ["fc2"], bias=T.pf[:, 11:12], scale=2.0)
-        act(T.NFs[:, r * L + 15:(r + 1) * L:16], T.PT[:, 1536:1544], SIGN, ["B3", "fc1", "nfs" + rs], ["nfs" + rs], bias=T.fc[:, 1:2], scale=-0.5)
-        send("nf" + rs, ["nfs" + rs])
-        if not last:
-            send("sa" + rs, ["a3" + rs])
-        mm(T.PD[:, 0:L], T.BO[:], zj, True, False, ["cBO", zjk], ["B4"])
-        mm(T.PD[:, 0:L], T.id5[:], T.TD[:, 1::2], False, True, ["id5", "Tf"], ["B4"])
-        mm(T.PD[:, 512:640], T.BO[:], zj, True, False, ["cBO", zjk], ["B5"])
-        mm(T.PD[:, 512:640], T.id4[:], T.TD[:, 1::2], False, False, ["id4", "Tf"], ["B5"])
-        act(T.qq[:], T.PD[:, 0:L], ID, ["B4"], ["qq"], bias=128.500732421875, scale=1.0 / 2048)
-        for nm in ("dd", "nf", "oj", "of"):
+            mm(T.PT[:, 512:520], wband(T.WB, mu), T.s15[:, 8 * mu:8 * mu + 8], ["WB", "s150", "s151"], "B1")
+        for h in range(2):
+            act(T.NFs[:, r * L + 64 * h + 15:r * L + 64 * h + 64:16], T.PT[:, 512 + h:520:2], SIGN,
+                ["B1", "fc0", "nfs" + rs], ["nf%s%d" % (rs, h)], bias=T.fc[:, 1:2], scale=-0.5)
+        send("nf" + rs, ["nfs" + rs, "nf%s0" % rs, "nf%s1" % rs])
+        for nm in ("dd", "nf", "oj"):
             arrive(nm + rs, [nm + rs])
         NF = T.NF[:, s(L)]
-        for n, (a, b) in enumerate(CH3):
-            tt(T.xs[:, a:b], Xw.indirect(T.Tj[:, r * L + a // 16:r * L + b // 16]), T.th3[:, a:b], ALU.subtract,
-               XK + [tjk] + TH3, cols("xs", a, b))
+        v3 = S3[0][0]
+        act(T.t3[:], (zj, T.cP0[:]), RELU, [zjk, "cP0", "capp"], ["t3"], bias=T.capf[:, 1:2], scale=-1.0)
+        mm(T.P7[:, L:2 * L], T.t3[:], T.idb[:], ["t3", "idb"], "B7")
+        act(T.t3T[:], T.P7[:, L:2 * L], ID, ["B7"], ["t3T"], scale=-1.0)
+        spread(T.t3T[:], "t3T", S3)
+        for k in range(16):
+            act(T.th[:, k:v3:16], T.t3[:, 0:v3 // 16], ID, ["t3"], ["th%d" % k])
+        cp(T.TD[:, 1::2], T.Tj[:, r * 256 + L:r * 256 + 256], [tjk], ["Tf"])
+        mm(T.PD[:, 0:L], T.BO[:], zj, ["cBO", zjk], "B4")
+        mm(T.PD[:, 0:L], T.id5[:], T.TD[:, 1::2], ["id5", "Tf"], "B4")
+        act(T.qq[:], T.PD[:, 0:L], ID, ["B4"], ["qq"], bias=128.500732421875, scale=1.0 / 2048)
+        mm(T.PD[:, 512:640], T.BO[:], zj, ["cBO", zjk], "B5")
+        mm(T.PD[:, 512:640], T.id4[:], T.TD[:, 1::2], ["id4", "Tf"], "B5")
+        mm(T.PD[:, 512:640], T.idq[:], T.qq[:], ["idq", "qq"], "B5")
+        act(T.TD[:, 0::2], T.PD[:, 512:640], ID, ["B5"], ["dT"], bias=264193.0)
+        cp(T.Ofs[:, 8:16], T.Oj[:, s(8)], ["oj" + rs], ["of"])
+        mm(T.PD[:, 0:8], T.idf[:], T.Ofs[:, 8:16], ["idf", "of"], "B4")
+        mm(T.PD[:, 0:8], T.idp[:], T.NF[:, r * L + 15:(r + 1) * L:16], ["idp", "nf" + rs], "B4")
+        mm(T.PD[:, 0:8], T.idp[:], T.ones[:, 0:8], ["idp", "ones"], "B4")
+        tt(T.E[:, 0::32], T.PD[:, 0:8], dum, ALU.min, ["B4", "dum", "E0"], ["E0"])
+        act(T.fc[:, 3:4], Fj, ID, [Fjk], ["fc3"], bias=-5.0, scale=-1.0)
+        act(T.NFm[:], NF, ID, ["nf" + rs, "fc3"], ["NFm"], bias=T.fc[:, 3:4], scale=-6.0)
+        mm(T.P6[:, 0:L], T.idu[:], T.NFm[:], ["idu", "NFm"], "B6")
+        for a, b in V3:
+            tt(T.xs[:, a:b], (Xl, T.Tj[:, r * 256 + a // 16:r * 256 + b // 16]), T.th[:, a:b], ALU.subtract,
+               ["X", tjk] + TH, cols("xs", a, b))
             act(T.bo[:, a:b], T.xs[:, a:b], RELU, cols("xs", a, b), cols("bo", a, b), bias=1.0)
-            if b <= SGN3:
-                act(T.bb[:, a:b], T.xs[:, a:b], SIGN, cols("xs", a, b), cols("bb", a, b), bias=0.5)
-            else:
-                ts(T.bb[:, a:b], T.xs[:, a:b], 0.0, ALU.is_ge, cols("xs", a, b), cols("bb", a, b), 2.0, ALU.mult)
-            for which in ((0, 1) if b <= SGN3 else (1, 0)):
-                for mu in range(a // L, b // L):
-                    if which == 0:
-                        mm(T.P6[:, 0:L], wband(T.WS, mu), T.bo[:, mu * L:(mu + 1) * L], mu == 0, mu == 15, ["WS", "bo%d" % mu], ["B6"])
-                    else:
-                        mm(T.P7[:, 0:L], wband(T.WB, mu), T.bb[:, mu * L:(mu + 1) * L], mu == 0, mu == 15, ["WB", "bb%d" % mu], ["B7"])
-            if n == 0:
-                mm(T.PD[:, 512:640], T.idq[:], T.qq[:], False, True, ["idq", "qq"], ["B5"])
-            if n == len(CH3) - 2:
-                mm(T.P7[:, 0:L], T.idq[:], NF, False, False, ["idq", "nf" + rs], ["B7"])
-                act(T.TD[:, 0::2], T.PD[:, 512:640], ID, ["B5"], ["dT"], bias=264193.0)
-
-        def shadow_values():
-            tt(mn3, Xw.indirect(T.Oj[:, s(8)]), T.nj[:], ALU.min, XK + ["oj" + rs, "nj"], ["mn3" + rs])
-        shadow_values()
+            ts(T.bb[:, a:b], T.xs[:, a:b], 0.0, ALU.is_ge, cols("xs", a, b), cols("bb", a, b))
+        for n, (a, b) in enumerate(S3):
+            o = T.PT[:, 512 * n:512 * n + b - a]
+            act(T.xs[:, a:b], (Xl, T.Tj[:, r * 256 + a // 16:r * 256 + b // 16]), ID, ["X", tjk], cols("xs", a, b))
+            mm(o, T.idb[:], T.xs[:, a:b], ["idb"] + cols("xs", a, b), "B%d" % n)
+            act(T.bo[:, a:b], o, RELU, ["B%d" % n], cols("bo", a, b), bias=1.0)
+            ts(T.bb[:, a:b], T.bo[:, a:b], 0.5, ALU.is_ge, cols("bo", a, b), cols("bb", a, b))
+        for u in range(32):
+            c = slice(64 * (u // 16), 64 * (u // 16) + 64)
+            mm(T.P6[:, c], wband(T.WU, u % 16), T.bb[:, 64 * u:64 * u + 64], ["WU", "bb%d" % u], "B6")
+            mm(T.P7[:, c], wband(T.WS, u % 16), T.bo[:, 64 * u:64 * u + 64], ["WS", "bo%d" % u], "B7")
+        act(T.X[:, W:SP], zj, ID, [zjk], ["Xz"])
+        tt(mn3, (Xw, T.Oj[:, s(8)]), T.nj[:], ALU.min, XK + ["oj" + rs, "nj"], ["mn3" + rs])
+        tt(T.E[:, 1::2], T.P6[:, 0:L], T.spT[:], ALU.min, ["B6", "spT", "E1"], ["E1"])
+        scan(T.Es[:], T.rs2[:], T.E[:], ALU.mult, ALU.max, ["rs2", "E0", "E1"], ["Es"])
+        cp(T.SOs[:, s(8)], T.Es[:, 31::32], ["Es"], ["sos" + rs])
         if not last:
-            send("sv" + rs, ["mn3" + rs])
-        if r == 0:
-            act(T.id16[:], T.idb[:], ID, ["idb"], ["id16"], scale=16.0)
-        ts(T.ee[:], T.P7[:, 0:L], T.fc[:, 2:3], ALU.is_ge, ["B7", "fc2"], ["ee"])
-
-        def refused():
-            scan(T.rf[:], T.rst[:], T.ee[:], ALU.mult, ALU.max, ["rst", "ee"], ["rf"])
-            mm(T.PD[:, 0:8], T.idf[:], T.Of[:, s(8)], True, False, ["idf", "of" + rs], ["B4"])
-            mm(T.PD[:, 0:8], T.idp[:], T.NF[:, r * L + 15:(r + 1) * L:16], False, False, ["idp", "nf" + rs], ["B4"])
-            for n in range(2):
-                mm(T.PD[:, 0:8], T.idp[:], T.rf[:, 15::16], False, n == 1, ["idp", "rf"], ["B4"])
-            for n in range(2):
-                mm(T.PD[:, 512:520], T.idp[:], T.rf[:, 15::16], n == 0, n == 1, ["idp", "rf"], ["B5"])
-
-        def shadow_offsets():
-            tt(T.o3[:], T.PD[:, 0:8], T.dumm[:], ALU.min, ["B4", "dumm"], ["o3"])
-            ts(T.SOs[:, s(8)], T.o3[:], float(W), ALU.add, ["o3"], ["sos" + rs])
-        if not last:
-            refused()
-        tt(T.KB[:, 1:129], T.ee[:], T.P6[:, 0:L], ALU.mult, ["ee", "B6", "KB"], ["KB"])
-        if not last:
-            shadow_offsets()
+            send("sv" + rs, ["mn3" + rs, "a3" + rs])
             send("so" + rs, ["sos" + rs])
-        scan(T.P6[:, L:2 * L], T.KB[:, 0:L], T.cMx[:], ALU.max, ALU.min, ["KB", "cMx"], ["B6"])
-        if last:
-            z4, z4k, F4, F4k, cap4, cap4k = T.Zh[:, 0:L], "zh0", T.Zh[:, L:L + 1], "zh0", T.capf[:, 0:1], "capm"
-        else:
-            z4, z4k, F4, F4k, cap4, cap4k = zc, zck, Fc, Fck, T.Ch[:, 0:1], "caph"
-        act(T.X[:, XW:XZ], zj, ID, [zjk], ["Xz"])
-        thr_transposed(T.thA4, T.thT4, "thA4", "thT4", z4, [z4k], cap4, [cap4k], 1.0, T.P7[:, 0:L], "B7")
-        tt(T.ng3[:], T.KB[:, 1:129], T.P6[:, L:2 * L], ALU.is_le, ["KB", "B6"], ["ng3"])
+        tt(T.KB[:, 1:129], T.E[:, 1::2], T.P7[:, 0:L], ALU.min, ["E1", "B7", "KB"], ["KB"])
+        scan(T.P7[:, L:2 * L], T.KB[:, 0:L], T.cMx[:], ALU.max, ALU.min, ["KB", "cMx"], ["B7"])
+        tt(T.ng3[:], T.KB[:, 1:129], T.P7[:, L:2 * L], ALU.is_le, ["KB", "B7"], ["ng3"])
         scan(T.y3[:], T.ng3[:], T.DD[:, s(L)], ALU.mult, ALU.add, ["ng3", "dd" + rs], ["y3"])
         cp(T.Tmu[:], T.y3[:, 15::16], ["y3"], ["Tmu"])
-        cp(T.Vp[:], T.man[:].indirect(T.Tmu[:]), MAN + ["Tmu"], ["Vp"])
-        cp(T.Vs[:, s(L)], T.Vp[:].indirect(T.cUn[:]), ["Vp", "cUn"], ["vs" + rs])
+        cp(T.Vs[:, s(L)], (T.man[:], T.Tmu[:]), MAN + ["Tmu"], ["vs" + rs])
         send("V" + rs, ["vs" + rs])
-        for b in range(2 if last else 4):
-            thr_bank(T.thT4, "thT4", b, True)
-        if last:
-            refused()
-        act(T.tt[:], T.rf[:, 15::16], ID, ["rf"], ["tt"], bias=16.0, scale=-64.0)
-        v4 = V4L if last else V4
-        if not last:
-            act(T.th3[:, v4:W], T.PT[:, v4:W], ID, ["B3"], TH3, bias=200.0)
+        scan(T.rq[:], T.rst[:], T.E[:, 1::2], ALU.mult, ALU.max, ["rst", "E1"], ["rq"])
         scan(T.js[:], T.rst[:], NF, ALU.mult, ALU.add, ["rst", "nf" + rs], ["js"])
-        tt(T.w1[:], T.dumz[:], T.PD[:, 512:520], ALU.subtract, ["dumz", "B5"], ["w1"])
-        tt(T.vv[:], T.tt[:], T.js[:, 15::16], ALU.max, ["tt", "js"], ["vv"])
-        tt(T.w2[:], T.w1[:], T.y3[:, 15::16], ALU.max, ["w1", "y3"], ["w2"])
-        tt(T.ex[:], T.vv[:].indirect(T.cEx[:]), T.mA[:], ALU.mult, ["vv", "cEx", "mA"], ["ex"])
-        cp(T.Yu[:], T.w2[:], ["w2"], ["Yu"])
-        mm(T.P7[:, 0:L], T.BO[:], T.ex[:], True, True, ["cBO", "ex"], ["B7"])
+        act(T.ww[:, 16:24], T.rq[:, 15::16], ID, ["rq"], ["tt"], bias=16.0, scale=-1.0)
+        tt(T.vv[:], T.ww[:, 16:24], T.js[:, 15::16], ALU.max, ["tt", "js"], ["vv"])
+        tt(T.ex[:], (T.vv[:], T.cEx[:]), T.mK[:], ALU.mult, ["vv", "cEx", "mK"], ["ex"])
+        mm(T.P6[:, 0:L], T.BO[:], T.ex[:], ["cBO", "ex"], "B6")
+        act(T.AP2[:, 1::2], T.P6[:, 0:L], RELU, ["B6"], ["ap", "nn"], bias=-7.0, scale=0.5, acc=T.nn[:, 0:1])
+        act(T.Rm[:, 0:L], T.P6[:, 0:L], RELU, ["B6", "pf11"], ["R"], bias=T.pf[:, 11:12], scale=0.5)
+        act(T.Rm[:, L:2 * L], T.Rm[:, 0:L], RELU, ["R"], ["Rm"], bias=1.0, scale=-1.0)
+        tt(T.ys[:], (T.man[:], T.Tmu[:]), T.TD[:, 1::2], ALU.subtract, MAN + ["Tmu", "Tf"], ["ys"])
+        scan(T.DAs[:, s(256)], T.AP2[:], T.TD[:], ALU.mult, ALU.add, ["AP0", "ap", "Tf", "dT"], ["aa" + rs])
+        tt(T.DAs[:, r * 256:(r + 1) * 256:2], T.ys[:], T.Rm[:, L:2 * L], ALU.mult, ["ys", "Rm", "aa" + rs], ["aa" + rs])
+        send("da" + rs, ["aa" + rs])
+        tt(T.ww[:, 0:8], dumz, T.rq[:, 15::16], ALU.subtract, ["dumz", "rq"], ["w1"])
+        tt(T.ww[:, 8:16], T.ww[:, 0:8], T.y3[:, 15::16], ALU.max, ["w1", "y3"], ["w2"])
+        cp(T.Yu[:], T.ww[:, 8:16], ["w2"], ["Yu"])
+        act(T.ymp[:], (Xw, T.Yu[:]), ID, XK + ["Yu"], ["ymp"])
+        nz = L if last else 2 * L
+        for x, xk in ((zj, zjk), (T.ymp[:], "ymp")):
+            mm(T.PT[:, 1024:1152], T.idb[:], x, ["idb", xk], "B2")
+            if not last:
+                mm(T.PT[:, 1152:1280], x, T.idb[:], ["idb", xk], "B2")
+        act(T.hp[:, 0:nz], T.PT[:, 1024:1024 + nz], ID, ["B2"], ["hp"], bias=MAGIC, scale=0.4999)
+        act(T.Zj[:, zn:zn + L], T.hp[:, 0:L], ID, ["hp"], ["zj" + ns], bias=-MAGIC)
         if last:
-            for b in (3, 2):
-                thr_bank(T.thT4, "thT4", b, True)
-        act(T.ymp[:], T.X[:, 0:XZ].indirect(T.Yu[:]), ID, XK + ["Xz", "Yu"], ["ymp"])
-        act(T.AP2[:, 1::2], T.P7[:, 0:L], RELU, ["B7"], ["ap", "nn"], bias=-7.0, scale=0.5, acc=T.nn[:, 0:1])
-        act(T.Zj[:, zn + 144:zn + ZW], T.P7[:, 0:L], RELU, ["B7", "pf9"], ["zjR" + ns], bias=T.pf[:, 9:10], scale=0.5)
-        send("R" + rs, ["zjR" + ns])
-
-        def new_points():
-            scan(T.DAs[:, s(256)], T.AP2[:], T.TD[:], ALU.mult, ALU.add, ["AP0", "ap", "Tf", "dT"], ["aa" + rs])
-            tt(T.DAs[:, r * 256:(r + 1) * 256:2], T.Vp[:].indirect(T.cUn[:]), T.TD[:, 1::2], ALU.subtract,
-               ["Vp", "cUn", "Tf", "aa" + rs], ["aa" + rs])
-            send("da" + rs, ["aa" + rs])
-        if last:
-            shadow_offsets()
-            new_points()
+            send("Z" + rs, ["zj" + ns])
+            tt((Xw, T.SOs[:, s(8)]), mn3, a3, ALU.add, ["sos" + rs, "mn3" + rs, "a3" + rs] + XK, XK)
+            dma("Y", "ysect", T.X[:, 0:W], ["X"], ["ysect"], 3000)
         else:
-            for nm in ("v2", "orp", "sa", "sv", "so"):
-                arrive(nm + rs, [nm + rs])
-            tt(XRw.indirect(T.Orp[:, s(8)]), T.V2[:, r * 256:r * 256 + L], T.V2[:, r * 256 + L:r * 256 + 256], ALU.add,
-               ["orp" + rs, "v2" + rs, "XR0", "XR1", "XRd", "XR"], ["XR"])
-        tt(T.ss[:], T.ymp[:].indirect(T.cUn[:]), zj, ALU.add, ["ymp", "cUn", zjk], ["ss"])
-        if not last:
             act(T.nq[:, 0:1], T.nn[:, 0:1], ID, ["nn"], ["nq"], bias=128.75, scale=0.5)
-        act(T.hp[:], T.ss[:], ID, ["ss"], ["hp"], bias=MAGIC, scale=0.4999)
-        if not last:
-            act(T.nf[:, 0:1], T.nq[:, 0:1], ID, ["nq", "nn"], ["nf"], bias=T.nn[:, 0:1], scale=-2.0)
-        act(T.Zj[:, zn:zn + L], T.hp[:], ID, ["hp"], ["zj" + ns], bias=-MAGIC)
-        if not last:
-            act(T.Zj[:, zn + L:zn + L + 1], T.nf[:, 0:1], ID, ["nf", "zjF" + ns], ["zjF" + ns], bias=264.0)
-        send("Z" + rs, ["zj" + ns, "zjF" + ns])
-        if last:
-            tt(Xw.indirect(T.SOs[:, s(8)]), mn3, a3, ALU.add, ["sos" + rs, "mn3" + rs, "a3" + rs] + XK, ["X"])
-            dma("Y", T.ysect[:], T.X[:, 0:W], ["X"], ["ysect"])
-            act(T.th3[:, v4:W], T.PT[:, v4:W], ID, ["B3"], TH3, bias=200.0)
-        else:
-            tt(XRw.indirect(T.SO[:, s(8)]), T.SV[:, r * 256:r * 256 + L], T.SV[:, r * 256 + L:r * 256 + 256], ALU.add,
-               ["so" + rs, "sv" + rs, "sa" + rs, "XR"], ["XR"])
-            new_points()
+            act(T.nn[:, 1:2], T.nq[:, 0:1], ID, ["nq", "nn"], ["nf"], bias=T.nn[:, 0:1], scale=-2.0)
+            act(T.Zj[:, zn + ZT:zn + ZR], T.hp[:, L:2 * L], ID, ["hp"], ["zjT" + ns], bias=-MAGIC - 150.0)
+            act(T.Zj[:, zn + L:zn + L + 1], T.nn[:, 1:2], ID, ["nf", "zjF" + ns], ["zjF" + ns], bias=264.0)
+            send("Z" + rs, ["zj" + ns, "zjF" + ns, "zjT" + ns])
+            cp((Xw, T.SOs[:, s(8)]), mn3, ["sos" + rs, "mn3" + rs] + XK, XK)
+            quarters(T.Zj[:, zn:zn + L], ["zj" + ns], T.a1j, T.SVs[:, (r + 1) * 256 + L:(r + 2) * 256], "a3" + ns, T.nj, "j")
+            for nm in ("v2", "orp", "sv", "so"):
+                arrive(nm + rs, [nm + rs])
+            cp((XRw, T.Orp[:, s(8)]), T.V2[:, s(L)], ["orp" + rs, "v2" + rs, "XR0", "XR1", "XRd", "XR"], ["XR"])
+            tt((XRw, T.SO[:, s(8)]), T.SV[:, r * 256:r * 256 + L], T.SV[:, r * 256 + L:r * 256 + 256], ALU.add,
+               ["so" + rs, "sv" + rs, "XR"], ["XR"])
         if r == RO - 2:
-            send("Zb" + rs, ["zj" + ns, "zjF" + ns])
+            send("Zb" + rs, ["zj" + ns, "zjF" + ns, "zjT" + ns])
             arrive("Zb" + rs, ["zh0"])
         arrive("V" + rs, ["vl" + rs])
         arrive("da" + rs, ["da" + rs])
-        arrive("R" + rs, ["R" + rs])
         if last:
             arrive("Z" + rs, ["zh1"])
-            dma("Y", T.yamt[:], T.Zh[:, ZW:ZW + L], ["zh1"], ["yamt"])
-            win, wk, R, Rk = Xw, XK, T.Zh[:, ZW + 144:2 * ZW], "R" + rs
+            dma("Y", "yamt", T.Zh[:, ZW:ZW + L], ["zh1"], ["yamt"], 1500)
+            win, wk = Xl, "X"
+            z4, z4k, F4, F4k, zt4, zt4k = T.Zh[:, 0:L], "zh0", T.Zh[:, L:L + 1], "zh0", T.Zh[:, ZT:ZR], "zh0"
+            cap4, cap4b, cap4k = T.capf[:, 2:3], T.capf[:, 0:1], ["capo", "capb"]
         else:
             arrive("Z" + rs, ["zc" + ns])
-            win, wk, R, Rk = XRw, ["XR"], T.Zc[:, zn + 144:zn + ZW], "R" + rs
-            tri(*runs[0])
-            tri(*runs[1])
-
-        def off4(a, b):
-            return win.indirect(T.Vl[:, r * L + a // 16:r * L + b // 16])
-        ch4 = CH4L if last else CH4
-        for a, b in ch4:
-            act(T.xs[:, a:b], off4(a, b), ID, wk + ["vl" + rs], cols("xs", a, b), bias=-200.0)
-        tt(T.bb[:, v4:W], off4(v4, W), T.th3[:, v4:W], ALU.is_gt, wk + ["vl" + rs] + TH3, cols("bb", v4, W))
-        if not last:
-            act(T.thA[:], T.Zc[:, zn:zn + L], ID, ["zc" + ns, "cap2"], ["thA"], bias=T.capf[:, 2:3], scale=-sg2)
-        for a, b in ch4:
-            tt(T.bb[:, a:b], T.xs[:, a:b], T.PT[:, a:b], ALU.is_gt, cols("xs", a, b) + [bank(a), bank(b - 1)], cols("bb", a, b))
-            if b == ch4[-1][1]:
-                b = W
-                if not last:
-                    mm(T.P6[:, 0:L], T.thA[:], T.idb[:], True, True, ["thA", "idb"], ["B6"])
-                    act(T.thT[:], T.P6[:, 0:L], ID, ["B6"], ["thT"])
-                    quarters(T.Zj[:, zn:zn + L], ["zj" + ns], T.a1j, T.SVs[:, (r + 1) * 256 + L:(r + 2) * 256], "a3" + ns, T.nj, "j")
-                    for k in range(TH3EARLY):
-                        th3_piece(k, T.Zj[:, zn:zn + L], "zj" + ns)
-            if b % 1024 == 0:
-                h = b // 1024 - 1
-                if h == 1:
-                    for hh in range(2):
-                        mm(T.P7[:, 64 * hh:64 * hh + 64], T.id16[:], R[:, 64 * hh:64 * hh + 64], False, False, ["id16", Rk], ["B7"])
-                for k in range(16):
-                    mm(T.P7[:, 64 * h:64 * h + 64], wband(T.WB, k), T.bb[:, 1024 * h + k:1024 * h + 1024:16], h == 0 and k == 0,
-                       h == 1 and k == 15, ["WB"] + cols("bb", b - 1024, b), ["B7"])
-        if not last:
-            cp(Xw.indirect(T.SOs[:, s(8)]), mn3, ["sos" + rs, "mn3" + rs] + XK, ["X"])
-        ts(T.TK[:, 1::2], T.P7[:, 0:L], F4, ALU.is_lt, ["B7", F4k, "TK"], ["TK"])
-        scan(T.Tn[:], T.TK[:], T.DA[:, s(256)], ALU.mult, ALU.add, ["TK", "da" + rs], ["Tn"])
-        if last:
-            cp(T.To[:], T.Tn[:, 1::2], ["Tn"], ["To"])
-            dma("Y", T.ytraj[:], T.To[:], ["To"], ["ytraj"])
-        else:
-            cp(T.Tc[:, (r + 1) * L:(r + 2) * L], T.Tn[:, 1::2], ["Tn"], ["tc" + ns])
-            for b in B2ORDER:
-                thr_bank(T.thT, "thT", b, not S2PE)
+            win, wk = XRl, "XR"
+            z4, z4k, F4, F4k, zt4, zt4k = zc, zck, Fc, Fck, zt, ztk
+            cap4, cap4b, cap4k = T.capf[:, 3:4], T.capf[:, 4:5], ["capH", "capJ"]
+        v4 = S4[0][0]
+        spread(zt4, zt4k, S4)
+        for k in range(16):
+            act(T.th[:, k:v4:16], z4[:, 0:v4 // 16], ID, [z4k] + cap4k, ["th%d" % k], bias=cap4, scale=-1.0)
+        act(T.fc[:, 4:5], F4, ID, [F4k], ["fc4"], bias=16.0, scale=-1.0)
+        act(T.off[:, v4 // 16:L], T.ones[:, v4 // 16:L], ID, ["ones", "fc4", "off"], ["off"], scale=T.fc[:, 4:5])
+        for a, b in V4:
+            tt(T.bb[:, a:b], (win, T.Vl[:, r * L + a // 16:r * L + b // 16]), T.th[:, a:b], ALU.is_gt,
+               [wk, "vl" + rs] + TH, cols("bb", a, b))
+        for n, (a, b) in enumerate(S4):
+            o = T.PT[:, 512 * n:512 * n + b - a]
+            act(T.xs[:, a:b], (win, T.Vl[:, r * L + a // 16:r * L + b // 16]), ID, [wk, "vl" + rs] + cap4k, cols("xs", a, b), bias=cap4b)
+            mm(o, T.idb[:], T.xs[:, a:b], ["idb"] + cols("xs", a, b), "B%d" % n)
+            act(T.bb[:, a:b], o, SIGN, ["B%d" % n], cols("bb", a, b), bias=-0.5)
+        for h in range(2):
+            pk, bk, c = (T.P6, T.P7)[h][:, 0:64], "B%d" % (6 + h), slice(128 * h, 128 * h + 128)
+            if h:
+                mm(pk, T.idb[:], T.off[:, 64:L], ["idb", "off"], bk)
+            for k in range(16):
+                mm(pk, wband(T.WB, k), T.bb[:, 1024 * h + k:1024 * h + 1024:16], ["WB"] + cols("bb", 1024 * h, 1024 * h + 1024), bk)
+            ts(T.TK[:, 128 * h + 1:128 * h + 128:2], pk, F4, ALU.is_lt, [bk, F4k, "TK%d" % h], ["TK%d" % h])
+            scan(T.Tn[:, c], T.TK[:, c], T.DA[:, r * 256 + 128 * h:r * 256 + 128 * h + 128], ALU.mult, ALU.add,
+                 ["TK%d" % h, "da" + rs], ["Tn%d" % h])
+            if last:
+                cp(T.To[:, 64 * h:64 * h + 64], T.Tn[:, 128 * h + 1:128 * h + 128:2], ["Tn%d" % h, "To"], ["To%d" % h])
+            else:
+                c0 = (r + 1) * 256 + 64 * h
+                cp(T.Tc[:, c0:c0 + 64], (T.Tn[:, c], T.cP1[:, 0:4]), ["Tn%d" % h, "cP1"], ["tc%d%d" % (r + 1, h)])
+    dma("Y", "ytraj", T.To[:], ["To0", "To1"], ["ytraj"], 1500)
     op("Y", None, ["ysect", "yamt", "ytraj"], ())
+    return ops, eng, total["sent"]
+
+
+def rank_program(g, core, T, topo):
+    if T.rank_of(core) is None:
+        helper_program(g, core, T, topo)
+        return
+    ops, eng, sent = record(g, core, T, topo)
+    order = lay_out(ops)
 
     def token(i):
         o = ops[i]
         return o["ext"] if o["ext"] else ("q" + o["q"], o["n"])
 
     known = {q: {} for q in eng}
-    rankof, plan = {q: 0 for q in eng}, []
-    for i, o in enumerate(ops):
+    rankof, plan, place, ends = {q: 0 for q in eng}, [], {}, {}
+    for n, i in enumerate(order):
+        o = ops[i]
+        place[i] = n
         if o["q"] == "X":
             o["know"] = {}
             continue
+        if o["group"] is not None:
+            ends[o["group"]] = (ends.get(o["group"], (i, i))[0], i)
         if not o["ext"]:
             rankof[o["q"]] += 1
             o["n"] = rankof[o["q"]]
         kn, need = known[o["q"]], []
-        for d in sorted(o["deps"], reverse=True):
+        for d in sorted(o["deps"], key=lambda x: -place[x]):
             sem, n = token(d)
             if sem == "-" or kn.get(sem, 0) >= n:
                 continue
@@ -714,7 +722,7 @@ def rank_program(g, core, T, topo):
                 eng[o["q"]].wait_ge(T.sem["q" + ops[d]["q"]], val[d])
         if o["fn"] is None:
             continue
-        ins = o["fn"]()
+        ins = o["fn"]() if o["group"] is None else o["fn"](ends[o["group"]][0] == i, ends[o["group"]][1] == i)
         if o["ext"]:
             if o["ext"][0] != "-":
                 ins.then_inc(T.sem[o["ext"][0]], o["ext"][1])
@@ -722,4 +730,4 @@ def rank_program(g, core, T, topo):
             count[o["q"]] += 1
             val[i] = count[o["q"]]
             ins.then_inc(T.sem["q" + o["q"]], 1)
-    g.wait_ge(T.sem.sent, total["sent"])
+    g.wait_ge(T.sem.sent, sent)

@@ -1,3 +1,4 @@
+from concourse.bass import DstId, RemoteDMATransfer
 from concourse.mybir import AluOpType as ALU, ActivationFunctionType as ACT
 
 N, W, L, Q, RO, SB, SC = 6, 2048, 128, 512, 3, 1, 4
@@ -7,19 +8,31 @@ SP = W + L
 XW = SP + 2 * L
 ZW = 272
 ZT, ZR = 144, 272
-LATE_ENGINES = ("bk", "iZ", "iC", "v2", "or", "sv", "Zb")
+LATE_ENGINES = ("bk", "iZ", "iC", "v2", "or", "sv", "Zb", "fN", "dd", "zF")
 UNIT = 2560.0
-S0 = 1280
+S0 = 512
 S3 = [(1280, 1792), (1792, 2048)]
 V3 = [(0, 512), (512, 1024), (1024, 1280)]
-S4 = [(1280, 1792), (1792, 2048)]
-V4 = [(0, 512), (512, 1024), (1024, 1280)]
-FIRST2 = "V0:512 S512:1024 S1024:1536 S1536:1792 S1792:2048"
-NEXT2 = "S0:512 V512:1024 S1024:1536 S1536:2048"
-EQS = 2
+ORD3 = "Vgv0 Sgs0 Vgv1 Sgs1 Sev0 Vmv0 Ses0 Vgv2 Vmv1 Ses1 Vms0 Sev1 Vmv2 Vev2 Vms1"
+FIRST, SLACK = 800, 1000
+ROOM = {"fN": 4, "zF": 2, "dd": 3, "fT": 1.5, "v": 1.2, "orp": 0.8, "sv": 0.5, "Zb": 3, "iC": 3, "fZ": 1, "nf": 1.5, "oj": 0.8,
+        "da": 0.4, "Z": 0.7, "bk": 3}
+STEP4 = [([(768, 1024), (1664, 2048)], [(0, 768), (1024, 1664)]),
+         ([(1280, 1792), (1792, 2048)], [(0, 512), (512, 1024), (1024, 1280)])]
+FIRST2 = "S0:512 V512:768 S768:1024 S1024:1536 D1536:2048"
+NEXT2 = "S0:512 S512:1024 S1024:1408 D1408:1664 D1664:2048"
+EQS = 1
 MAGIC = 12582912.0
-CYC, PEC, LINK, HOP, ISSUE, FIXV, FIXS, GATHER, SCATTER = 0.83, 0.42, 170, 1600, 300, 30, 40, 1.56, 3.8
-LOAD = 1300
+CYC, PEC, LINK, HOP, ISSUE, FIXV, FIXS, GATHER, SCATTER = 0.83, 0.45, 180, 1350, 250, 25, 35, 1.56, 3.8
+FIXP, TRI_AT = 5, 0
+G3, G4 = (0, 6, 6), (6, 6, 6)
+LOAD, GIVE = 1300, 150
+CHAINS = {}
+CHAINS0 = {"S": ["2xs0 2xs16 2xs12 2a1c"], "G": ["1pi0 1pi8 1x8a 1xr 1iZ 1iT 1lc 1x8b 1x8c 1xq"],
+           "V": ["1pi6 1pi7 1pq 1cP0", "2xs8 2zt0 2hp 2Tn00 2Tm0 2Tm1"]}
+LATE_Z, NXW, ONV = 700, 1, "j"
+LANE = {"fN": 2, "dd": 3, "zF": 1, "Zb": 3}
+RUNS = [(0, 2, 4), (2, 4, 5), (4, 6, 1), (6, 8, 2)]
 
 
 def sb(n, d):
@@ -28,53 +41,58 @@ def sb(n, d):
 
 SCRATCH = {
     "X": sb(XW, BF), "XR": sb(XW, BF), "man": sb(W, F32), "mv32": sb(Q, I32), "tr32": sb(L, I32), "Th": sb(L, U16),
-    "cap32": sb(1, I32), "mn2": sb(L, BF), "a2": sb(L, BF), "Rm": sb(256, BF), "cIn": sb(8, U16),
+    "cap32": sb(1, I32), "Rm": sb(L, BF), "cIn": sb(8, U16),
     "Zs": sb(L, BF), "Cs": sb(8, BF), "Ch": sb(8, BF),
-    "Tc": sb(RO * 256, U16), "Zc": sb(RO * ZW, BF), "Tj": sb(RO * 256, U16), "Zj": sb(4 * ZW, BF), "Zh": sb(2 * ZW, BF),
+    "Tc": sb(RO * L, U16), "Zc": sb(RO * ZW, BF), "Tj": sb(RO * L, U16), "Zj": sb(4 * ZW, BF), "Zh": sb(2 * ZW, BF),
     "DDs": sb(RO * L, F32), "DD": sb(RO * L, F32), "NFs": sb(RO * L, BF), "NF": sb(RO * L, BF), "NFm": sb(L, BF),
     "Ous": sb(RO * 8, U16), "Oj": sb(RO * 8, U16), "Orp": sb(RO * 8, U16), "Ofs": sb(16, F32),
     "V2s": sb(RO * L, BF), "V2": sb(RO * L, BF), "SVs": sb(RO * 256, BF), "SV": sb(RO * 256, BF),
     "SOs": sb(RO * 8, U16), "SO": sb(RO * 8, U16), "Vs": sb(RO * L, U16), "Vl": sb(RO * L, U16),
     "DAs": sb(RO * 256, H), "DA": sb(RO * 256, H),
-    "xs": sb(W, BF), "bb": sb(W, BF), "bo": sb(W, BF), "th": sb(W, BF), "ECp": sb(W, BF), "ECn": sb(W - S0, BF),
+    "xs": sb(W, BF), "bb": sb(W, BF), "bo": sb(W, BF), "th": sb(3 * W, BF), "ECp": sb(W, BF), "ECn": sb(W - S0, BF),
     "eq": sb(1024, BF), "ab": sb(512, BF), "SEL": sb(1024, H), "NSEL": sb(1024, H), "Tm": sb(1024, F32),
-    "pi": sb(8, I32), "pf": sb(24, F32), "xr": sb(144, F32), "xq": sb(L, F32), "xm": sb(L, F32), "xk": sb(L, F32),
+    "pi": sb(16, I32), "pf": sb(24, F32), "xr": sb(144, F32), "xq": sb(L, F32), "xm": sb(L, F32), "xk": sb(L, F32),
     "lc": sb(L, F32), "lx": sb(L, F32), "x8": sb(24, F32),
     "idb": sb(L, BF), "idc": sb(L, BF), "idf": sb(L, F32), "id4": sb(L, F32), "id5": sb(L, F32), "idq": sb(L, BF), "idp": sb(L, BF),
-    "idu": sb(L, BF),
-    "WB": sb(144, BF), "WS": sb(144, BF), "WU": sb(144, BF), "BO": sb(L, BF), "TRI": sb(L, BF), "mA": sb(L, BF), "mK": sb(L, BF),
-    "ones": sb(L, BF), "Dm": sb(32, F32), "C15": sb(512, BF), "rst": sb(L, BF), "rs2": sb(256, BF),
-    "cMx": sb(L, F32), "c4k": sb(8, BF), "spT": sb(L, F32),
-    "cTm": sb(8, U16), "cPA": sb(8, U16), "cEx": sb(8, U16), "cP0": sb(8, U16), "cP1": sb(8, U16),
+    "idu": sb(L, BF), "id6": sb(L, BF),
+    "WB": sb(144, BF), "WS": sb(144, BF), "BO": sb(L, BF), "TRI": sb(L, BF), "mA": sb(L, BF), "mK": sb(2 * L, BF),
+    "ones": sb(L, BF), "Dm": sb(32, F32), "C15": sb(512, BF), "rst": sb(L, BF), "k0": sb(L, BF),
+    "cMx": sb(L, F32), "c4k": sb(8, BF), "spT": sb(256, F32),
+    "cTm": sb(8, U16), "cPA": sb(8, U16), "cEx": sb(8, U16), "cP0": sb(8, U16), "cP1": sb(8, U16), "cP3": sb(16, U16),
+    "Tk": sb(RO * L, U16), "ful": sb(L, BF),
     "dum": sb(16, F32), "capf": sb(8, F32), "F6": sb(8, BF), "fc": sb(16, F32),
-    "t3": sb(L, BF), "t3T": sb(L, BF), "off": sb(L, BF),
-    "a1": sb(L, BF), "nc": sb(L, BF), "a1j": sb(L, BF), "nj": sb(L, BF), "s15": sb(L, BF),
+    "t3": sb(2 * L, BF), "t3T": sb(L, BF), "off": sb(L, BF), "onS": sb(2 * L, BF),
+    "upc": sb(3 * L, BF), "upj": sb(3 * L, BF), "s15": sb(L, BF),
     "FB": sb(144, BF), "ys": sb(L, F32), "PA": sb(L, H), "Pu": sb(8, U16),
-    "E": sb(256, H), "Es": sb(256, H), "rq": sb(L, F32), "KB": sb(144, F32), "ng3": sb(L, BF), "y3": sb(L, F32), "Tmu": sb(8, U16),
+    "Es": sb(256, F32), "rq": sb(L, F32), "KB": sb(L, F32), "ng3": sb(L, BF), "y3": sb(L, F32), "Tmu": sb(8, U16),
     "js": sb(L, F32), "ww": sb(24, F32), "Yu": sb(8, U16),
-    "vv": sb(8, F32), "ex": sb(L, BF), "AP2": sb(256, BF), "nn": sb(8, F32), "nq": sb(8, BF),
+    "ex": sb(2 * L, BF), "AP2": sb(256, BF), "nn": sb(8, F32), "nq": sb(8, BF),
     "ymp": sb(L, BF), "hp": sb(256, F32),
-    "TD": sb(256, F32), "qq": sb(L, BF), "TK": sb(256, BF), "Tn": sb(256, F32), "To": sb(L, F32),
+    "TD": sb(RO * 256, F32), "qq": sb(L, BF), "TK": sb(256, BF), "Tn": sb(4 * 256, F32), "To": sb(L, F32),
     "PT": ("psum", [128, 2048], F32), "PD": ("psum", [128, 1024], F32), "P6": ("psum", [128, 512], F32), "P7": ("psum", [128, 512], F32),
 }
-PER_ROUND = ["fT", "dd", "nf", "v2", "oj", "orp", "sv", "so", "V", "da", "Z", "Zb"]
-SEMAPHORES = (["qV", "qS", "qP", "qG", "sent", "bulk", "iT", "iZ", "iC", "fZ", "bk0", "bk1"]
+PER_ROUND = ["fT", "fN", "dd", "nf", "v2", "oj", "orp", "sv", "so", "V", "da", "Z", "zF", "Zb"]
+PAIRS = [("oj", "orp")]
+SEMAPHORES = (["qV", "qS", "qP", "qG", "sent", "bulk", "iT", "iZ", "iC", "fZ", "bk0", "bk1", "bk2", "bk3"]
               + ["%s%d" % (m, r) for m in PER_ROUND for r in range(RO)]
               + ["d%d" % i for i in range(12)])
-PASSES, ORDER_END = 1, []
+PASSES, PARTS, PADS, SLOW, ORDER_END = 3, (0.33, 0.5, 0.7), (0.0, 20.0, 40.0, 60.0), 700.0, []
 ORDER, SENDS = [], []
 
 
 def messages(T):
     m = {"iT": (SB, T.Th[:], T.Tc[:, 0:L], 0), "iZ": (SB, T.Zs[:], T.Zc[:, 0:L], 1), "iC": (SB, T.Cs[:], T.Ch[:], 1),
          "fZ": (SC - SB, T.Zc[:, 0:L], T.Zj[:, 0:L], 1),
-         "bk0": (1, T.X[:, 0:W // 2], T.XR[:, 0:W // 2], 2), "bk1": (1, T.X[:, W // 2:W], T.XR[:, W // 2:W], 3)}
+         }
+    for n in range(4):
+        m["bk%d" % n] = (1, T.X[:, n * Q:(n + 1) * Q], T.XR[:, n * Q:(n + 1) * Q], 2 + n)
     for r in range(RO):
         last = r == RO - 1
         ex = (-SC if last else SB - SC) % N
         s = lambda n: slice(r * n, (r + 1) * n)
-        m["fT%d" % r] = (SC - SB, T.Tc[:, s(256)], T.Tj[:, s(256)], 1)
-        m["dd%d" % r] = (SC - SB, T.DDs[:, s(L)], T.DD[:, s(L)], 1)
+        m["fT%d" % r] = (SC - SB, T.Tk[:, s(L)], T.Tj[:, s(L)], 1)
+        m["fN%d" % r] = (SC - SB, T.Tn[:, s(256)], T.TD[:, s(256)], LANE["fN"])
+        m["dd%d" % r] = (SC - SB, T.DDs[:, s(L)], T.DD[:, s(L)], LANE["dd"])
         m["nf%d" % r] = (SC - SB, T.NFs[:, s(L)], T.NF[:, s(L)], 1)
         m["oj%d" % r] = (SC - SB, T.Ous[:, s(8)], T.Oj[:, s(8)], 1)
         m["V%d" % r] = (ex, T.Vs[:, s(L)], T.Vl[:, s(L)], 0)
@@ -83,13 +101,14 @@ def messages(T):
         if last:
             m["Z%d" % r] = (ex, T.Zj[:, zn:zn + L], T.Zh[:, ZW:ZW + L], 0)
         else:
-            m["Z%d" % r] = (ex, T.Zj[:, zn:zn + ZW], T.Zc[:, zn:zn + ZW], 0)
+            m["Z%d" % r] = (ex, T.Zj[:, zn + ZT:zn + ZW], T.Zc[:, zn + ZT:zn + ZW], 0)
+            m["zF%d" % r] = (ex, T.Zj[:, zn:zn + ZT], T.Zc[:, zn:zn + ZT], LANE["zF"])
             m["v2%d" % r] = (1, T.V2s[:, s(L)], T.V2[:, s(L)], 1)
             m["orp%d" % r] = (1, T.Ous[:, s(8)], T.Orp[:, s(8)], 1)
             m["sv%d" % r] = (1, T.SVs[:, s(256)], T.SV[:, s(256)], 1)
             m["so%d" % r] = (1, T.SOs[:, s(8)], T.SO[:, s(8)], 0)
         if r == RO - 2:
-            m["Zb%d" % r] = (-SC % N, T.Zj[:, zn:zn + ZW], T.Zh[:, 0:ZW], 1)
+            m["Zb%d" % r] = (-SC % N, T.Zj[:, zn:zn + ZW], T.Zh[:, 0:ZW], LANE["Zb"])
     return m
 
 
@@ -100,16 +119,29 @@ def first_hop(T, topo, rank, step, lane):
     able = [c for c in topo.cores_of(src) if c != src and all(topo.may_write(c, d) for d in T.cores)]
     near = [c for c in able if topo.die(c) == topo.die(src)]
     far = [c for c in able if topo.die(c) != topo.die(src)]
-    return (near + far)[lane]
+    return (near + far + near)[lane]
 
 
 def small_mask(topo, src, dst, name):
     e = topo.engines(src, dst)
-    if name[:2] in LATE_ENGINES:
+    if name[:2] in LATE_ENGINES and name not in ("bk2", "bk3"):
         e = e[-8:]
-    elif name[0] == "i":
+    elif name[0] in "ib":
         e = e[:8]
     return sum(1 << x for x in e), len(e)
+
+
+def first_mask(T, topo, msgs, rank, name):
+    src, to = T.cores[rank], first_hop(T, topo, rank, msgs[name][0], msgs[name][3])
+    for a, b in PAIRS:
+        if name[:-1] in (a, b) and a + name[-1] in msgs and b + name[-1] in msgs:
+            ea, eb = (topo.engines(src, first_hop(T, topo, rank, msgs[x][0], msgs[x][3])) for x in (a + name[-1], b + name[-1]))
+            eb = [x for x in eb if x not in ea]
+            if not eb:
+                ea, eb = ea[:len(ea) // 2], ea[len(ea) // 2:]
+            e = ea if name[:-1] == a else eb
+            return sum(1 << x for x in e), len(e)
+    return small_mask(topo, src, to, name)
 
 
 def helper_program(g, core, T, topo):
@@ -125,7 +157,7 @@ def helper_program(g, core, T, topo):
             if first_hop(T, topo, rank, step, lane) != core:
                 continue
             dst = T.cores[(rank + step) % N]
-            g.wait_ge(T.sem[name], small_mask(topo, T.cores[rank], core, name)[1])
+            g.wait_ge(T.sem[name], first_mask(T, topo, msgs, rank, name)[1])
             mask, n = small_mask(topo, core, dst, name)
             rid, pid = topo.addr(dst, core)
             g.remote_dma(land, land, T.sem[name], T.sem.sent, pid, rid, mask)
@@ -145,18 +177,23 @@ def lay_out(ops):
             before[i][d] = max(before[i].get(d, 0), ops[d]["lat"])
         for d, lat in before[i].items():
             after[d].append((i, lat))
-    tail = [0.0] * n
-    for i in range(n - 1, -1, -1):
-        tail[i] = ops[i]["cost"] + max([lat + tail[j] for j, lat in after[i]] + [0.0])
+    left = [len(b) for b in before]
+    flow = [i for i in range(n) if not left[i]]
+    for i in flow:
+        for j, _ in after[i]:
+            left[j] -= 1
+            if not left[j]:
+                flow.append(j)
+    assert len(flow) == n
+    pos = {i: k for k, i in enumerate(flow)}
 
-
-    def place(turn, nxt):
+    def place(turn, nxt, part, cost):
         at, busy, end = [0.0] * n, {}, [0.0] * n
         for i in turn:
-            t, c, line = at[i], ops[i]["cost"], busy.setdefault(ops[i]["q"], [])
+            t, c, line = at[i], cost[i], busy.setdefault(ops[i]["q"], [])
             k = 0
             if ops[i]["q"] != "X":
-                while k < len(line) and line[k][0] < t + c:
+                while k < len(line) and (line[k][0] <= t or line[k][0] < t + c - min(GIVE, c * part)):
                     t = max(t, line[k][1])
                     k += 1
                 line.insert(k, (t, t + c))
@@ -164,23 +201,49 @@ def lay_out(ops):
             for j, lat in nxt[i]:
                 at[j] = max(at[j], t + c + lat)
         return end
-    back = [list(b.items()) for b in before]
-    end = place(sorted(range(n), key=lambda i: (-tail[i], i)), after)
-    for _ in range(PASSES):
-        late = place(sorted(range(n), key=lambda i: (-end[i], -i)), back)
-        again = place(sorted(range(n), key=lambda i: (-late[i], i)), after)
-        if max(again) <= max(end):
-            end = again
-    ORDER.extend(sorted(range(n), key=lambda i: (end[i] - ops[i]["cost"], end[i], i)))
-    ORDER_END.append(max(end))
-    SENDS.extend(ops[i]["send"] for i in ORDER if ops[i]["send"])
+
+    def length(order, slow):
+        end, free = [0.0] * n, {}
+        for i in order:
+            o = ops[i]
+            t = max([end[d] + lat for d, lat in back[i]] + [0.0])
+            if o["q"] == "X":
+                end[i] = t - o["room"] + slow
+            else:
+                end[i] = free[o["q"]] = max(t, free.get(o["q"], 0.0)) + o["cost"] + (slow / 25 if o["q"] in "VS" else 0.0)
+        return max(end)
+    back, tried = [list(b.items()) for b in before], []
+    for pad, part in [(x, y) for x in PADS for y in PARTS]:
+        cost = [o["cost"] + (pad if o["q"] in "VS" else 0.0) for o in ops]
+        tail = [0.0] * n
+        for i in flow[::-1]:
+            tail[i] = cost[i] + max([lat + tail[j] for j, lat in after[i]] + [0.0])
+        end = place(sorted(range(n), key=lambda i: (-round(tail[i], 2), pos[i])), after, part, cost)
+        for _ in range(PASSES):
+            late = place(sorted(range(n), key=lambda i: (-round(end[i], 2), -pos[i])), back, part, cost)
+            end = place(sorted(range(n), key=lambda i: (-round(late[i], 2), pos[i])), after, part, cost)
+            order = sorted(range(n), key=lambda i: (round(end[i] - cost[i], 2), round(end[i], 2), pos[i]))
+            tried.append((length(order, 0.0) + length(order, SLOW), len(tried), order))
+    ORDER.extend(min(tried)[2])
+    ORDER_END.append(min(tried)[0] / 2)
+    SENDS.extend(x for i in ORDER for x in ops[i]["send"] or [])
     return ORDER
 
 
 def record(g, core, T, topo):
     rank = T.rank_of(core)
     msgs = messages(T)
-    ops, lastw, readers, opened, sent_at = [], {}, {}, {}, {}
+    ops, lastw, readers, opened, sent_at, tags, stage = [], {}, {}, {}, {}, {}, ["0"]
+
+    def chain(r, q, words):
+        found = []
+        for x in words.split():
+            rr, st = (r + 1, int(x[0]) - 3) if x[0] in "56" else (r, int(x[0]))
+            x = tags.get("%d%d%s%s" % (rr, st, q, x[1:].replace("#", str(rr)).replace("$", str(rr + 1))))
+            if x is not None:
+                found.append(x)
+        for a, b in zip(found, found[1:]):
+            ops[b]["soft"][a] = 0
     eng = {"V": g.vector, "S": g.scalar, "P": g.tensor, "G": g, "Y": g.sync} if g else {}
 
     def op(q, fn, r=(), w=(), ext=None, cost=0.0, lat=LINK, send=None, soft=()):
@@ -207,7 +270,10 @@ def record(g, core, T, topo):
                 else:
                     soft[x] = 0
             lastw[k].append(i)
-        ops.append({"q": q, "fn": fn, "deps": deps, "soft": soft, "ext": ext, "cost": cost, "lat": lat, "send": send, "group": group})
+        if w:
+            tags[stage[0] + q + w[0]] = i
+        ops.append({"q": q, "fn": fn, "deps": deps, "soft": soft, "ext": ext, "cost": cost, "lat": lat, "send": send, "group": group,
+                    "room": 0.0})
         for k in r:
             if k not in w:
                 readers.setdefault(k, []).append(i)
@@ -216,21 +282,32 @@ def record(g, core, T, topo):
         step, _, land, lane = msgs[name]
         src = (rank - step) % N
         via = first_hop(T, topo, src, step, lane)
-        n = small_mask(topo, T.cores[src] if via == core else via, core, name)[1]
+        n = (first_mask(T, topo, msgs, src, name) if via == core else small_mask(topo, via, core, name))[1]
         hops = max(1 if first_hop(T, topo, x, step, lane) in T.cores else 2 for x in range(N))
-        op("X", None, (), keys, (name, n), lat=0, soft={sent_at[name]: hops * (HOP + land.shape[1])})
+        room = SLACK * ROOM.get(name.rstrip("0123"), 0.0)
+        time = hops * (HOP + land.shape[1] + (FIRST if name[0] == "i" else 0)) + LATE_Z * (name == "iZ")
+        op("X", None, (), keys, (name, n), lat=0, soft={sent_at[name]: time + room})
+        ops[-1]["room"] = room
 
     total = {"sent": 0, "bulk": 0}
 
-    def send(name, keys):
-        step, src, land, lane = msgs[name]
-        to = first_hop(T, topo, rank, step, lane)
-        mask, n = small_mask(topo, core, to, name)
-        rid, pid = topo.addr(to, core)
-        loc = "bulk" if lane >= 2 else "sent"
-        total[loc] += n
-        sent_at[name] = len(ops)
-        op("G", lambda: g.remote_dma(land, src, T.sem[name], T.sem[loc], pid, rid, mask), keys, (), ("-", 0), ISSUE, send=name)
+    def send(names, keys):
+        parts, loc = [], "bulk" if names[:2] == "bk" else "sent"
+        for name in names.split():
+            step, src, land, lane = msgs[name]
+            mask, n = first_mask(T, topo, msgs, rank, name)
+            parts.append((land, src, name, topo.addr(first_hop(T, topo, rank, step, lane), core), mask))
+            total[loc] += n
+            sent_at[name] = tags[stage[0] + "G" + name] = len(ops)
+
+        def issue():
+            if len(parts) == 1:
+                land, src, name, (rid, pid), mask = parts[0]
+                return g.remote_dma(land, src, T.sem[name], T.sem[loc], pid, rid, mask)
+            return g.remote_dma_fused([RemoteDMATransfer(dst_ids=[DstId(rid=rid, pnc=pid)], dma_engine_mask=mask, remote_sem=T.sem[name],
+                                                         src=src, dst=land) for land, src, name, (rid, pid), mask in parts],
+                                      local_sem=T.sem[loc])
+        op("G", issue, keys, (), ("-", 0), ISSUE, send=names.split())
 
     ndma = [0]
 
@@ -278,9 +355,16 @@ def record(g, core, T, topo):
     def act(out, in_, f, r, w, bias=0.0, scale=1.0, acc=None):
         op("S", lambda: g.scalar.activation(out, view(in_), f, bias=bias, scale=scale, accum_out=acc), r, w, cost=price(FIXS, out, in_, 1.0))
 
-    def mm(out, lhsT, rhs, r, w):
+    leads = {}
+
+    def mm(out, lhsT, rhs, r, w, lead=False):
         op("P", lambda first, final: g.tensor.matmul(out, lhsT, rhs, first, final), r, [w],
-           cost=max(64, rhs.shape[1]) * PEC * (1 if narrow(rhs) else 4))
+           cost=FIXP + max(64, rhs.shape[1]) * PEC * (1 if narrow(rhs) else 4))
+        mine = leads.setdefault(ops[-1]["group"], [])
+        if lead:
+            mine.append(len(ops) - 1)
+        else:
+            ops[-1]["soft"].update({x: 0 for x in mine})
 
     def iota(out, pat, w, base=0, step=0):
         op("G", lambda: g.iota(out, pat, base, step, allow_small_or_imprecise_dtypes=True), (), w, cost=130 + 2 * CYC * out.shape[1])
@@ -296,11 +380,13 @@ def record(g, core, T, topo):
     dma("Y", T.Zs[:], "amt", (), ["zs"], LOAD)
     dma("Y", T.cap32[:], "cap", (), ["cap32"], LOAD)
     dma("S", T.X[:, 0:W], "sect", (), ["X"], 2 * LOAD)
+    stage[0] = "01"
     op("G", lambda: g.iota(T.pi[:, 0:1], [[0, 1]], 0, 1), (), ["pi0"], cost=130)
+    op("G", lambda: g.iota(T.pi[:, 8:9], [[0, 1]], 0, 16), (), ["pi8"], cost=130)
     iota(T.lc[:], [[64, 2], [1, 16], [16, 4]], ["lc"])
     iota(T.xr[:], [[1, 144]], ["xr"])
     iota(T.x8[:, 0:8], [[64, 2], [4, 4]], ["x8a"])
-    iota(T.x8[:, 8:16], [[1, 8]], ["x8b"], 0, 8)
+    iota(T.x8[:, 8:16], [[1, 8]], ["x8b"], 0, 4)
     iota(T.x8[:, 16:24], [[64, 2], [1, 4]], ["x8c"])
     iota(T.xq[:], [[16, 8], [0, 16]], ["xq"])
     iota(T.xm[:], [[1, 16], [0, 8]], ["xm"])
@@ -308,42 +394,43 @@ def record(g, core, T, topo):
     iota(T.xk[:], [[0, 8], [1, 16]], ["xk"])
     ms(T.ones[:], 1.0, ["ones"])
     ms(T.X[:, W:XW], 0.0, ["Xz", "Xd"])
-    ms(T.XR[:, W:XW], 0.0, ["XRd"])
+    iota(T.XR[:, W:XW], [[0, XW - W]], ["XRd"])
     ms(T.C15[:], 1.0, ["C15"])
     ms(T.C15[:, 15::16], 0.0, ["C15"], ["C15"])
-    ms(T.rs2[:], 1.0, ["rs2"])
-    ms(T.rs2[:, 0::32], 0.0, ["rs2"], ["rs2"])
     ms(T.FB[:, 0:8], 0.0, ["FB"])
     ms(T.F6[:], 6.0, ["F6"])
     ms(T.c4k[:], 4096.0, ["c4k"])
     ms(T.fc[:, 8:9], -0.5, ["fb0"])
     ms(T.fc[:, 9:10], -8.5, ["fb1"])
-    ms(T.KB[:, 0:8], 0.0, ["KB"])
-    ms(T.E[:], 0.0, ["E0", "E1"])
-    ms(T.TK[:], 0.0, ["TK0", "TK1"])
-    ms(T.AP2[:], 0.0, ["AP0", "ap"])
-    ms(T.off[:], 0.0, ["off"])
+    iota(T.TK[:], [[0, 256]], ["TK0", "TK1"])
+    iota(T.AP2[:], [[0, 256]], ["AP0", "ap"])
+    ms(T.onS[:], 0.0, ["onS"])
+    for n in range(2):
+        for a, b in STEP4[n][0]:
+            ms(T.onS[:, L * n + a // 16:L * n + b // 16], 1.0, ["onS"], ["onS"])
     for n in range(1, RO):
-        ms(T.Zj[:, n * ZW + L:n * ZW + ZT], 0.0, ["zjF%d" % n])
+        iota(T.Zj[:, n * ZW + L:n * ZW + ZT], [[0, 16]], ["zjF%d" % n])
     ts(T.pi[:, 1:2], T.pi[:, 0:1], 15, ALU.bitwise_and, ["pi0"], ["pi1"])
     ts(T.pi[:, 2:3], T.pi[:, 0:1], 112, ALU.bitwise_and, ["pi0"], ["pi2"])
     ts(T.pi[:, 3:4], T.pi[:, 0:1], 7, ALU.bitwise_and, ["pi0"], ["pi3"])
     ts(T.pi[:, 4:5], T.pi[:, 0:1], 3, ALU.logical_shift_right, ["pi0"], ["pi4"])
-    ts(T.pi[:, 5:6], T.pi[:, 0:1], 2, ALU.logical_shift_right, ["pi0"], ["pi5"], 3, ALU.bitwise_and)
-    ts(T.pi[:, 6:7], T.pi[:, 0:1], 3, ALU.bitwise_and, ["pi0"], ["pi6"])
-    cp(T.pf[:, 0:7], T.pi[:, 0:7], ["pi%d" % i for i in range(7)], ["pf"])
-    pc, kc, gc_, a8, p8, p4, p3 = (T.pf[:, i:i + 1] for i in range(7))
+    ts(T.pi[:, 5:6], T.pi[:, 0:1], 3, ALU.logical_shift_right, ["pi0"], ["pi5"], 1, ALU.bitwise_and)
+    ts(T.pi[:, 6:7], T.pi[:, 0:1], 2, ALU.logical_shift_right, ["pi0"], ["pi6"], 3, ALU.bitwise_and)
+    ts(T.pi[:, 7:8], T.pi[:, 8:9], 48, ALU.bitwise_and, ["pi8"], ["pi7"])
+    cp(T.pf[:, 0:6], T.pi[:, 0:6], ["pi%d" % i for i in range(6)], ["pf"])
+    cp(T.pf[:, 6:8], T.pi[:, 6:8], ["pi6", "pi7"], ["pq"])
+    pc, kc, gc_, a8, p8, p1, p4, p3 = (T.pf[:, i:i + 1] for i in range(8))
     ts(T.idc[:], T.lc[:], pc, ALU.is_equal, ["lc", "pf"], ["idc"])
     ts(T.idb[:], T.xr[:, 0:L], pc, ALU.is_equal, ["xr", "pf"], ["idb"])
-    ts(T.pf[:, 8:9], p3, 16.0, ALU.mult, ["pf"], ["pf8"], p4, ALU.add)
+    tt(T.pf[:, 8:9], p3, p4, ALU.add, ["pq"], ["pf8"])
     ts(T.pf[:, 9:10], a8, 16.0, ALU.mult, ["pf"], ["pf9"], 15.0, ALU.add)
     ts(T.pf[:, 10:11], a8, 16.0, ALU.mult, ["pf"], ["pf10"], p8, ALU.add)
-    ts(T.pf[:, 11:12], kc, -1.0, ALU.mult, ["pf"], ["pf11"], 8.0, ALU.add)
+    ts(T.pf[:, 11:12], kc, -1.0, ALU.mult, ["pf"], ["pf11"], 24.0, ALU.add)
     ts(T.pf[:, 12:13], kc, 2.0, ALU.mult, ["pf"], ["pf12"], float(SP), ALU.add)
     ts(T.pf[:, 13:14], kc, float(W), ALU.add, ["pf"], ["pf13"])
     ts(T.pf[:, 14:15], T.pf[:, 8:9], 2.0, ALU.mult, ["pf8"], ["pf14"], 1.0, ALU.add)
     ts(T.pf[:, 15:16], kc, 4.0, ALU.mult, ["pf"], ["pf15"])
-    ts(T.cP0[:], T.x8[:, 0:8], T.pf[:, 8:9], ALU.add, ["x8a", "pf8"], ["cP0"])
+    ts(T.cP0[:], T.x8[:, 0:8], p3, ALU.add, ["x8a", "pq"], ["cP0"], p4, ALU.add)
     ts(T.cIn[:], T.x8[:, 16:24], T.pf[:, 15:16], ALU.add, ["x8c", "pf15"], ["cIn"])
     cp(T.Th[:], (T.tr32[:], T.cP0[:]), ["tr32", "cP0"], ["Th"])
     send("iT", ["Th"])
@@ -351,16 +438,16 @@ def record(g, core, T, topo):
     ms(T.Cs[:], 0.0, ["cs"])
     ts(T.Cs[:, 0:1], T.cap32[:], -200.0, ALU.add, ["cap32", "cs"], ["cs"])
     send("iC", ["cs"])
-    send("bk0", ["X"])
-    send("bk1", ["X"])
-    op("X", None, (), ["Xsent"], ("bulk", total["bulk"]), lat=0, soft={sent_at["bk0"]: 3000, sent_at["bk1"]: 3000})
+    for n in range(4):
+        send("bk%d" % n, ["X"])
+    op("X", None, (), ["Xsent"], ("bulk", total["bulk"]), lat=0, soft={sent_at["bk%d" % n]: 3000 for n in range(4)})
     arrive("iT", ["tc00", "tc01"])
     arrive("iZ", ["zc0"])
     arrive("iC", ["caph"])
     send("fZ", ["zc0"])
     arrive("fZ", ["zj0"])
-    arrive("bk0", ["XR0"])
-    arrive("bk1", ["XR1"])
+    for n in range(4):
+        arrive("bk%d" % n, ["XR%d" % n])
     dma("Y", T.mv32[:], "mv", ["zc0"], ["mv32"], 2 * LOAD)
     cp(T.man[:, 0:Q], T.mv32[:], ["mv32"], ["man0"])
     for i in range(1, W // Q):
@@ -384,7 +471,7 @@ def record(g, core, T, topo):
     ts(T.cP1[:], x8, 8.0, ALU.mult, ["xr", "pf14"], ["cP1"], T.pf[:, 14:15], ALU.add)
     cp(T.cTm[:], T.x8[:, 8:16], ["x8b"], ["cTm"])
     ts(T.cPA[:], x8, 0.0, ALU.mult, ["xr", "pf9"], ["cPA"], T.pf[:, 9:10], ALU.add)
-    cp(T.cEx[:], x8, ["xr"], ["cEx"])
+    ts(T.cEx[:], x8, 16.0, ALU.mult, ["xr"], ["cEx"], 15.0, ALU.add)
     ts(T.Dm[:, 0:16], T.xr[:, 0:16], kc, ALU.is_equal, ["xr", "pf"], ["Dm"])
     ts(T.Dm[:, 16:32], T.xr[:, 1:17], kc, ALU.is_equal, ["xr", "pf"], ["Dm2"])
     tt(T.Dm[:, 0:16], T.Dm[:, 0:16], T.Dm[:, 16:32], ALU.subtract, ["Dm", "Dm2"], ["Dm"])
@@ -393,42 +480,49 @@ def record(g, core, T, topo):
     ts(dumz, x8, 16.0, ALU.mult, ["xr", "pf13"], ["dumz"], T.pf[:, 13:14], ALU.add)
     ts(T.BO[:], T.xq[:], gc_, ALU.is_equal, ["xq", "pf"], ["cBO"])
     ts(T.mA[:], T.xm[:], kc, ALU.is_equal, ["xm", "pf"], ["mA"])
-    ts(T.mK[:], T.xk[:], kc, ALU.is_equal, ["xk", "pf"], ["mK"])
+    ts(T.mK[:, 0:L], T.xk[:], kc, ALU.is_equal, ["xk", "pf"], ["mK0"], -0.5, ALU.mult)
+    ts(T.mK[:, L:2 * L], T.mK[:, 0:L], -32.0, ALU.mult, ["mK0"], ["mK"])
     ts(T.TRI[:], T.lx[:], T.pf[:, 10:11], ALU.is_le, ["lx", "pf10"], ["TRI"], 4096.0, ALU.mult)
     for gg in range(8):
         ts(T.SEL[:, gg * L:(gg + 1) * L], T.ones[:], T.BO[:, 16 * gg:16 * gg + 1], ALU.mult, ["ones", "cBO"], ["SEL%d" % gg])
     SELK = ["SEL%d" % gg for gg in range(8)]
-    ts(T.NSEL[:], T.SEL[:], -1.0, ALU.mult, SELK, ["NSEL"])
+    ts(T.NSEL[:, 0:1024 - RUNS[-1][0] * L], T.SEL[:, RUNS[-1][0] * L:1024], -1.0, ALU.mult, SELK, ["NSEL"])
+    ts(T.pf[:, 16:17], a8, 16.0, ALU.mult, ["pf"], ["pf16"], p1, ALU.add)
+    ts(T.cP3[:, 0:8], T.xr[:, 0:16:2], T.pf[:, 16:17], ALU.add, ["xr", "pf16"], ["cP3"])
+    ts(T.pf[:, 17:18], T.pf[:, 16:17], 2.0, ALU.mult, ["pf16"], ["pf17"], 1.0, ALU.add)
+    ts(T.cP3[:, 8:16], T.xr[:, 0:32:4], T.pf[:, 17:18], ALU.add, ["xr", "pf17"], ["cP4"])
     ts(T.rst[:], T.xk[:], 0.0, ALU.is_gt, ["xk"], ["rst"])
     ts(T.cMx[:], T.xk[:], 0.0, ALU.is_gt, ["xk"], ["cMx"], 17000000.0, ALU.mult)
     ts(T.cMx[:], T.cMx[:], -1000000.0, ALU.add, ["cMx"], ["cMx"])
-    ts(T.spT[:], T.xq[:], 2.0, ALU.mult, ["xq", "pf12"], ["spT"], T.pf[:, 12:13], ALU.add)
-    act(T.Tm[:], T.ECp[:, 0:1024], ID, ECP, ["Tm"], scale=0.0)
-    for buf, c in ((T.idf, 1.0), (T.idp, 2048.0), (T.idq, -2048.0), (T.idu, UNIT), (T.id4, 4.0), (T.id5, 5.0)):
+    for h in range(2):
+        ts(T.spT[:, h::2], T.xq[:], 2.0, ALU.mult, ["xq", "pf12"], ["spT%d" % h], T.pf[:, 12:13], ALU.add)
+    ms(T.spT[:, 0::32], 0.0, ["spT"], ["spT0", "spT1"])
+    ts(T.k0[:], T.xk[:], 0.0, ALU.is_equal, ["xk"], ["k0"])
+    ts(T.capf[:, 5:6], T.cap32[:], -150.0, ALU.add, ["cap32"], ["capd"])
+    act(T.Tm[:], T.ECp[:, 0:1024], ID, ECP, ["Tm0", "Tm1"], scale=0.0)
+    for buf, c in ((T.idf, 1.0), (T.idp, 2048.0), (T.idq, -2048.0), (T.idu, UNIT), (T.id4, 4.0), (T.id5, 5.0), (T.id6, -6.0)):
         act(buf[:], T.idb[:], ID, ["idb"], [buf.name], scale=c)
     act(T.WS[:], T.WB[:], ID, ["WB"], ["WS"], scale=0.25)
-    act(T.WU[:], T.WB[:], ID, ["WB"], ["WU"], scale=UNIT)
 
     def wband(buf, k):
         return buf[:, 15 - k:143 - k]
 
-    def quarters(z, zk, a1, a, ak, n, tag):
-        act(a1[:], z, ID, zk, ["a1" + tag], bias=128.625, scale=0.25)
-        act(n[:], a1[:], ID, ["a1" + tag], ["n" + tag], bias=384.0, scale=-1.0)
-        act(a, a1[:], ID, ["a1" + tag], [ak], bias=-129.0)
-
-    nv = 8 - EQS
-    half = (nv + 1) // 2
-
     def dpos(gg, n=1):
-        if gg >= nv:
-            c = 1024 + (gg - nv) * L
-            return T.PT[:, c:c + n * L], "B2"
-        h = gg // half
-        c = 512 * h + (gg - h * half) * L
-        return T.PD[:, c:c + n * L], "B%d" % (4 + h)
-    runs = [(0, half), (half, nv)] + ([(nv, 8)] if EQS else [])
-    TH = ["th%d" % k for k in range(16)]
+        a, _, bk = [x for x in RUNS if x[0] <= gg < x[1]][0]
+        c = 512 * (bk % 4) + (gg - a) * L
+        return (T.PT, T.PD)[bk // 4][:, c:c + n * L], "B%d" % bk
+    runs = [x[:2] for x in RUNS]
+    EQK = ["eq%d" % n for n in range(8)]
+    TH, TH4 = (["%s%d" % (x, k) for k in range(16)] for x in ("th", "tf"))
+
+    def pieces(out, src, sk, keys, ng):
+        n = src.shape[1]
+        for k in range(16):
+            if k < ng:
+                op("G", lambda o=out[:, k::16]: g.affine_select(o, src, [[0, n]], ALU.is_ge, 0.0, 0, 0), [sk], [keys[k]],
+                   cost=170 + 2 * CYC * n)
+            else:
+                act(out[:, k::16], src, ID, [sk], [keys[k]])
 
     def bank2(a, b):
         c = (a + 1024) % W
@@ -436,13 +530,30 @@ def record(g, core, T, topo):
 
     def spread(lhs, lk, pieces):
         for n, (a, b) in enumerate(pieces):
-            mm(T.PT[:, 512 * n:512 * n + b - a], lhs, T.ECn[:, a - S0:b - S0], [lk] + ECN, "B%d" % n)
+            mm(T.PT[:, 512 * n:512 * n + b - a], lhs, T.ECn[:, a - S0:b - S0], [lk] + ECN, "B%d" % n, True)
 
+    stage[0] = "02"
     cp(T.hp[:, 0:L], T.Tc[:, 0:L], ["tc00", "tc01"], ["hp"])
-    cp(T.To[:], (T.hp[:, 0:L], T.cIn[:]), ["hp", "cIn"], ["To"])
+    ms(T.Tn[:, 0:256:2], 0.0, ["Tne"])
+    cp(T.Tn[:, 1:256:2], (T.hp[:, 0:L], T.cIn[:]), ["hp", "cIn", "Tne"], ["Tn00", "Tn01"])
     mm(T.P7[:, 0:L], T.Zc[:, 0:L], T.idb[:], ["zc0", "idb"], "B7")
-    act(T.Zc[:, ZT:ZR], T.P7[:, 0:L], ID, ["B7"], ["zt0"], bias=-150.0)
-    quarters(T.Zj[:, 0:L], ["zj0"], T.a1j, T.SVs[:, L:256], "a30", T.nj, "j")
+    ts(T.Zc[:, ZT:ZR], T.P7[:, 0:L], -150.0, ALU.add, ["B7"], ["zt0"])
+
+    def raised(win, wk, off, ok, z, zk, ps, bk, val, vk, tag, low=None, lk="low"):
+        a1, old, u = (T["up" + tag][:, n * L:(n + 1) * L] for n in range(3))
+        act(a1, z, ID, [zk], ["a1" + tag], bias=128.625, scale=0.25)
+        if tag in ONV:
+            mn = low if low is not None else u
+            act(old, a1, ID, ["a1" + tag], ["old" + tag], bias=384.0, scale=-1.0)
+            tt(mn, (win, off), old, ALU.min, wk + [ok, "old" + tag], [lk])
+            act(val, a1, ID, ["a1" + tag], [vk], bias=-129.0)
+            return a1, u
+        act(old, (win, off), ID, wk + [ok], ["old" + tag])
+        mm(ps, T.idb[:], a1, ["idb", "a1" + tag], bk)
+        mm(ps, T.idb[:], old, ["idb", "old" + tag], bk)
+        act(u, ps, RELU, [bk], ["u" + tag], bias=384.0, scale=-1.0)
+        act(val, u, ID, ["u" + tag], [vk], bias=255.0, scale=-1.0)
+        return a1, u
 
     for r in range(RO):
         last = r == RO - 1
@@ -450,77 +561,93 @@ def record(g, core, T, topo):
         rs, ns, zn = str(r), str(r + 1), (r + 1) * ZW
         tjk = "tj" + rs
         zc, zck = T.Zc[:, r * ZW:r * ZW + L], "zc" + rs
-        zt, ztk = T.Zc[:, r * ZW + ZT:r * ZW + ZR], ("zt0" if r == 0 else zck)
+        zt, ztk = T.Zc[:, r * ZW + ZT:r * ZW + ZR], "zt" + rs
         zj, zjk = T.Zj[:, r * ZW:r * ZW + L], "zj" + rs
         Fc, Fck = (T.F6[:, 0:1], "F6") if r == 0 else (T.Zc[:, r * ZW + L:r * ZW + L + 1], zck)
         Fj, Fjk = (T.F6[:, 0:1], "F6") if r == 0 else (T.Zj[:, r * ZW + L:r * ZW + L + 1], "zjF" + rs)
-        mn2, a2 = T.mn2[:], T.a2[:]
-        mn3, a3 = T.SVs[:, r * 256:r * 256 + L], T.SVs[:, r * 256 + L:r * 256 + 256]
-        tsrc, tsk = (T.To[:], ["To"]) if r == 0 else (T.Tn[:, 1::2], ["Tn0", "Tn1"])
-        cp((T.Tm[:], T.cTm[:]), tsrc, tsk + ["cTm", "Tm"], ["Tm"])
-        cp(T.Tc[:, r * 256 + L:r * 256 + 256], tsrc, tsk, ["tn" + rs])
-        send("fT" + rs, ["tc%d0" % r, "tc%d1" % r, "tn" + rs])
+        mn3, val3 = T.SVs[:, r * 256:r * 256 + L], T.SVs[:, r * 256 + L:r * 256 + 256]
+        stage[0] = rs + "2"
+        cp(T.Tk[:, s(L)], (T.Tn[:, s(256)], T.cP3[:, 8:16]), ["Tn%d0" % r, "Tn%d1" % r, "cP4"], ["tk" + rs])
+        send("fT" + rs, ["tk" + rs])
         arrive("fT" + rs, [tjk])
-        for lam in range(8):
-            mm(T.P7[:, 16 * lam:16 * lam + 16], T.Tm[:, lam::8], T.Dm[:, 0:16], ["Tm", "Dm"], "B7")
-        act(T.DDs[:, s(L)], T.P7[:, 0:L], ID, ["B7"], ["dds" + rs])
-        send("dd" + rs, ["dds" + rs])
-        for n in range(4):
-            o, bk = bank2(512 * n, 512 * n + 512)
-            mm(o, zt, T.ECp[:, 512 * n:512 * n + 512], [ztk] + ECP, bk)
-        for word in (NEXT2 if r else FIRST2).split():
-            a, b = (int(x) for x in word[1:].split(":"))
-            src = (Xl, T.Tc[:, r * 256 + a // 16:r * 256 + b // 16])
-            rk = ["X", "capb", "tc%d%d" % (r, a // 1024)]
-            if word[0] == "V":
+        send("fN" + rs, ["Tn%d0" % r, "Tn%d1" % r])
+        arrive("fN" + rs, ["Tf" + rs])
+        Tf, dT, TD = T.TD[:, r * 256 + 1:r * 256 + 256:2], T.TD[:, r * 256:r * 256 + 256:2], T.TD[:, s(256)]
+        for h in range(2):
+            tmk, c0 = "Tm%d" % h, r * 256 + 128 * h
+            cp((T.Tm[:, 512 * h:512 * h + 512], T.cTm[:, 0:4]), T.Tn[:, c0 + 1:c0 + 128:2], ["Tn%d%d" % (r, h), "cTm", tmk], [tmk])
+            for lam in range(4):
+                mm(T.P7[:, 64 * h + 16 * lam:64 * h + 16 * lam + 16], T.Tm[:, 512 * h + lam:512 * h + 512:4], T.Dm[:, 0:16], [tmk, "Dm"], "B7")
+        words = [(x[0],) + tuple(int(y) for y in x[1:].split(":")) for x in (NEXT2 if r else FIRST2).split()]
+        banks = {"D": [4, 5], "S": [2, 3, 0, 1]}
+        for e, a, b in words:
+            n = banks["D" if e == "D" else "S"].pop(0)
+            o, bk = (T.PT, T.PD)[n // 4][:, 512 * (n % 4):512 * (n % 4) + b - a], "B%d" % n
+            src = (Xl, T.Tc[:, r * L + a // 16:r * L + b // 16])
+            rk = ["X", "capb", "tc%d%d" % (r, a // 1024), "tc%d%d" % (r, (b - 1) // 1024)]
+            mm(o, zt, T.ECp[:, a:b], [ztk] + ECP, bk)
+            if e == "D":
+                act(T.th[:, 2 * W + a:2 * W + b], o, ID, [bk, "capd"], cols("td", a, b), bias=T.capf[:, 5:6], scale=-1.0)
+                tt(T.bb[:, a:b], src, T.th[:, 2 * W + a:2 * W + b], ALU.is_gt, rk + cols("td", a, b), cols("bb", a, b))
+                scan(T.bo[:, a:b], T.bb[:, a:b], T.C15[:, 0:b - a], ALU.max, ALU.min, cols("bb", a, b) + ["C15"], cols("bo", a, b))
+                continue
+            if e == "V":
                 ts(T.xs[:, a:b], src, T.capf[:, 0:1], ALU.add, rk, cols("xs", a, b))
             else:
                 act(T.xs[:, a:b], src, ID, rk, cols("xs", a, b), bias=T.capf[:, 0:1])
-            o, bk = bank2(a, b)
             mm(o, T.idb[:], T.xs[:, a:b], ["idb"] + cols("xs", a, b), bk)
-        for a in range(0, W, 512):
-            o, bk = bank2(a, a + 512)
-            scan(T.bo[:, a:a + 512], o, T.C15[:], ALU.max, ALU.min, [bk, "C15"], cols("bo", a, a + 512))
+            scan(T.bo[:, a:b], o, T.C15[:, 0:b - a], ALU.max, ALU.min, [bk, "C15"], cols("bo", a, b))
         for u in range(32):
             mm(T.P6[:, 64 * (u // 16):64 * (u // 16) + 64], wband(T.WB, u % 16), T.bo[:, 64 * u:64 * u + 64], ["WB", "bo%d" % u], "B6")
-        quarters(zc, [zck], T.a1, a2, "a2", T.nc, "c")
         act(T.fc[:, 0:2], T.fc[:, 8:10], ID, [Fck, "fb0", "fb1"], ["fc0"], bias=Fc)
         if r == 1:
             cp((XRw, T.SO[:, 0:8]), T.SV[:, 0:L], ["so0", "sv0", "XR"], ["XR"])
         ts(T.FB[:, 1:129], T.P6[:, 0:L], Fc, ALU.is_ge, ["B6", Fck, "FB"], ["FB"])
         act(T.NFs[:, s(L)], T.P6[:, 0:L], SIGN, ["B6", "fc0"], ["nfs" + rs], bias=T.fc[:, 0:1], scale=-1.0)
-        scan(T.ys[:], T.FB[:, 0:L], T.DDs[:, s(L)], ALU.mult, ALU.add, ["FB", "dds" + rs], ["ys"])
+        scan(T.ys[:], T.FB[:, 0:L], T.P7[:, 0:L], ALU.mult, ALU.add, ["FB", "B7"], ["ys"])
+        act(T.DDs[:, s(L)], T.P7[:, 0:L], ID, ["B7"], ["dds" + rs])
+        send("dd" + rs, ["dds" + rs])
+        act(T.X[:, W:SP], zj, ID, [zjk], ["Xz"])
         tt(T.PA[:], (T.ys[:], T.cPA[:]), T.mA[:], ALU.mult, ["ys", "cPA", "mA"], ["PA"])
         cp(T.Pu[:], T.ys[:, 15::16], ["ys"], ["Pu"])
-        tt(mn2, (Xl, T.Pu[:]), T.nc[:], ALU.min, ["X", "Pu", "nc"], ["mn2"])
-        if not last:
-            tt(T.V2s[:, s(L)], mn2, a2, ALU.add, ["mn2", "a2"], ["v2s" + rs])
+        raised(Xl, ["X"], T.Pu[:], "Pu", zc, zck, T.P6[:, 0:L], "B6", T.V2s[:, s(L)], "v2s" + rs, "c")
+        mm(T.P7[:, 0:8], T.PA[:], T.SEL[:, 0::L], SELK + ["PA"], "B7")
         for n, (a, b) in enumerate(runs):
             for gg in range(a, b):
                 o, bk = dpos(gg)
-                mm(o, T.idb[:], T.TRI[:], ["idb", "TRI"], bk)
-                mm(o, T.NSEL[:, gg * L:(gg + 1) * L], T.PA[:], ["NSEL", "PA"], bk)
-            o, bk = dpos(a, b - a)
-            mm(o, T.PA[:], T.SEL[:, a * L:b * L], SELK + ["PA"], bk)
-            if n < 2:
-                ts(T.eq[:, a * L:b * L], o, 0.0, ALU.is_equal, [bk], ["eq%d" % n])
+                mm(o, T.idb[:], T.TRI[:], ["idb", "TRI"] + cols("bo", TRI_AT, TRI_AT + 64), bk, True)
+            for gg in range(a, b):
+                o, bk = dpos(gg)
+                mm(o, T.SEL[:, gg * L:(gg + 1) * L], T.PA[:], SELK + ["PA"], bk)
+            if n < len(runs) - 1:
+                for gg in range(a, b):
+                    ts(T.eq[:, gg * L:(gg + 1) * L], dpos(gg)[0], T.P7[:, gg:gg + 1], ALU.is_equal, [bk, "B7"], [EQK[gg]])
             else:
-                act(T.ab[:, 0:EQS * L], o, ABS, [bk], ["ab"])
-                act(T.eq[:, a * L:b * L], T.ab[:, 0:EQS * L], RELU, ["ab"], ["eq2"], bias=1.0, scale=-1.0)
-        mm(T.PT[:, 1536:1544], T.idf[:], T.ys[:, 15::16], ["idf", "ys"], "B3")
+                o, bk = dpos(a, b - a)
+                mm(o, T.PA[:], T.NSEL[:, 0:(b - a) * L], ["NSEL", "PA"], bk)
+                act(T.ab[:, 0:(b - a) * L], o, ABS, [bk], ["ab"])
+                act(T.eq[:, a * L:b * L], T.ab[:, 0:(b - a) * L], RELU, ["ab"], EQK[a:b], bias=1.0, scale=-1.0)
+        mm(T.PT[:, 1536:1544], T.idf[:], T.ys[:, 15::16], ["idf", "ys"], "B3", True)
         for c in range(8):
-            mm(T.PT[:, 1536 + c:1537 + c], T.eq[:, c::8], T.c4k[:, 0:1], ["eq0", "eq1", "eq2", "c4k"], "B3")
+            mm(T.PT[:, 1536 + c:1537 + c], T.eq[:, c::8], T.c4k[:, 0:1], EQK + ["c4k"], "B3")
         tt(T.Ofs[:, 0:8], T.PT[:, 1536:1544], dum, ALU.min, ["B3", "dum"], ["ofs"])
         cp(T.Ous[:, s(8)], T.Ofs[:, 0:8], ["ofs"], ["ous" + rs])
-        tt((Xw, T.Ous[:, s(8)]), mn2, a2, ALU.add, ["ous" + rs, "mn2", "a2", "Xsent"] + XK, XK)
-        send("oj" + rs, ["ous" + rs])
-        if not last:
-            send("v2" + rs, ["v2s" + rs])
-            send("orp" + rs, ["ous" + rs])
-        o15 = T.PT[:, 0:L]
-        mm(o15, T.idb[:], T.xs[:, 15::16], ["idb"] + cols("xs", 0, W), "B0")
-        mm(o15, T.idp[:], T.bo[:, 14::16], ["idp"] + cols("bo", 0, W), "B0")
-        mm(o15, zt, T.idc[:], [ztk, "idc"], "B0")
+        cp((Xw, T.Ous[:, s(8)]), T.V2s[:, s(L)], ["ous" + rs, "v2s" + rs, "Xsent"] + XK, XK)
+        send("oj" + rs + (" orp" + rs) * (not last), ["ous" + rs])
+        mm(T.PT[:, 0:L], T.idp[:], T.bo[:, 14::16], ["idp"] + cols("bo", 0, W), "B0", True)
+        spans = []
+        for e, a, b in sorted(words, key=lambda x: x[1]):
+            if spans and spans[-1][0] == (e == "D"):
+                spans[-1][2] = b
+            else:
+                spans.append([e == "D", a, b])
+        for direct, a, b in spans:
+            o = T.PT[:, a // 16:b // 16]
+            if direct:
+                mm(o, T.idp[:], T.bb[:, a + 15:b:16], ["idp"] + cols("bb", a, b), "B0")
+            else:
+                mm(o, T.idb[:], T.xs[:, a + 15:b:16], ["idb"] + cols("xs", a, b), "B0")
+                mm(o, zt, T.idc[:, a // 16:b // 16], [ztk, "idc"], "B0")
         for h in range(2):
             act(T.s15[:, h::2], T.PT[:, 64 * h:64 * h + 64], SIGN, ["B0"], ["s15%d" % h], bias=-0.5)
         for mu in range(16):
@@ -529,74 +656,95 @@ def record(g, core, T, topo):
             act(T.NFs[:, r * L + 64 * h + 15:r * L + 64 * h + 64:16], T.PT[:, 512 + h:520:2], SIGN,
                 ["B1", "fc0", "nfs" + rs], ["nf%s%d" % (rs, h)], bias=T.fc[:, 1:2], scale=-0.5)
         send("nf" + rs, ["nfs" + rs, "nf%s0" % rs, "nf%s1" % rs])
+        if not last:
+            send("v2" + rs, ["v2s" + rs])
         for nm in ("dd", "nf", "oj"):
             arrive(nm + rs, [nm + rs])
+        stage[0] = rs + "3"
         NF = T.NF[:, s(L)]
         v3 = S3[0][0]
-        act(T.t3[:], (zj, T.cP0[:]), RELU, [zjk, "cP0", "capp"], ["t3"], bias=T.capf[:, 1:2], scale=-1.0)
-        mm(T.P7[:, L:2 * L], T.t3[:], T.idb[:], ["t3", "idb"], "B7")
+        act(T.t3[:, 0:L], (zj, T.cP3[:, 0:8]), RELU, [zjk, "cP3", "capp"], ["t3"], bias=T.capf[:, 1:2], scale=-1.0)
+        mm(T.P7[:, L:2 * L], T.t3[:, 0:L], T.idb[:], ["t3", "idb"], "B7")
         act(T.t3T[:], T.P7[:, L:2 * L], ID, ["B7"], ["t3T"], scale=-1.0)
         spread(T.t3T[:], "t3T", S3)
-        for k in range(16):
-            act(T.th[:, k:v3:16], T.t3[:, 0:v3 // 16], ID, ["t3"], ["th%d" % k])
-        cp(T.TD[:, 1::2], T.Tj[:, r * 256 + L:r * 256 + 256], [tjk], ["Tf"])
+        pieces(T.th[:, 0:v3], T.t3[:, 0:v3 // 16], "t3", TH, G3[r])
         mm(T.PD[:, 0:L], T.BO[:], zj, ["cBO", zjk], "B4")
-        mm(T.PD[:, 0:L], T.id5[:], T.TD[:, 1::2], ["id5", "Tf"], "B4")
+        mm(T.PD[:, 0:L], T.id5[:], Tf, ["id5", "Tf" + rs], "B4")
         act(T.qq[:], T.PD[:, 0:L], ID, ["B4"], ["qq"], bias=128.500732421875, scale=1.0 / 2048)
         mm(T.PD[:, 512:640], T.BO[:], zj, ["cBO", zjk], "B5")
-        mm(T.PD[:, 512:640], T.id4[:], T.TD[:, 1::2], ["id4", "Tf"], "B5")
+        mm(T.PD[:, 512:640], T.id4[:], Tf, ["id4", "Tf" + rs], "B5")
         mm(T.PD[:, 512:640], T.idq[:], T.qq[:], ["idq", "qq"], "B5")
-        act(T.TD[:, 0::2], T.PD[:, 512:640], ID, ["B5"], ["dT"], bias=264193.0)
+        act(dT, T.PD[:, 512:640], ID, ["B5", "Tf" + rs], ["dT"], bias=264193.0)
+        a1, u = raised(Xw, XK, T.Oj[:, s(8)], "oj" + rs, zj, zjk, T.PD[:, 0:L], "B4", val3, "val3" + rs, "j", mn3, "mn3" + rs)
+        if not last and "j" not in ONV:
+            mm(T.PD[:, 0:L], T.idb[:], a1, ["idb", "a1j"], "B4")
+            mm(T.PD[:, 0:L], T.idb[:], u, ["idb", "uj"], "B4")
+            act(mn3, T.PD[:, 0:L], ID, ["B4"], ["mn3" + rs], bias=384.0, scale=-1.0)
         cp(T.Ofs[:, 8:16], T.Oj[:, s(8)], ["oj" + rs], ["of"])
-        mm(T.PD[:, 0:8], T.idf[:], T.Ofs[:, 8:16], ["idf", "of"], "B4")
-        mm(T.PD[:, 0:8], T.idp[:], T.NF[:, r * L + 15:(r + 1) * L:16], ["idp", "nf" + rs], "B4")
-        mm(T.PD[:, 0:8], T.idp[:], T.ones[:, 0:8], ["idp", "ones"], "B4")
-        tt(T.E[:, 0::32], T.PD[:, 0:8], dum, ALU.min, ["B4", "dum", "E0"], ["E0"])
+        mm(T.P6[:, 1:256:2], T.idp[:], T.k0[:], ["idp", "k0"], "B6", True)
+        mm(T.P6[:, 1:256:32], T.idf[:], T.Ofs[:, 8:16], ["idf", "of"], "B6")
+        mm(T.P6[:, 1:256:32], T.idp[:], T.NF[:, r * L + 15:(r + 1) * L:16], ["idp", "nf" + rs], "B6")
         act(T.fc[:, 3:4], Fj, ID, [Fjk], ["fc3"], bias=-5.0, scale=-1.0)
-        act(T.NFm[:], NF, ID, ["nf" + rs, "fc3"], ["NFm"], bias=T.fc[:, 3:4], scale=-6.0)
-        mm(T.P6[:, 0:L], T.idu[:], T.NFm[:], ["idu", "NFm"], "B6")
-        for a, b in V3:
-            tt(T.xs[:, a:b], (Xl, T.Tj[:, r * 256 + a // 16:r * 256 + b // 16]), T.th[:, a:b], ALU.subtract,
-               ["X", tjk] + TH, cols("xs", a, b))
-            act(T.bo[:, a:b], T.xs[:, a:b], RELU, cols("xs", a, b), cols("bo", a, b), bias=1.0)
-            ts(T.bb[:, a:b], T.xs[:, a:b], 0.0, ALU.is_ge, cols("xs", a, b), cols("bb", a, b))
-        for n, (a, b) in enumerate(S3):
-            o = T.PT[:, 512 * n:512 * n + b - a]
-            act(T.xs[:, a:b], (Xl, T.Tj[:, r * 256 + a // 16:r * 256 + b // 16]), ID, ["X", tjk], cols("xs", a, b))
-            mm(o, T.idb[:], T.xs[:, a:b], ["idb"] + cols("xs", a, b), "B%d" % n)
-            act(T.bo[:, a:b], o, RELU, ["B%d" % n], cols("bo", a, b), bias=1.0)
-            ts(T.bb[:, a:b], T.bo[:, a:b], 0.5, ALU.is_ge, cols("bo", a, b), cols("bb", a, b))
-        for u in range(32):
-            c = slice(64 * (u // 16), 64 * (u // 16) + 64)
-            mm(T.P6[:, c], wband(T.WU, u % 16), T.bb[:, 64 * u:64 * u + 64], ["WU", "bb%d" % u], "B6")
-            mm(T.P7[:, c], wband(T.WS, u % 16), T.bo[:, 64 * u:64 * u + 64], ["WS", "bo%d" % u], "B7")
-        act(T.X[:, W:SP], zj, ID, [zjk], ["Xz"])
-        tt(mn3, (Xw, T.Oj[:, s(8)]), T.nj[:], ALU.min, XK + ["oj" + rs, "nj"], ["mn3" + rs])
-        tt(T.E[:, 1::2], T.P6[:, 0:L], T.spT[:], ALU.min, ["B6", "spT", "E1"], ["E1"])
-        scan(T.Es[:], T.rs2[:], T.E[:], ALU.mult, ALU.max, ["rs2", "E0", "E1"], ["Es"])
+        act(T.NFm[:], T.idb[:], ID, ["idb", "fc3"], ["NFm"], scale=T.fc[:, 3:4])
+        mm(T.PT[:, 1536:1664], T.ones[:], T.NFm[:], ["ones", "NFm"], "B3", True)
+        mm(T.PT[:, 1536:1664], NF, T.id6[:], ["id6", "nf" + rs], "B3")
+        tail_of = {}
+        for word in ORD3.split():
+            n = int(word[3])
+            a, b = (V3 if word[2] == "v" else S3)[n]
+            src, o = (Xl, T.Tj[:, r * L + a // 16:r * L + b // 16]), T.PT[:, 512 * n:512 * n + b - a]
+            xs, bo, bb = cols("xs", a, b), cols("bo", a, b), cols("bb", a, b)
+            if word[:3] == "Vgv":
+                tt(T.xs[:, a:b], src, T.th[:, a:b], ALU.subtract, ["X", tjk] + TH, xs)
+            elif word[:3] == "Sgs":
+                act(T.xs[:, a:b], src, ID, ["X", tjk], xs)
+            elif word[:3] == "Sev":
+                act(T.bo[:, a:b], T.xs[:, a:b], RELU, xs, bo, bias=1.0)
+            elif word[:3] == "Vev":
+                ts(T.bo[:, a:b], T.xs[:, a:b], 1.0, ALU.add, xs, bo, 0.0, ALU.max)
+            elif word[:3] == "Ses":
+                act(T.bo[:, a:b], o, RELU, ["B%d" % n], bo, bias=1.0)
+            elif word[:3] == "Vmv":
+                ts(T.bb[:, a:b], T.xs[:, a:b], 0.0, ALU.is_ge, xs, bb)
+            else:
+                ts(T.bb[:, a:b], T.bo[:, a:b], 0.5, ALU.is_ge, bo, bb)
+            if word[0] in tail_of:
+                ops[-1]["soft"][tail_of[word[0]]] = 0
+            tail_of[word[0]] = len(ops) - 1
+            if word[:3] == "Sgs":
+                mm(o, T.idb[:], T.xs[:, a:b], ["idb"] + xs, "B%d" % n)
+        key = T.P7[:, 16:16 + L]
+        for mu in range(16):
+            c = slice(L * mu, L * mu + L)
+            mm(T.PT[:, 1536 + mu:1664:16], T.bb[:, c], T.BO[:, 0::16], ["cBO"] + cols("bb", c.start, c.stop), "B3")
+            mm(key, wband(T.WS, mu), T.bo[:, c], ["WS"] + cols("bo", c.start, c.stop), "B7")
+        ts(T.ful[:], T.PT[:, 1536:1664], 0.5, ALU.is_ge, ["B3"], ["ful"])
+        mm(key, T.ful[:], T.idu[:], ["idu", "ful"], "B7")
+        mm(T.P6[:, 0:256:2], T.ful[:], T.idu[:], ["idu", "ful"], "B6")
+        scan(T.Es[:], T.spT[:], T.P6[:, 0:256], ALU.min, ALU.max, ["spT", "B6"], ["Es"])
         cp(T.SOs[:, s(8)], T.Es[:, 31::32], ["Es"], ["sos" + rs])
         if not last:
-            send("sv" + rs, ["mn3" + rs, "a3" + rs])
+            send("sv" + rs, ["mn3" + rs, "val3" + rs])
             send("so" + rs, ["sos" + rs])
-        tt(T.KB[:, 1:129], T.E[:, 1::2], T.P7[:, 0:L], ALU.min, ["E1", "B7", "KB"], ["KB"])
-        scan(T.P7[:, L:2 * L], T.KB[:, 0:L], T.cMx[:], ALU.max, ALU.min, ["KB", "cMx"], ["B7"])
-        tt(T.ng3[:], T.KB[:, 1:129], T.P7[:, L:2 * L], ALU.is_le, ["KB", "B7"], ["ng3"])
+        scan(T.KB[:], T.P7[:, 15:15 + L], T.cMx[:], ALU.max, ALU.min, ["B7", "cMx"], ["KB"])
+        tt(T.ng3[:], key, T.KB[:], ALU.is_le, ["KB", "B7"], ["ng3"])
         scan(T.y3[:], T.ng3[:], T.DD[:, s(L)], ALU.mult, ALU.add, ["ng3", "dd" + rs], ["y3"])
         cp(T.Tmu[:], T.y3[:, 15::16], ["y3"], ["Tmu"])
         cp(T.Vs[:, s(L)], (T.man[:], T.Tmu[:]), MAN + ["Tmu"], ["vs" + rs])
         send("V" + rs, ["vs" + rs])
-        scan(T.rq[:], T.rst[:], T.E[:, 1::2], ALU.mult, ALU.max, ["rst", "E1"], ["rq"])
+        scan(T.rq[:], T.rst[:], T.P6[:, 0:256:2], ALU.mult, ALU.max, ["rst", "B6"], ["rq"])
         scan(T.js[:], T.rst[:], NF, ALU.mult, ALU.add, ["rst", "nf" + rs], ["js"])
-        act(T.ww[:, 16:24], T.rq[:, 15::16], ID, ["rq"], ["tt"], bias=16.0, scale=-1.0)
-        tt(T.vv[:], T.ww[:, 16:24], T.js[:, 15::16], ALU.max, ["tt", "js"], ["vv"])
-        tt(T.ex[:], (T.vv[:], T.cEx[:]), T.mK[:], ALU.mult, ["vv", "cEx", "mK"], ["ex"])
-        mm(T.P6[:, 0:L], T.BO[:], T.ex[:], ["cBO", "ex"], "B6")
-        act(T.AP2[:, 1::2], T.P6[:, 0:L], RELU, ["B6"], ["ap", "nn"], bias=-7.0, scale=0.5, acc=T.nn[:, 0:1])
-        act(T.Rm[:, 0:L], T.P6[:, 0:L], RELU, ["B6", "pf11"], ["R"], bias=T.pf[:, 11:12], scale=0.5)
-        act(T.Rm[:, L:2 * L], T.Rm[:, 0:L], RELU, ["R"], ["Rm"], bias=1.0, scale=-1.0)
-        tt(T.ys[:], (T.man[:], T.Tmu[:]), T.TD[:, 1::2], ALU.subtract, MAN + ["Tmu", "Tf"], ["ys"])
-        scan(T.DAs[:, s(256)], T.AP2[:], T.TD[:], ALU.mult, ALU.add, ["AP0", "ap", "Tf", "dT"], ["aa" + rs])
-        tt(T.DAs[:, r * 256:(r + 1) * 256:2], T.ys[:], T.Rm[:, L:2 * L], ALU.mult, ["ys", "Rm", "aa" + rs], ["aa" + rs])
+        tt(T.ex[:, 0:L], (T.js[:], T.cEx[:]), T.mK[:, 0:L], ALU.mult, ["js", "cEx", "mK"], ["exj"])
+        tt(T.ex[:, L:2 * L], (T.rq[:], T.cEx[:]), T.mK[:, L:2 * L], ALU.min, ["rq", "cEx", "mK"], ["ex"])
+        mm(T.PT[:, 1536:1664], T.BO[:], T.ex[:, 0:L], ["cBO", "exj"], "B3")
+        mm(T.PT[:, 1536:1664], T.BO[:], T.ex[:, L:2 * L], ["cBO", "ex"], "B3")
+        mm(T.PT[:, 1664:1792], T.BO[:], T.ex[:, L:2 * L], ["cBO", "ex"], "B3")
+        act(T.AP2[:, 1::2], T.PT[:, 1664:1792], RELU, ["B3"], ["ap", "nn"], bias=1.0, scale=-1.0, acc=T.nn[:, 0:1])
+        act(T.Rm[:], T.PT[:, 1536:1664], RELU, ["B3", "pf11"], ["R"], bias=T.pf[:, 11:12], scale=-1.0)
+        act(T.PT[:, 1536:1664], T.Rm[:], RELU, ["R"], ["B3"], bias=1.0, scale=-1.0)
+        tt(T.ys[:], (T.man[:], T.Tmu[:]), Tf, ALU.subtract, MAN + ["Tmu", "Tf" + rs], ["ys"])
+        scan(T.DAs[:, s(256)], T.AP2[:], TD, ALU.mult, ALU.add, ["AP0", "ap", "Tf" + rs, "dT"], ["aa" + rs])
+        tt(T.DAs[:, r * 256:(r + 1) * 256:2], T.ys[:], T.PT[:, 1536:1664], ALU.mult, ["ys", "B3", "aa" + rs], ["aa" + rs])
         send("da" + rs, ["aa" + rs])
         tt(T.ww[:, 0:8], dumz, T.rq[:, 15::16], ALU.subtract, ["dumz", "rq"], ["w1"])
         tt(T.ww[:, 8:16], T.ww[:, 0:8], T.y3[:, 15::16], ALU.max, ["w1", "y3"], ["w2"])
@@ -611,26 +759,31 @@ def record(g, core, T, topo):
         act(T.Zj[:, zn:zn + L], T.hp[:, 0:L], ID, ["hp"], ["zj" + ns], bias=-MAGIC)
         if last:
             send("Z" + rs, ["zj" + ns])
-            tt((Xw, T.SOs[:, s(8)]), mn3, a3, ALU.add, ["sos" + rs, "mn3" + rs, "a3" + rs] + XK, XK)
+            tt((Xw, T.SOs[:, s(8)]), mn3, val3, ALU.add, ["sos" + rs, "mn3" + rs, "val3" + rs] + XK, XK)
             dma("Y", "ysect", T.X[:, 0:W], ["X"], ["ysect"], 3000)
         else:
             act(T.nq[:, 0:1], T.nn[:, 0:1], ID, ["nn"], ["nq"], bias=128.75, scale=0.5)
-            act(T.nn[:, 1:2], T.nq[:, 0:1], ID, ["nq", "nn"], ["nf"], bias=T.nn[:, 0:1], scale=-2.0)
+            act(T.nn[:, 1:2], T.nn[:, 0:1], ID, ["nn"], ["nf"], bias=264.0)
             act(T.Zj[:, zn + ZT:zn + ZR], T.hp[:, L:2 * L], ID, ["hp"], ["zjT" + ns], bias=-MAGIC - 150.0)
-            act(T.Zj[:, zn + L:zn + L + 1], T.nn[:, 1:2], ID, ["nf", "zjF" + ns], ["zjF" + ns], bias=264.0)
-            send("Z" + rs, ["zj" + ns, "zjF" + ns, "zjT" + ns])
-            cp((Xw, T.SOs[:, s(8)]), mn3, ["sos" + rs, "mn3" + rs] + XK, XK)
-            quarters(T.Zj[:, zn:zn + L], ["zj" + ns], T.a1j, T.SVs[:, (r + 1) * 256 + L:(r + 2) * 256], "a3" + ns, T.nj, "j")
+            act(T.Zj[:, zn + L:zn + L + 1], T.nq[:, 0:1], ID, ["nq", "nf", "zjF" + ns], ["zjF" + ns], bias=T.nn[:, 1:2], scale=-2.0)
+            send("Z" + rs, ["zjT" + ns])
+            send("zF" + rs, ["zj" + ns, "zjF" + ns])
+            if r == RO - 2:
+                send("Zb" + rs, ["zj" + ns, "zjF" + ns, "zjT" + ns])
+            cp((Xw, T.SOs[:, s(8)]), mn3, ["sos" + rs, "mn3" + rs] + XK, ["net"] + XK)
             for nm in ("v2", "orp", "sv", "so"):
                 arrive(nm + rs, [nm + rs])
-            cp((XRw, T.Orp[:, s(8)]), T.V2[:, s(L)], ["orp" + rs, "v2" + rs, "XR0", "XR1", "XRd", "XR"], ["XR"])
+            for h in range(NXW):
+                n = 8 // NXW
+                cp((XRw, T.Orp[:, r * 8 + n * h:r * 8 + n * h + n]), T.V2[:, r * L + 16 * n * h:r * L + 16 * n * (h + 1)],
+                   ["orp" + rs, "v2" + rs, "XR0", "XR1", "XR2", "XR3", "XRd", "XR"], ["xw%d" % h, "XR"])
             tt((XRw, T.SO[:, s(8)]), T.SV[:, r * 256:r * 256 + L], T.SV[:, r * 256 + L:r * 256 + 256], ALU.add,
                ["so" + rs, "sv" + rs, "XR"], ["XR"])
         if r == RO - 2:
-            send("Zb" + rs, ["zj" + ns, "zjF" + ns, "zjT" + ns])
             arrive("Zb" + rs, ["zh0"])
         arrive("V" + rs, ["vl" + rs])
         arrive("da" + rs, ["da" + rs])
+        stage[0] = rs + "4"
         if last:
             arrive("Z" + rs, ["zh1"])
             dma("Y", "yamt", T.Zh[:, ZW:ZW + L], ["zh1"], ["yamt"], 1500)
@@ -638,19 +791,21 @@ def record(g, core, T, topo):
             z4, z4k, F4, F4k, zt4, zt4k = T.Zh[:, 0:L], "zh0", T.Zh[:, L:L + 1], "zh0", T.Zh[:, ZT:ZR], "zh0"
             cap4, cap4b, cap4k = T.capf[:, 2:3], T.capf[:, 0:1], ["capo", "capb"]
         else:
-            arrive("Z" + rs, ["zc" + ns])
+            arrive("Z" + rs, ["zt" + ns])
+            arrive("zF" + rs, ["zc" + ns])
             win, wk = XRl, "XR"
             z4, z4k, F4, F4k, zt4, zt4k = zc, zck, Fc, Fck, zt, ztk
             cap4, cap4b, cap4k = T.capf[:, 3:4], T.capf[:, 4:5], ["capH", "capJ"]
-        v4 = S4[0][0]
+        S4, V4 = STEP4[last]
+        v4 = V4[-1][1]
         spread(zt4, zt4k, S4)
-        for k in range(16):
-            act(T.th[:, k:v4:16], z4[:, 0:v4 // 16], ID, [z4k] + cap4k, ["th%d" % k], bias=cap4, scale=-1.0)
+        act(T.t3[:, L:2 * L], z4, ID, [z4k] + cap4k, ["t4"], bias=cap4, scale=-1.0)
+        pieces(T.th[:, W:W + v4], T.t3[:, L:L + v4 // 16], "t4", TH4, G4[r])
         act(T.fc[:, 4:5], F4, ID, [F4k], ["fc4"], bias=16.0, scale=-1.0)
-        act(T.off[:, v4 // 16:L], T.ones[:, v4 // 16:L], ID, ["ones", "fc4", "off"], ["off"], scale=T.fc[:, 4:5])
+        act(T.off[:], T.onS[:, L * last:L * last + L], ID, ["onS", "fc4"], ["off"], scale=T.fc[:, 4:5])
         for a, b in V4:
-            tt(T.bb[:, a:b], (win, T.Vl[:, r * L + a // 16:r * L + b // 16]), T.th[:, a:b], ALU.is_gt,
-               [wk, "vl" + rs] + TH, cols("bb", a, b))
+            tt(T.bb[:, a:b], (win, T.Vl[:, r * L + a // 16:r * L + b // 16]), T.th[:, W + a:W + b], ALU.is_gt,
+               [wk, "vl" + rs] + TH4, cols("bb", a, b))
         for n, (a, b) in enumerate(S4):
             o = T.PT[:, 512 * n:512 * n + b - a]
             act(T.xs[:, a:b], (win, T.Vl[:, r * L + a // 16:r * L + b // 16]), ID, [wk, "vl" + rs] + cap4k, cols("xs", a, b), bias=cap4b)
@@ -658,20 +813,25 @@ def record(g, core, T, topo):
             act(T.bb[:, a:b], o, SIGN, ["B%d" % n], cols("bb", a, b), bias=-0.5)
         for h in range(2):
             pk, bk, c = (T.P6, T.P7)[h][:, 0:64], "B%d" % (6 + h), slice(128 * h, 128 * h + 128)
-            if h:
-                mm(pk, T.idb[:], T.off[:, 64:L], ["idb", "off"], bk)
+            if [1 for a, b in S4 if a // 1024 == h]:
+                mm(pk, T.idb[:], T.off[:, 64 * h:64 * h + 64], ["idb", "off"], bk)
             for k in range(16):
                 mm(pk, wband(T.WB, k), T.bb[:, 1024 * h + k:1024 * h + 1024:16], ["WB"] + cols("bb", 1024 * h, 1024 * h + 1024), bk)
             ts(T.TK[:, 128 * h + 1:128 * h + 128:2], pk, F4, ALU.is_lt, [bk, F4k, "TK%d" % h], ["TK%d" % h])
-            scan(T.Tn[:, c], T.TK[:, c], T.DA[:, r * 256 + 128 * h:r * 256 + 128 * h + 128], ALU.mult, ALU.add,
-                 ["TK%d" % h, "da" + rs], ["Tn%d" % h])
+            n0, tnk = (r + 1) * 256 + 128 * h, "Tn%d%d" % (r + 1, h)
+            scan(T.Tn[:, n0:n0 + 128], T.TK[:, c], T.DA[:, r * 256 + 128 * h:r * 256 + 128 * h + 128], ALU.mult, ALU.add,
+                 ["TK%d" % h, "da" + rs], [tnk])
             if last:
-                cp(T.To[:, 64 * h:64 * h + 64], T.Tn[:, 128 * h + 1:128 * h + 128:2], ["Tn%d" % h, "To"], ["To%d" % h])
+                cp(T.To[:, 64 * h:64 * h + 64], T.Tn[:, n0 + 1:n0 + 128:2], [tnk], ["To%d" % h])
             else:
-                c0 = (r + 1) * 256 + 64 * h
-                cp(T.Tc[:, c0:c0 + 64], (T.Tn[:, c], T.cP1[:, 0:4]), ["Tn%d" % h, "cP1"], ["tc%d%d" % (r + 1, h)])
-    dma("Y", "ytraj", T.To[:], ["To0", "To1"], ["ytraj"], 1500)
+                c0 = (r + 1) * L + 64 * h
+                cp(T.Tc[:, c0:c0 + 64], (T.Tn[:, n0:n0 + 128], T.cP1[:, 0:4]), [tnk, "cP1"], ["tc%d%d" % (r + 1, h)])
+    dma("Y", "ytraj", T.To[:], ["To0", "To1"], ["ytraj"], LOAD)
     op("Y", None, ["ysect", "yamt", "ytraj"], ())
+    for r in range(RO):
+        for q, lines in list(CHAINS.items()) + (list(CHAINS0.items()) if r == 0 else []):
+            for words in lines:
+                chain(r, q, words)
     return ops, eng, total["sent"]
 
 

from concourse.bass import DstId, RemoteDMATransfer
from concourse.mybir import AluOpType as ALU, ActivationFunctionType as ACT

N, W, L, Q, RO, SB, SC = 6, 2048, 128, 512, 3, 1, 4
H = "float16"
BF, F32, U16, I32 = "bfloat16", "float32", "uint16", "int32"
SP = W + L
XW = SP + 2 * L
ZW = 272
ZT, ZR = 144, 272
LATE_ENGINES = ("bk", "iZ", "iC", "v2", "or", "sv", "Zb", "fN", "dd", "zF")
UNIT = 2560.0
S0 = 512
S3 = [(1280, 1792), (1792, 2048)]
V3 = [(0, 512), (512, 1024), (1024, 1280)]
ORD3 = "Vgv0 Sgs0 Vgv1 Sgs1 Sev0 Vmv0 Ses0 Vgv2 Vmv1 Ses1 Vms0 Sev1 Vmv2 Vev2 Vms1"
FIRST, SLACK = 800, 1000
ROOM = {"fN": 4, "zF": 2, "dd": 3, "fT": 1.5, "v": 1.2, "orp": 0.8, "sv": 0.5, "Zb": 3, "iC": 3, "fZ": 1, "nf": 1.5, "oj": 0.8,
        "da": 0.4, "Z": 0.7, "bk": 3}
STEP4 = [([(768, 1024), (1664, 2048)], [(0, 768), (1024, 1664)]),
         ([(1280, 1792), (1792, 2048)], [(0, 512), (512, 1024), (1024, 1280)])]
FIRST2 = "S0:512 V512:768 S768:1024 S1024:1536 D1536:2048"
NEXT2 = "S0:512 S512:1024 S1024:1408 D1408:1664 D1664:2048"
EQS = 1
MAGIC = 12582912.0
CYC, PEC, LINK, HOP, ISSUE, FIXV, FIXS, GATHER, SCATTER = 0.83, 0.45, 180, 1350, 250, 25, 35, 1.56, 3.8
FIXP, TRI_AT = 5, 0
G3, G4 = (0, 6, 6), (6, 6, 6)
LOAD, GIVE = 1300, 150
CHAINS = {}
CHAINS0 = {"S": ["2xs0 2xs16 2xs12 2a1c"], "G": ["1pi0 1pi8 1x8a 1xr 1iZ 1iT 1lc 1x8b 1x8c 1xq"],
           "V": ["1pi6 1pi7 1pq 1cP0", "2xs8 2zt0 2hp 2Tn00 2Tm0 2Tm1"]}
LATE_Z, NXW, ONV = 700, 1, "j"
LANE = {"fN": 2, "dd": 3, "zF": 1, "Zb": 3}
RUNS = [(0, 2, 4), (2, 4, 5), (4, 6, 1), (6, 8, 2)]


def sb(n, d):
    return ("sbuf", [128, n], d)


SCRATCH = {
    "X": sb(XW, BF), "XR": sb(XW, BF), "man": sb(W, F32), "mv32": sb(Q, I32), "tr32": sb(L, I32), "Th": sb(L, U16),
    "cap32": sb(1, I32), "Rm": sb(L, BF), "cIn": sb(8, U16),
    "Zs": sb(L, BF), "Cs": sb(8, BF), "Ch": sb(8, BF),
    "Tc": sb(RO * L, U16), "Zc": sb(RO * ZW, BF), "Tj": sb(RO * L, U16), "Zj": sb(4 * ZW, BF), "Zh": sb(2 * ZW, BF),
    "DDs": sb(RO * L, F32), "DD": sb(RO * L, F32), "NFs": sb(RO * L, BF), "NF": sb(RO * L, BF), "NFm": sb(L, BF),
    "Ous": sb(RO * 8, U16), "Oj": sb(RO * 8, U16), "Orp": sb(RO * 8, U16), "Ofs": sb(16, F32),
    "V2s": sb(RO * L, BF), "V2": sb(RO * L, BF), "SVs": sb(RO * 256, BF), "SV": sb(RO * 256, BF),
    "SOs": sb(RO * 8, U16), "SO": sb(RO * 8, U16), "Vs": sb(RO * L, U16), "Vl": sb(RO * L, U16),
    "DAs": sb(RO * 256, H), "DA": sb(RO * 256, H),
    "xs": sb(W, BF), "bb": sb(W, BF), "bo": sb(W, BF), "th": sb(3 * W, BF), "ECp": sb(W, BF), "ECn": sb(W - S0, BF),
    "eq": sb(1024, BF), "ab": sb(512, BF), "SEL": sb(1024, H), "NSEL": sb(1024, H), "Tm": sb(1024, F32),
    "pi": sb(16, I32), "pf": sb(24, F32), "xr": sb(144, F32), "xq": sb(L, F32), "xm": sb(L, F32), "xk": sb(L, F32),
    "lc": sb(L, F32), "lx": sb(L, F32), "x8": sb(24, F32),
    "idb": sb(L, BF), "idc": sb(L, BF), "idf": sb(L, F32), "id4": sb(L, F32), "id5": sb(L, F32), "idq": sb(L, BF), "idp": sb(L, BF),
    "idu": sb(L, BF), "id6": sb(L, BF),
    "WB": sb(144, BF), "WS": sb(144, BF), "BO": sb(L, BF), "TRI": sb(L, BF), "mA": sb(L, BF), "mK": sb(2 * L, BF),
    "ones": sb(L, BF), "Dm": sb(32, F32), "C15": sb(512, BF), "rst": sb(L, BF), "k0": sb(L, BF),
    "cMx": sb(L, F32), "c4k": sb(8, BF), "spT": sb(256, F32),
    "cTm": sb(8, U16), "cPA": sb(8, U16), "cEx": sb(8, U16), "cP0": sb(8, U16), "cP1": sb(8, U16), "cP3": sb(16, U16),
    "Tk": sb(RO * L, U16), "ful": sb(L, BF),
    "dum": sb(16, F32), "capf": sb(8, F32), "F6": sb(8, BF), "fc": sb(16, F32),
    "t3": sb(2 * L, BF), "t3T": sb(L, BF), "off": sb(L, BF), "onS": sb(2 * L, BF),
    "upc": sb(3 * L, BF), "upj": sb(3 * L, BF), "s15": sb(L, BF),
    "FB": sb(144, BF), "ys": sb(L, F32), "PA": sb(L, H), "Pu": sb(8, U16),
    "Es": sb(256, F32), "rq": sb(L, F32), "KB": sb(L, F32), "ng3": sb(L, BF), "y3": sb(L, F32), "Tmu": sb(8, U16),
    "js": sb(L, F32), "ww": sb(24, F32), "Yu": sb(8, U16),
    "ex": sb(2 * L, BF), "AP2": sb(256, BF), "nn": sb(8, F32), "nq": sb(8, BF),
    "ymp": sb(L, BF), "hp": sb(256, F32),
    "TD": sb(RO * 256, F32), "qq": sb(L, BF), "TK": sb(256, BF), "Tn": sb(4 * 256, F32), "To": sb(L, F32),
    "PT": ("psum", [128, 2048], F32), "PD": ("psum", [128, 1024], F32), "P6": ("psum", [128, 512], F32), "P7": ("psum", [128, 512], F32),
}
PER_ROUND = ["fT", "fN", "dd", "nf", "v2", "oj", "orp", "sv", "so", "V", "da", "Z", "zF", "Zb"]
PAIRS = [("oj", "orp")]
SEMAPHORES = (["qV", "qS", "qP", "qG", "sent", "bulk", "iT", "iZ", "iC", "fZ", "bk0", "bk1", "bk2", "bk3"]
              + ["%s%d" % (m, r) for m in PER_ROUND for r in range(RO)]
              + ["d%d" % i for i in range(12)])
PASSES, PARTS, PADS, SLOW, ORDER_END = 3, (0.33, 0.5, 0.7), (0.0, 20.0, 40.0, 60.0), 700.0, []
ORDER, SENDS = [], []


def messages(T):
    m = {"iT": (SB, T.Th[:], T.Tc[:, 0:L], 0), "iZ": (SB, T.Zs[:], T.Zc[:, 0:L], 1), "iC": (SB, T.Cs[:], T.Ch[:], 1),
         "fZ": (SC - SB, T.Zc[:, 0:L], T.Zj[:, 0:L], 1),
         }
    for n in range(4):
        m["bk%d" % n] = (1, T.X[:, n * Q:(n + 1) * Q], T.XR[:, n * Q:(n + 1) * Q], 2 + n)
    for r in range(RO):
        last = r == RO - 1
        ex = (-SC if last else SB - SC) % N
        s = lambda n: slice(r * n, (r + 1) * n)
        m["fT%d" % r] = (SC - SB, T.Tk[:, s(L)], T.Tj[:, s(L)], 1)
        m["fN%d" % r] = (SC - SB, T.Tn[:, s(256)], T.TD[:, s(256)], LANE["fN"])
        m["dd%d" % r] = (SC - SB, T.DDs[:, s(L)], T.DD[:, s(L)], LANE["dd"])
        m["nf%d" % r] = (SC - SB, T.NFs[:, s(L)], T.NF[:, s(L)], 1)
        m["oj%d" % r] = (SC - SB, T.Ous[:, s(8)], T.Oj[:, s(8)], 1)
        m["V%d" % r] = (ex, T.Vs[:, s(L)], T.Vl[:, s(L)], 0)
        m["da%d" % r] = (ex, T.DAs[:, s(256)], T.DA[:, s(256)], 1)
        zn = (r + 1) * ZW
        if last:
            m["Z%d" % r] = (ex, T.Zj[:, zn:zn + L], T.Zh[:, ZW:ZW + L], 0)
        else:
            m["Z%d" % r] = (ex, T.Zj[:, zn + ZT:zn + ZW], T.Zc[:, zn + ZT:zn + ZW], 0)
            m["zF%d" % r] = (ex, T.Zj[:, zn:zn + ZT], T.Zc[:, zn:zn + ZT], LANE["zF"])
            m["v2%d" % r] = (1, T.V2s[:, s(L)], T.V2[:, s(L)], 1)
            m["orp%d" % r] = (1, T.Ous[:, s(8)], T.Orp[:, s(8)], 1)
            m["sv%d" % r] = (1, T.SVs[:, s(256)], T.SV[:, s(256)], 1)
            m["so%d" % r] = (1, T.SOs[:, s(8)], T.SO[:, s(8)], 0)
        if r == RO - 2:
            m["Zb%d" % r] = (-SC % N, T.Zj[:, zn:zn + ZW], T.Zh[:, 0:ZW], LANE["Zb"])
    return m


def first_hop(T, topo, rank, step, lane):
    src, dst = T.cores[rank], T.cores[(rank + step) % N]
    if lane < 2 and topo.may_write(src, dst):
        return dst
    able = [c for c in topo.cores_of(src) if c != src and all(topo.may_write(c, d) for d in T.cores)]
    near = [c for c in able if topo.die(c) == topo.die(src)]
    far = [c for c in able if topo.die(c) != topo.die(src)]
    return (near + far + near)[lane]


def small_mask(topo, src, dst, name):
    e = topo.engines(src, dst)
    if name[:2] in LATE_ENGINES and name not in ("bk2", "bk3"):
        e = e[-8:]
    elif name[0] in "ib":
        e = e[:8]
    return sum(1 << x for x in e), len(e)


def first_mask(T, topo, msgs, rank, name):
    src, to = T.cores[rank], first_hop(T, topo, rank, msgs[name][0], msgs[name][3])
    for a, b in PAIRS:
        if name[:-1] in (a, b) and a + name[-1] in msgs and b + name[-1] in msgs:
            ea, eb = (topo.engines(src, first_hop(T, topo, rank, msgs[x][0], msgs[x][3])) for x in (a + name[-1], b + name[-1]))
            eb = [x for x in eb if x not in ea]
            if not eb:
                ea, eb = ea[:len(ea) // 2], ea[len(ea) // 2:]
            e = ea if name[:-1] == a else eb
            return sum(1 << x for x in e), len(e)
    return small_mask(topo, src, to, name)


def helper_program(g, core, T, topo):
    sent = 0
    for rank in range(N):
        if core not in topo.cores_of(T.cores[rank]):
            continue
        msgs = messages(T)
        if not SENDS:
            lay_out(record(None, T.cores[rank], T, topo)[0])
        for name in SENDS:
            step, _, land, lane = msgs[name]
            if first_hop(T, topo, rank, step, lane) != core:
                continue
            dst = T.cores[(rank + step) % N]
            g.wait_ge(T.sem[name], first_mask(T, topo, msgs, rank, name)[1])
            mask, n = small_mask(topo, core, dst, name)
            rid, pid = topo.addr(dst, core)
            g.remote_dma(land, land, T.sem[name], T.sem.sent, pid, rid, mask)
            sent += n
    if sent:
        g.wait_ge(T.sem.sent, sent)


def lay_out(ops):
    if ORDER:
        return ORDER
    n = len(ops)
    after = [[] for _ in ops]
    before = [dict(o["soft"]) for o in ops]
    for i, o in enumerate(ops):
        for d in o["deps"]:
            before[i][d] = max(before[i].get(d, 0), ops[d]["lat"])
        for d, lat in before[i].items():
            after[d].append((i, lat))
    left = [len(b) for b in before]
    flow = [i for i in range(n) if not left[i]]
    for i in flow:
        for j, _ in after[i]:
            left[j] -= 1
            if not left[j]:
                flow.append(j)
    assert len(flow) == n
    pos = {i: k for k, i in enumerate(flow)}

    def place(turn, nxt, part, cost):
        at, busy, end = [0.0] * n, {}, [0.0] * n
        for i in turn:
            t, c, line = at[i], cost[i], busy.setdefault(ops[i]["q"], [])
            k = 0
            if ops[i]["q"] != "X":
                while k < len(line) and (line[k][0] <= t or line[k][0] < t + c - min(GIVE, c * part)):
                    t = max(t, line[k][1])
                    k += 1
                line.insert(k, (t, t + c))
            end[i] = t + c
            for j, lat in nxt[i]:
                at[j] = max(at[j], t + c + lat)
        return end

    def length(order, slow):
        end, free = [0.0] * n, {}
        for i in order:
            o = ops[i]
            t = max([end[d] + lat for d, lat in back[i]] + [0.0])
            if o["q"] == "X":
                end[i] = t - o["room"] + slow
            else:
                end[i] = free[o["q"]] = max(t, free.get(o["q"], 0.0)) + o["cost"] + (slow / 25 if o["q"] in "VS" else 0.0)
        return max(end)
    back, tried = [list(b.items()) for b in before], []
    for pad, part in [(x, y) for x in PADS for y in PARTS]:
        cost = [o["cost"] + (pad if o["q"] in "VS" else 0.0) for o in ops]
        tail = [0.0] * n
        for i in flow[::-1]:
            tail[i] = cost[i] + max([lat + tail[j] for j, lat in after[i]] + [0.0])
        end = place(sorted(range(n), key=lambda i: (-round(tail[i], 2), pos[i])), after, part, cost)
        for _ in range(PASSES):
            late = place(sorted(range(n), key=lambda i: (-round(end[i], 2), -pos[i])), back, part, cost)
            end = place(sorted(range(n), key=lambda i: (-round(late[i], 2), pos[i])), after, part, cost)
            order = sorted(range(n), key=lambda i: (round(end[i] - cost[i], 2), round(end[i], 2), pos[i]))
            tried.append((length(order, 0.0) + length(order, SLOW), len(tried), order))
    ORDER.extend(min(tried)[2])
    ORDER_END.append(min(tried)[0] / 2)
    SENDS.extend(x for i in ORDER for x in ops[i]["send"] or [])
    return ORDER


def record(g, core, T, topo):
    rank = T.rank_of(core)
    msgs = messages(T)
    ops, lastw, readers, opened, sent_at, tags, stage = [], {}, {}, {}, {}, {}, ["0"]

    def chain(r, q, words):
        found = []
        for x in words.split():
            rr, st = (r + 1, int(x[0]) - 3) if x[0] in "56" else (r, int(x[0]))
            x = tags.get("%d%d%s%s" % (rr, st, q, x[1:].replace("#", str(rr)).replace("$", str(rr + 1))))
            if x is not None:
                found.append(x)
        for a, b in zip(found, found[1:]):
            ops[b]["soft"][a] = 0
    eng = {"V": g.vector, "S": g.scalar, "P": g.tensor, "G": g, "Y": g.sync} if g else {}

    def op(q, fn, r=(), w=(), ext=None, cost=0.0, lat=LINK, send=None, soft=()):
        i, deps, soft = len(ops), set(), dict(soft)
        group = None
        for k in r:
            deps.update(lastw.get(k, []))
            opened.pop(k, None)
            if k[0] == "B":
                deps.update(x for x in readers.get(k, []) if ops[x]["q"] != q)
        for k in w:
            if q == "P" and k in opened:
                group, old = opened[k]
            else:
                old = readers.get(k, []) + lastw.get(k, [])
                opened.pop(k, None)
                lastw[k], readers[k] = [], []
                if q == "P":
                    group = i
                    opened[k] = (group, old)
            for x in old:
                if ops[x]["q"] != q or ops[x]["ext"]:
                    deps.add(x)
                else:
                    soft[x] = 0
            lastw[k].append(i)
        if w:
            tags[stage[0] + q + w[0]] = i
        ops.append({"q": q, "fn": fn, "deps": deps, "soft": soft, "ext": ext, "cost": cost, "lat": lat, "send": send, "group": group,
                    "room": 0.0})
        for k in r:
            if k not in w:
                readers.setdefault(k, []).append(i)

    def arrive(name, keys):
        step, _, land, lane = msgs[name]
        src = (rank - step) % N
        via = first_hop(T, topo, src, step, lane)
        n = (first_mask(T, topo, msgs, src, name) if via == core else small_mask(topo, via, core, name))[1]
        hops = max(1 if first_hop(T, topo, x, step, lane) in T.cores else 2 for x in range(N))
        room = SLACK * ROOM.get(name.rstrip("0123"), 0.0)
        time = hops * (HOP + land.shape[1] + (FIRST if name[0] == "i" else 0)) + LATE_Z * (name == "iZ")
        op("X", None, (), keys, (name, n), lat=0, soft={sent_at[name]: time + room})
        ops[-1]["room"] = room

    total = {"sent": 0, "bulk": 0}

    def send(names, keys):
        parts, loc = [], "bulk" if names[:2] == "bk" else "sent"
        for name in names.split():
            step, src, land, lane = msgs[name]
            mask, n = first_mask(T, topo, msgs, rank, name)
            parts.append((land, src, name, topo.addr(first_hop(T, topo, rank, step, lane), core), mask))
            total[loc] += n
            sent_at[name] = tags[stage[0] + "G" + name] = len(ops)

        def issue():
            if len(parts) == 1:
                land, src, name, (rid, pid), mask = parts[0]
                return g.remote_dma(land, src, T.sem[name], T.sem[loc], pid, rid, mask)
            return g.remote_dma_fused([RemoteDMATransfer(dst_ids=[DstId(rid=rid, pnc=pid)], dma_engine_mask=mask, remote_sem=T.sem[name],
                                                         src=src, dst=land) for land, src, name, (rid, pid), mask in parts],
                                      local_sem=T.sem[loc])
        op("G", issue, keys, (), ("-", 0), ISSUE, send=names.split())

    ndma = [0]

    def dma(q, out, in_, r, w, lat):
        s = "d%d" % ndma[0]
        ndma[0] += 1
        op(q, lambda: eng[q].dma_start(T[out][:] if isinstance(out, str) else out, T[in_][:] if isinstance(in_, str) else in_),
           r, w, (s, 16), 50, lat)

    def view(x):
        return x[0].indirect(x[1]) if isinstance(x, tuple) else x

    def narrow(*xs):
        return all(SCRATCH[x.name][2] in (BF, H, U16) for x in xs)

    def price(fix, out, a, rate):
        if isinstance(out, tuple):
            return 50 + a.shape[1] * SCATTER * CYC
        if isinstance(a, tuple):
            return 50 + out.shape[1] * GATHER * CYC
        return fix + max(64, out.shape[1] * rate) * CYC

    def half_rate(out, *xs):
        return 1.0 if isinstance(out, tuple) or isinstance(xs[0], tuple) or not narrow(out, *xs) else 0.5

    def ts(out, in0, s1, o0, r, w, s2=None, o1=None):
        c = price(FIXV, out, in0, half_rate(out, in0))
        if o1 is None:
            op("V", lambda: g.vector.tensor_scalar(out, view(in0), s1, None, o0), r, w, cost=c)
        else:
            op("V", lambda: g.vector.tensor_scalar(out, view(in0), s1, s2, o0, o1), r, w, cost=c)

    def tt(out, a, b, o, r, w):
        op("V", lambda: g.vector.tensor_tensor(view(out), view(a), b, o), r, w, cost=price(FIXV, out, a, 1.0))

    def cp(out, a, r, w):
        op("V", lambda: g.vector.tensor_copy(view(out), view(a)), r, w, cost=price(FIXV, out, a, half_rate(out, a)))

    def scan(out, d0, d1, o0, o1, r, w):
        op("V", lambda: g.vector.tensor_tensor_scan(out, d0, d1, 0.0, o0, o1), r, w, cost=price(FIXV, out, d0, half_rate(out, d0, d1)))

    def ms(ap, c, w, r=()):
        op("V", lambda: g.vector.memset(ap, c), r, w, cost=price(FIXV, ap, ap, half_rate(ap, ap)))

    def act(out, in_, f, r, w, bias=0.0, scale=1.0, acc=None):
        op("S", lambda: g.scalar.activation(out, view(in_), f, bias=bias, scale=scale, accum_out=acc), r, w, cost=price(FIXS, out, in_, 1.0))

    leads = {}

    def mm(out, lhsT, rhs, r, w, lead=False):
        op("P", lambda first, final: g.tensor.matmul(out, lhsT, rhs, first, final), r, [w],
           cost=FIXP + max(64, rhs.shape[1]) * PEC * (1 if narrow(rhs) else 4))
        mine = leads.setdefault(ops[-1]["group"], [])
        if lead:
            mine.append(len(ops) - 1)
        else:
            ops[-1]["soft"].update({x: 0 for x in mine})

    def iota(out, pat, w, base=0, step=0):
        op("G", lambda: g.iota(out, pat, base, step, allow_small_or_imprecise_dtypes=True), (), w, cost=130 + 2 * CYC * out.shape[1])

    def cols(name, a, b):
        return ["%s%d" % (name, x) for x in range(a // 64, (b - 1) // 64 + 1)]

    ID, RELU, SIGN, ABS = ACT.Identity, ACT.Relu, ACT.Sign, ACT.Abs
    Xl, Xw, XRl, XRw = T.X[:, 0:W], T.X[:], T.XR[:, 0:W], T.XR[:]
    XK = ["X", "Xz", "Xd"]

    dma("S", T.tr32[:], "traj", (), ["tr32"], LOAD)
    dma("Y", T.Zs[:], "amt", (), ["zs"], LOAD)
    dma("Y", T.cap32[:], "cap", (), ["cap32"], LOAD)
    dma("S", T.X[:, 0:W], "sect", (), ["X"], 2 * LOAD)
    stage[0] = "01"
    op("G", lambda: g.iota(T.pi[:, 0:1], [[0, 1]], 0, 1), (), ["pi0"], cost=130)
    op("G", lambda: g.iota(T.pi[:, 8:9], [[0, 1]], 0, 16), (), ["pi8"], cost=130)
    iota(T.lc[:], [[64, 2], [1, 16], [16, 4]], ["lc"])
    iota(T.xr[:], [[1, 144]], ["xr"])
    iota(T.x8[:, 0:8], [[64, 2], [4, 4]], ["x8a"])
    iota(T.x8[:, 8:16], [[1, 8]], ["x8b"], 0, 4)
    iota(T.x8[:, 16:24], [[64, 2], [1, 4]], ["x8c"])
    iota(T.xq[:], [[16, 8], [0, 16]], ["xq"])
    iota(T.xm[:], [[1, 16], [0, 8]], ["xm"])
    iota(T.lx[:], [[1, 16], [16, 8]], ["lx"])
    iota(T.xk[:], [[0, 8], [1, 16]], ["xk"])
    ms(T.ones[:], 1.0, ["ones"])
    ms(T.X[:, W:XW], 0.0, ["Xz", "Xd"])
    iota(T.XR[:, W:XW], [[0, XW - W]], ["XRd"])
    ms(T.C15[:], 1.0, ["C15"])
    ms(T.C15[:, 15::16], 0.0, ["C15"], ["C15"])
    ms(T.FB[:, 0:8], 0.0, ["FB"])
    ms(T.F6[:], 6.0, ["F6"])
    ms(T.c4k[:], 4096.0, ["c4k"])
    ms(T.fc[:, 8:9], -0.5, ["fb0"])
    ms(T.fc[:, 9:10], -8.5, ["fb1"])
    iota(T.TK[:], [[0, 256]], ["TK0", "TK1"])
    iota(T.AP2[:], [[0, 256]], ["AP0", "ap"])
    ms(T.onS[:], 0.0, ["onS"])
    for n in range(2):
        for a, b in STEP4[n][0]:
            ms(T.onS[:, L * n + a // 16:L * n + b // 16], 1.0, ["onS"], ["onS"])
    for n in range(1, RO):
        iota(T.Zj[:, n * ZW + L:n * ZW + ZT], [[0, 16]], ["zjF%d" % n])
    ts(T.pi[:, 1:2], T.pi[:, 0:1], 15, ALU.bitwise_and, ["pi0"], ["pi1"])
    ts(T.pi[:, 2:3], T.pi[:, 0:1], 112, ALU.bitwise_and, ["pi0"], ["pi2"])
    ts(T.pi[:, 3:4], T.pi[:, 0:1], 7, ALU.bitwise_and, ["pi0"], ["pi3"])
    ts(T.pi[:, 4:5], T.pi[:, 0:1], 3, ALU.logical_shift_right, ["pi0"], ["pi4"])
    ts(T.pi[:, 5:6], T.pi[:, 0:1], 3, ALU.logical_shift_right, ["pi0"], ["pi5"], 1, ALU.bitwise_and)
    ts(T.pi[:, 6:7], T.pi[:, 0:1], 2, ALU.logical_shift_right, ["pi0"], ["pi6"], 3, ALU.bitwise_and)
    ts(T.pi[:, 7:8], T.pi[:, 8:9], 48, ALU.bitwise_and, ["pi8"], ["pi7"])
    cp(T.pf[:, 0:6], T.pi[:, 0:6], ["pi%d" % i for i in range(6)], ["pf"])
    cp(T.pf[:, 6:8], T.pi[:, 6:8], ["pi6", "pi7"], ["pq"])
    pc, kc, gc_, a8, p8, p1, p4, p3 = (T.pf[:, i:i + 1] for i in range(8))
    ts(T.idc[:], T.lc[:], pc, ALU.is_equal, ["lc", "pf"], ["idc"])
    ts(T.idb[:], T.xr[:, 0:L], pc, ALU.is_equal, ["xr", "pf"], ["idb"])
    tt(T.pf[:, 8:9], p3, p4, ALU.add, ["pq"], ["pf8"])
    ts(T.pf[:, 9:10], a8, 16.0, ALU.mult, ["pf"], ["pf9"], 15.0, ALU.add)
    ts(T.pf[:, 10:11], a8, 16.0, ALU.mult, ["pf"], ["pf10"], p8, ALU.add)
    ts(T.pf[:, 11:12], kc, -1.0, ALU.mult, ["pf"], ["pf11"], 24.0, ALU.add)
    ts(T.pf[:, 12:13], kc, 2.0, ALU.mult, ["pf"], ["pf12"], float(SP), ALU.add)
    ts(T.pf[:, 13:14], kc, float(W), ALU.add, ["pf"], ["pf13"])
    ts(T.pf[:, 14:15], T.pf[:, 8:9], 2.0, ALU.mult, ["pf8"], ["pf14"], 1.0, ALU.add)
    ts(T.pf[:, 15:16], kc, 4.0, ALU.mult, ["pf"], ["pf15"])
    ts(T.cP0[:], T.x8[:, 0:8], p3, ALU.add, ["x8a", "pq"], ["cP0"], p4, ALU.add)
    ts(T.cIn[:], T.x8[:, 16:24], T.pf[:, 15:16], ALU.add, ["x8c", "pf15"], ["cIn"])
    cp(T.Th[:], (T.tr32[:], T.cP0[:]), ["tr32", "cP0"], ["Th"])
    send("iT", ["Th"])
    send("iZ", ["zs"])
    ms(T.Cs[:], 0.0, ["cs"])
    ts(T.Cs[:, 0:1], T.cap32[:], -200.0, ALU.add, ["cap32", "cs"], ["cs"])
    send("iC", ["cs"])
    for n in range(4):
        send("bk%d" % n, ["X"])
    op("X", None, (), ["Xsent"], ("bulk", total["bulk"]), lat=0, soft={sent_at["bk%d" % n]: 3000 for n in range(4)})
    arrive("iT", ["tc00", "tc01"])
    arrive("iZ", ["zc0"])
    arrive("iC", ["caph"])
    send("fZ", ["zc0"])
    arrive("fZ", ["zj0"])
    for n in range(4):
        arrive("bk%d" % n, ["XR%d" % n])
    dma("Y", T.mv32[:], "mv", ["zc0"], ["mv32"], 2 * LOAD)
    cp(T.man[:, 0:Q], T.mv32[:], ["mv32"], ["man0"])
    for i in range(1, W // Q):
        act(T.man[:, i * Q:(i + 1) * Q], T.man[:, 0:Q], ID, ["man0"], ["man%d" % i])
    MAN = ["man%d" % i for i in range(W // Q)]
    ts(T.WB[:], T.xr[:], -15.0, ALU.add, ["xr", "pf"], ["WB"], gc_, ALU.is_equal)
    for k in range(16):
        if k % 2:
            act(T.ECp[:, k::16], T.idc[:], ID, ["idc"], ["ECp%d" % k])
        else:
            cp(T.ECp[:, k::16], T.idc[:], ["idc"], ["ECp%d" % k])
        act(T.ECn[:, k::16], T.idb[:, S0 // 16:L], ID, ["idb"], ["ECn%d" % k])
    ECP = ["ECp%d" % k for k in range(16)]
    ECN = ["ECn%d" % k for k in range(16)]
    ts(T.capf[:, 0:1], T.cap32[:], -1.0, ALU.mult, ["cap32"], ["capb"], 150.0, ALU.add)
    ts(T.capf[:, 1:2], T.cap32[:], 1.0, ALU.add, ["cap32"], ["capp"])
    ts(T.capf[:, 2:3], T.cap32[:], 0.0, ALU.add, ["cap32"], ["capo"])
    act(T.capf[:, 3:4], T.Ch[:, 0:1], ID, ["caph"], ["capH"], bias=200.0)
    act(T.capf[:, 4:5], T.Ch[:, 0:1], ID, ["caph"], ["capJ"], bias=-50.0, scale=-1.0)
    x8 = T.xr[:, 0:8]
    ts(T.cP1[:], x8, 8.0, ALU.mult, ["xr", "pf14"], ["cP1"], T.pf[:, 14:15], ALU.add)
    cp(T.cTm[:], T.x8[:, 8:16], ["x8b"], ["cTm"])
    ts(T.cPA[:], x8, 0.0, ALU.mult, ["xr", "pf9"], ["cPA"], T.pf[:, 9:10], ALU.add)
    ts(T.cEx[:], x8, 16.0, ALU.mult, ["xr"], ["cEx"], 15.0, ALU.add)
    ts(T.Dm[:, 0:16], T.xr[:, 0:16], kc, ALU.is_equal, ["xr", "pf"], ["Dm"])
    ts(T.Dm[:, 16:32], T.xr[:, 1:17], kc, ALU.is_equal, ["xr", "pf"], ["Dm2"])
    tt(T.Dm[:, 0:16], T.Dm[:, 0:16], T.Dm[:, 16:32], ALU.subtract, ["Dm", "Dm2"], ["Dm"])
    dum, dumz = T.dum[:, 0:8], T.dum[:, 8:16]
    ts(dum, x8, 32.0, ALU.mult, ["xr", "pf12"], ["dum"], T.pf[:, 12:13], ALU.add)
    ts(dumz, x8, 16.0, ALU.mult, ["xr", "pf13"], ["dumz"], T.pf[:, 13:14], ALU.add)
    ts(T.BO[:], T.xq[:], gc_, ALU.is_equal, ["xq", "pf"], ["cBO"])
    ts(T.mA[:], T.xm[:], kc, ALU.is_equal, ["xm", "pf"], ["mA"])
    ts(T.mK[:, 0:L], T.xk[:], kc, ALU.is_equal, ["xk", "pf"], ["mK0"], -0.5, ALU.mult)
    ts(T.mK[:, L:2 * L], T.mK[:, 0:L], -32.0, ALU.mult, ["mK0"], ["mK"])
    ts(T.TRI[:], T.lx[:], T.pf[:, 10:11], ALU.is_le, ["lx", "pf10"], ["TRI"], 4096.0, ALU.mult)
    for gg in range(8):
        ts(T.SEL[:, gg * L:(gg + 1) * L], T.ones[:], T.BO[:, 16 * gg:16 * gg + 1], ALU.mult, ["ones", "cBO"], ["SEL%d" % gg])
    SELK = ["SEL%d" % gg for gg in range(8)]
    ts(T.NSEL[:, 0:1024 - RUNS[-1][0] * L], T.SEL[:, RUNS[-1][0] * L:1024], -1.0, ALU.mult, SELK, ["NSEL"])
    ts(T.pf[:, 16:17], a8, 16.0, ALU.mult, ["pf"], ["pf16"], p1, ALU.add)
    ts(T.cP3[:, 0:8], T.xr[:, 0:16:2], T.pf[:, 16:17], ALU.add, ["xr", "pf16"], ["cP3"])
    ts(T.pf[:, 17:18], T.pf[:, 16:17], 2.0, ALU.mult, ["pf16"], ["pf17"], 1.0, ALU.add)
    ts(T.cP3[:, 8:16], T.xr[:, 0:32:4], T.pf[:, 17:18], ALU.add, ["xr", "pf17"], ["cP4"])
    ts(T.rst[:], T.xk[:], 0.0, ALU.is_gt, ["xk"], ["rst"])
    ts(T.cMx[:], T.xk[:], 0.0, ALU.is_gt, ["xk"], ["cMx"], 17000000.0, ALU.mult)
    ts(T.cMx[:], T.cMx[:], -1000000.0, ALU.add, ["cMx"], ["cMx"])
    for h in range(2):
        ts(T.spT[:, h::2], T.xq[:], 2.0, ALU.mult, ["xq", "pf12"], ["spT%d" % h], T.pf[:, 12:13], ALU.add)
    ms(T.spT[:, 0::32], 0.0, ["spT"], ["spT0", "spT1"])
    ts(T.k0[:], T.xk[:], 0.0, ALU.is_equal, ["xk"], ["k0"])
    ts(T.capf[:, 5:6], T.cap32[:], -150.0, ALU.add, ["cap32"], ["capd"])
    act(T.Tm[:], T.ECp[:, 0:1024], ID, ECP, ["Tm0", "Tm1"], scale=0.0)
    for buf, c in ((T.idf, 1.0), (T.idp, 2048.0), (T.idq, -2048.0), (T.idu, UNIT), (T.id4, 4.0), (T.id5, 5.0), (T.id6, -6.0)):
        act(buf[:], T.idb[:], ID, ["idb"], [buf.name], scale=c)
    act(T.WS[:], T.WB[:], ID, ["WB"], ["WS"], scale=0.25)

    def wband(buf, k):
        return buf[:, 15 - k:143 - k]

    def dpos(gg, n=1):
        a, _, bk = [x for x in RUNS if x[0] <= gg < x[1]][0]
        c = 512 * (bk % 4) + (gg - a) * L
        return (T.PT, T.PD)[bk // 4][:, c:c + n * L], "B%d" % bk
    runs = [x[:2] for x in RUNS]
    EQK = ["eq%d" % n for n in range(8)]
    TH, TH4 = (["%s%d" % (x, k) for k in range(16)] for x in ("th", "tf"))

    def pieces(out, src, sk, keys, ng):
        n = src.shape[1]
        for k in range(16):
            if k < ng:
                op("G", lambda o=out[:, k::16]: g.affine_select(o, src, [[0, n]], ALU.is_ge, 0.0, 0, 0), [sk], [keys[k]],
                   cost=170 + 2 * CYC * n)
            else:
                act(out[:, k::16], src, ID, [sk], [keys[k]])

    def bank2(a, b):
        c = (a + 1024) % W
        return T.PT[:, c:c + b - a], "B%d" % (c // 512)

    def spread(lhs, lk, pieces):
        for n, (a, b) in enumerate(pieces):
            mm(T.PT[:, 512 * n:512 * n + b - a], lhs, T.ECn[:, a - S0:b - S0], [lk] + ECN, "B%d" % n, True)

    stage[0] = "02"
    cp(T.hp[:, 0:L], T.Tc[:, 0:L], ["tc00", "tc01"], ["hp"])
    ms(T.Tn[:, 0:256:2], 0.0, ["Tne"])
    cp(T.Tn[:, 1:256:2], (T.hp[:, 0:L], T.cIn[:]), ["hp", "cIn", "Tne"], ["Tn00", "Tn01"])
    mm(T.P7[:, 0:L], T.Zc[:, 0:L], T.idb[:], ["zc0", "idb"], "B7")
    ts(T.Zc[:, ZT:ZR], T.P7[:, 0:L], -150.0, ALU.add, ["B7"], ["zt0"])

    def raised(win, wk, off, ok, z, zk, ps, bk, val, vk, tag, low=None, lk="low"):
        a1, old, u = (T["up" + tag][:, n * L:(n + 1) * L] for n in range(3))
        act(a1, z, ID, [zk], ["a1" + tag], bias=128.625, scale=0.25)
        if tag in ONV:
            mn = low if low is not None else u
            act(old, a1, ID, ["a1" + tag], ["old" + tag], bias=384.0, scale=-1.0)
            tt(mn, (win, off), old, ALU.min, wk + [ok, "old" + tag], [lk])
            act(val, a1, ID, ["a1" + tag], [vk], bias=-129.0)
            return a1, u
        act(old, (win, off), ID, wk + [ok], ["old" + tag])
        mm(ps, T.idb[:], a1, ["idb", "a1" + tag], bk)
        mm(ps, T.idb[:], old, ["idb", "old" + tag], bk)
        act(u, ps, RELU, [bk], ["u" + tag], bias=384.0, scale=-1.0)
        act(val, u, ID, ["u" + tag], [vk], bias=255.0, scale=-1.0)
        return a1, u

    for r in range(RO):
        last = r == RO - 1
        s = lambda n: slice(r * n, (r + 1) * n)
        rs, ns, zn = str(r), str(r + 1), (r + 1) * ZW
        tjk = "tj" + rs
        zc, zck = T.Zc[:, r * ZW:r * ZW + L], "zc" + rs
        zt, ztk = T.Zc[:, r * ZW + ZT:r * ZW + ZR], "zt" + rs
        zj, zjk = T.Zj[:, r * ZW:r * ZW + L], "zj" + rs
        Fc, Fck = (T.F6[:, 0:1], "F6") if r == 0 else (T.Zc[:, r * ZW + L:r * ZW + L + 1], zck)
        Fj, Fjk = (T.F6[:, 0:1], "F6") if r == 0 else (T.Zj[:, r * ZW + L:r * ZW + L + 1], "zjF" + rs)
        mn3, val3 = T.SVs[:, r * 256:r * 256 + L], T.SVs[:, r * 256 + L:r * 256 + 256]
        stage[0] = rs + "2"
        cp(T.Tk[:, s(L)], (T.Tn[:, s(256)], T.cP3[:, 8:16]), ["Tn%d0" % r, "Tn%d1" % r, "cP4"], ["tk" + rs])
        send("fT" + rs, ["tk" + rs])
        arrive("fT" + rs, [tjk])
        send("fN" + rs, ["Tn%d0" % r, "Tn%d1" % r])
        arrive("fN" + rs, ["Tf" + rs])
        Tf, dT, TD = T.TD[:, r * 256 + 1:r * 256 + 256:2], T.TD[:, r * 256:r * 256 + 256:2], T.TD[:, s(256)]
        for h in range(2):
            tmk, c0 = "Tm%d" % h, r * 256 + 128 * h
            cp((T.Tm[:, 512 * h:512 * h + 512], T.cTm[:, 0:4]), T.Tn[:, c0 + 1:c0 + 128:2], ["Tn%d%d" % (r, h), "cTm", tmk], [tmk])
            for lam in range(4):
                mm(T.P7[:, 64 * h + 16 * lam:64 * h + 16 * lam + 16], T.Tm[:, 512 * h + lam:512 * h + 512:4], T.Dm[:, 0:16], [tmk, "Dm"], "B7")
        words = [(x[0],) + tuple(int(y) for y in x[1:].split(":")) for x in (NEXT2 if r else FIRST2).split()]
        banks = {"D": [4, 5], "S": [2, 3, 0, 1]}
        for e, a, b in words:
            n = banks["D" if e == "D" else "S"].pop(0)
            o, bk = (T.PT, T.PD)[n // 4][:, 512 * (n % 4):512 * (n % 4) + b - a], "B%d" % n
            src = (Xl, T.Tc[:, r * L + a // 16:r * L + b // 16])
            rk = ["X", "capb", "tc%d%d" % (r, a // 1024), "tc%d%d" % (r, (b - 1) // 1024)]
            mm(o, zt, T.ECp[:, a:b], [ztk] + ECP, bk)
            if e == "D":
                act(T.th[:, 2 * W + a:2 * W + b], o, ID, [bk, "capd"], cols("td", a, b), bias=T.capf[:, 5:6], scale=-1.0)
                tt(T.bb[:, a:b], src, T.th[:, 2 * W + a:2 * W + b], ALU.is_gt, rk + cols("td", a, b), cols("bb", a, b))
                scan(T.bo[:, a:b], T.bb[:, a:b], T.C15[:, 0:b - a], ALU.max, ALU.min, cols("bb", a, b) + ["C15"], cols("bo", a, b))
                continue
            if e == "V":
                ts(T.xs[:, a:b], src, T.capf[:, 0:1], ALU.add, rk, cols("xs", a, b))
            else:
                act(T.xs[:, a:b], src, ID, rk, cols("xs", a, b), bias=T.capf[:, 0:1])
            mm(o, T.idb[:], T.xs[:, a:b], ["idb"] + cols("xs", a, b), bk)
            scan(T.bo[:, a:b], o, T.C15[:, 0:b - a], ALU.max, ALU.min, [bk, "C15"], cols("bo", a, b))
        for u in range(32):
            mm(T.P6[:, 64 * (u // 16):64 * (u // 16) + 64], wband(T.WB, u % 16), T.bo[:, 64 * u:64 * u + 64], ["WB", "bo%d" % u], "B6")
        act(T.fc[:, 0:2], T.fc[:, 8:10], ID, [Fck, "fb0", "fb1"], ["fc0"], bias=Fc)
        if r == 1:
            cp((XRw, T.SO[:, 0:8]), T.SV[:, 0:L], ["so0", "sv0", "XR"], ["XR"])
        ts(T.FB[:, 1:129], T.P6[:, 0:L], Fc, ALU.is_ge, ["B6", Fck, "FB"], ["FB"])
        act(T.NFs[:, s(L)], T.P6[:, 0:L], SIGN, ["B6", "fc0"], ["nfs" + rs], bias=T.fc[:, 0:1], scale=-1.0)
        scan(T.ys[:], T.FB[:, 0:L], T.P7[:, 0:L], ALU.mult, ALU.add, ["FB", "B7"], ["ys"])
        act(T.DDs[:, s(L)], T.P7[:, 0:L], ID, ["B7"], ["dds" + rs])
        send("dd" + rs, ["dds" + rs])
        act(T.X[:, W:SP], zj, ID, [zjk], ["Xz"])
        tt(T.PA[:], (T.ys[:], T.cPA[:]), T.mA[:], ALU.mult, ["ys", "cPA", "mA"], ["PA"])
        cp(T.Pu[:], T.ys[:, 15::16], ["ys"], ["Pu"])
        raised(Xl, ["X"], T.Pu[:], "Pu", zc, zck, T.P6[:, 0:L], "B6", T.V2s[:, s(L)], "v2s" + rs, "c")
        mm(T.P7[:, 0:8], T.PA[:], T.SEL[:, 0::L], SELK + ["PA"], "B7")
        for n, (a, b) in enumerate(runs):
            for gg in range(a, b):
                o, bk = dpos(gg)
                mm(o, T.idb[:], T.TRI[:], ["idb", "TRI"] + cols("bo", TRI_AT, TRI_AT + 64), bk, True)
            for gg in range(a, b):
                o, bk = dpos(gg)
                mm(o, T.SEL[:, gg * L:(gg + 1) * L], T.PA[:], SELK + ["PA"], bk)
            if n < len(runs) - 1:
                for gg in range(a, b):
                    ts(T.eq[:, gg * L:(gg + 1) * L], dpos(gg)[0], T.P7[:, gg:gg + 1], ALU.is_equal, [bk, "B7"], [EQK[gg]])
            else:
                o, bk = dpos(a, b - a)
                mm(o, T.PA[:], T.NSEL[:, 0:(b - a) * L], ["NSEL", "PA"], bk)
                act(T.ab[:, 0:(b - a) * L], o, ABS, [bk], ["ab"])
                act(T.eq[:, a * L:b * L], T.ab[:, 0:(b - a) * L], RELU, ["ab"], EQK[a:b], bias=1.0, scale=-1.0)
        mm(T.PT[:, 1536:1544], T.idf[:], T.ys[:, 15::16], ["idf", "ys"], "B3", True)
        for c in range(8):
            mm(T.PT[:, 1536 + c:1537 + c], T.eq[:, c::8], T.c4k[:, 0:1], EQK + ["c4k"], "B3")
        tt(T.Ofs[:, 0:8], T.PT[:, 1536:1544], dum, ALU.min, ["B3", "dum"], ["ofs"])
        cp(T.Ous[:, s(8)], T.Ofs[:, 0:8], ["ofs"], ["ous" + rs])
        cp((Xw, T.Ous[:, s(8)]), T.V2s[:, s(L)], ["ous" + rs, "v2s" + rs, "Xsent"] + XK, XK)
        send("oj" + rs + (" orp" + rs) * (not last), ["ous" + rs])
        mm(T.PT[:, 0:L], T.idp[:], T.bo[:, 14::16], ["idp"] + cols("bo", 0, W), "B0", True)
        spans = []
        for e, a, b in sorted(words, key=lambda x: x[1]):
            if spans and spans[-1][0] == (e == "D"):
                spans[-1][2] = b
            else:
                spans.append([e == "D", a, b])
        for direct, a, b in spans:
            o = T.PT[:, a // 16:b // 16]
            if direct:
                mm(o, T.idp[:], T.bb[:, a + 15:b:16], ["idp"] + cols("bb", a, b), "B0")
            else:
                mm(o, T.idb[:], T.xs[:, a + 15:b:16], ["idb"] + cols("xs", a, b), "B0")
                mm(o, zt, T.idc[:, a // 16:b // 16], [ztk, "idc"], "B0")
        for h in range(2):
            act(T.s15[:, h::2], T.PT[:, 64 * h:64 * h + 64], SIGN, ["B0"], ["s15%d" % h], bias=-0.5)
        for mu in range(16):
            mm(T.PT[:, 512:520], wband(T.WB, mu), T.s15[:, 8 * mu:8 * mu + 8], ["WB", "s150", "s151"], "B1")
        for h in range(2):
            act(T.NFs[:, r * L + 64 * h + 15:r * L + 64 * h + 64:16], T.PT[:, 512 + h:520:2], SIGN,
                ["B1", "fc0", "nfs" + rs], ["nf%s%d" % (rs, h)], bias=T.fc[:, 1:2], scale=-0.5)
        send("nf" + rs, ["nfs" + rs, "nf%s0" % rs, "nf%s1" % rs])
        if not last:
            send("v2" + rs, ["v2s" + rs])
        for nm in ("dd", "nf", "oj"):
            arrive(nm + rs, [nm + rs])
        stage[0] = rs + "3"
        NF = T.NF[:, s(L)]
        v3 = S3[0][0]
        act(T.t3[:, 0:L], (zj, T.cP3[:, 0:8]), RELU, [zjk, "cP3", "capp"], ["t3"], bias=T.capf[:, 1:2], scale=-1.0)
        mm(T.P7[:, L:2 * L], T.t3[:, 0:L], T.idb[:], ["t3", "idb"], "B7")
        act(T.t3T[:], T.P7[:, L:2 * L], ID, ["B7"], ["t3T"], scale=-1.0)
        spread(T.t3T[:], "t3T", S3)
        pieces(T.th[:, 0:v3], T.t3[:, 0:v3 // 16], "t3", TH, G3[r])
        mm(T.PD[:, 0:L], T.BO[:], zj, ["cBO", zjk], "B4")
        mm(T.PD[:, 0:L], T.id5[:], Tf, ["id5", "Tf" + rs], "B4")
        act(T.qq[:], T.PD[:, 0:L], ID, ["B4"], ["qq"], bias=128.500732421875, scale=1.0 / 2048)
        mm(T.PD[:, 512:640], T.BO[:], zj, ["cBO", zjk], "B5")
        mm(T.PD[:, 512:640], T.id4[:], Tf, ["id4", "Tf" + rs], "B5")
        mm(T.PD[:, 512:640], T.idq[:], T.qq[:], ["idq", "qq"], "B5")
        act(dT, T.PD[:, 512:640], ID, ["B5", "Tf" + rs], ["dT"], bias=264193.0)
        a1, u = raised(Xw, XK, T.Oj[:, s(8)], "oj" + rs, zj, zjk, T.PD[:, 0:L], "B4", val3, "val3" + rs, "j", mn3, "mn3" + rs)
        if not last and "j" not in ONV:
            mm(T.PD[:, 0:L], T.idb[:], a1, ["idb", "a1j"], "B4")
            mm(T.PD[:, 0:L], T.idb[:], u, ["idb", "uj"], "B4")
            act(mn3, T.PD[:, 0:L], ID, ["B4"], ["mn3" + rs], bias=384.0, scale=-1.0)
        cp(T.Ofs[:, 8:16], T.Oj[:, s(8)], ["oj" + rs], ["of"])
        mm(T.P6[:, 1:256:2], T.idp[:], T.k0[:], ["idp", "k0"], "B6", True)
        mm(T.P6[:, 1:256:32], T.idf[:], T.Ofs[:, 8:16], ["idf", "of"], "B6")
        mm(T.P6[:, 1:256:32], T.idp[:], T.NF[:, r * L + 15:(r + 1) * L:16], ["idp", "nf" + rs], "B6")
        act(T.fc[:, 3:4], Fj, ID, [Fjk], ["fc3"], bias=-5.0, scale=-1.0)
        act(T.NFm[:], T.idb[:], ID, ["idb", "fc3"], ["NFm"], scale=T.fc[:, 3:4])
        mm(T.PT[:, 1536:1664], T.ones[:], T.NFm[:], ["ones", "NFm"], "B3", True)
        mm(T.PT[:, 1536:1664], NF, T.id6[:], ["id6", "nf" + rs], "B3")
        tail_of = {}
        for word in ORD3.split():
            n = int(word[3])
            a, b = (V3 if word[2] == "v" else S3)[n]
            src, o = (Xl, T.Tj[:, r * L + a // 16:r * L + b // 16]), T.PT[:, 512 * n:512 * n + b - a]
            xs, bo, bb = cols("xs", a, b), cols("bo", a, b), cols("bb", a, b)
            if word[:3] == "Vgv":
                tt(T.xs[:, a:b], src, T.th[:, a:b], ALU.subtract, ["X", tjk] + TH, xs)
            elif word[:3] == "Sgs":
                act(T.xs[:, a:b], src, ID, ["X", tjk], xs)
            elif word[:3] == "Sev":
                act(T.bo[:, a:b], T.xs[:, a:b], RELU, xs, bo, bias=1.0)
            elif word[:3] == "Vev":
                ts(T.bo[:, a:b], T.xs[:, a:b], 1.0, ALU.add, xs, bo, 0.0, ALU.max)
            elif word[:3] == "Ses":
                act(T.bo[:, a:b], o, RELU, ["B%d" % n], bo, bias=1.0)
            elif word[:3] == "Vmv":
                ts(T.bb[:, a:b], T.xs[:, a:b], 0.0, ALU.is_ge, xs, bb)
            else:
                ts(T.bb[:, a:b], T.bo[:, a:b], 0.5, ALU.is_ge, bo, bb)
            if word[0] in tail_of:
                ops[-1]["soft"][tail_of[word[0]]] = 0
            tail_of[word[0]] = len(ops) - 1
            if word[:3] == "Sgs":
                mm(o, T.idb[:], T.xs[:, a:b], ["idb"] + xs, "B%d" % n)
        key = T.P7[:, 16:16 + L]
        for mu in range(16):
            c = slice(L * mu, L * mu + L)
            mm(T.PT[:, 1536 + mu:1664:16], T.bb[:, c], T.BO[:, 0::16], ["cBO"] + cols("bb", c.start, c.stop), "B3")
            mm(key, wband(T.WS, mu), T.bo[:, c], ["WS"] + cols("bo", c.start, c.stop), "B7")
        ts(T.ful[:], T.PT[:, 1536:1664], 0.5, ALU.is_ge, ["B3"], ["ful"])
        mm(key, T.ful[:], T.idu[:], ["idu", "ful"], "B7")
        mm(T.P6[:, 0:256:2], T.ful[:], T.idu[:], ["idu", "ful"], "B6")
        scan(T.Es[:], T.spT[:], T.P6[:, 0:256], ALU.min, ALU.max, ["spT", "B6"], ["Es"])
        cp(T.SOs[:, s(8)], T.Es[:, 31::32], ["Es"], ["sos" + rs])
        if not last:
            send("sv" + rs, ["mn3" + rs, "val3" + rs])
            send("so" + rs, ["sos" + rs])
        scan(T.KB[:], T.P7[:, 15:15 + L], T.cMx[:], ALU.max, ALU.min, ["B7", "cMx"], ["KB"])
        tt(T.ng3[:], key, T.KB[:], ALU.is_le, ["KB", "B7"], ["ng3"])
        scan(T.y3[:], T.ng3[:], T.DD[:, s(L)], ALU.mult, ALU.add, ["ng3", "dd" + rs], ["y3"])
        cp(T.Tmu[:], T.y3[:, 15::16], ["y3"], ["Tmu"])
        cp(T.Vs[:, s(L)], (T.man[:], T.Tmu[:]), MAN + ["Tmu"], ["vs" + rs])
        send("V" + rs, ["vs" + rs])
        scan(T.rq[:], T.rst[:], T.P6[:, 0:256:2], ALU.mult, ALU.max, ["rst", "B6"], ["rq"])
        scan(T.js[:], T.rst[:], NF, ALU.mult, ALU.add, ["rst", "nf" + rs], ["js"])
        tt(T.ex[:, 0:L], (T.js[:], T.cEx[:]), T.mK[:, 0:L], ALU.mult, ["js", "cEx", "mK"], ["exj"])
        tt(T.ex[:, L:2 * L], (T.rq[:], T.cEx[:]), T.mK[:, L:2 * L], ALU.min, ["rq", "cEx", "mK"], ["ex"])
        mm(T.PT[:, 1536:1664], T.BO[:], T.ex[:, 0:L], ["cBO", "exj"], "B3")
        mm(T.PT[:, 1536:1664], T.BO[:], T.ex[:, L:2 * L], ["cBO", "ex"], "B3")
        mm(T.PT[:, 1664:1792], T.BO[:], T.ex[:, L:2 * L], ["cBO", "ex"], "B3")
        act(T.AP2[:, 1::2], T.PT[:, 1664:1792], RELU, ["B3"], ["ap", "nn"], bias=1.0, scale=-1.0, acc=T.nn[:, 0:1])
        act(T.Rm[:], T.PT[:, 1536:1664], RELU, ["B3", "pf11"], ["R"], bias=T.pf[:, 11:12], scale=-1.0)
        act(T.PT[:, 1536:1664], T.Rm[:], RELU, ["R"], ["B3"], bias=1.0, scale=-1.0)
        tt(T.ys[:], (T.man[:], T.Tmu[:]), Tf, ALU.subtract, MAN + ["Tmu", "Tf" + rs], ["ys"])
        scan(T.DAs[:, s(256)], T.AP2[:], TD, ALU.mult, ALU.add, ["AP0", "ap", "Tf" + rs, "dT"], ["aa" + rs])
        tt(T.DAs[:, r * 256:(r + 1) * 256:2], T.ys[:], T.PT[:, 1536:1664], ALU.mult, ["ys", "B3", "aa" + rs], ["aa" + rs])
        send("da" + rs, ["aa" + rs])
        tt(T.ww[:, 0:8], dumz, T.rq[:, 15::16], ALU.subtract, ["dumz", "rq"], ["w1"])
        tt(T.ww[:, 8:16], T.ww[:, 0:8], T.y3[:, 15::16], ALU.max, ["w1", "y3"], ["w2"])
        cp(T.Yu[:], T.ww[:, 8:16], ["w2"], ["Yu"])
        act(T.ymp[:], (Xw, T.Yu[:]), ID, XK + ["Yu"], ["ymp"])
        nz = L if last else 2 * L
        for x, xk in ((zj, zjk), (T.ymp[:], "ymp")):
            mm(T.PT[:, 1024:1152], T.idb[:], x, ["idb", xk], "B2")
            if not last:
                mm(T.PT[:, 1152:1280], x, T.idb[:], ["idb", xk], "B2")
        act(T.hp[:, 0:nz], T.PT[:, 1024:1024 + nz], ID, ["B2"], ["hp"], bias=MAGIC, scale=0.4999)
        act(T.Zj[:, zn:zn + L], T.hp[:, 0:L], ID, ["hp"], ["zj" + ns], bias=-MAGIC)
        if last:
            send("Z" + rs, ["zj" + ns])
            tt((Xw, T.SOs[:, s(8)]), mn3, val3, ALU.add, ["sos" + rs, "mn3" + rs, "val3" + rs] + XK, XK)
            dma("Y", "ysect", T.X[:, 0:W], ["X"], ["ysect"], 3000)
        else:
            act(T.nq[:, 0:1], T.nn[:, 0:1], ID, ["nn"], ["nq"], bias=128.75, scale=0.5)
            act(T.nn[:, 1:2], T.nn[:, 0:1], ID, ["nn"], ["nf"], bias=264.0)
            act(T.Zj[:, zn + ZT:zn + ZR], T.hp[:, L:2 * L], ID, ["hp"], ["zjT" + ns], bias=-MAGIC - 150.0)
            act(T.Zj[:, zn + L:zn + L + 1], T.nq[:, 0:1], ID, ["nq", "nf", "zjF" + ns], ["zjF" + ns], bias=T.nn[:, 1:2], scale=-2.0)
            send("Z" + rs, ["zjT" + ns])
            send("zF" + rs, ["zj" + ns, "zjF" + ns])
            if r == RO - 2:
                send("Zb" + rs, ["zj" + ns, "zjF" + ns, "zjT" + ns])
            cp((Xw, T.SOs[:, s(8)]), mn3, ["sos" + rs, "mn3" + rs] + XK, ["net"] + XK)
            for nm in ("v2", "orp", "sv", "so"):
                arrive(nm + rs, [nm + rs])
            for h in range(NXW):
                n = 8 // NXW
                cp((XRw, T.Orp[:, r * 8 + n * h:r * 8 + n * h + n]), T.V2[:, r * L + 16 * n * h:r * L + 16 * n * (h + 1)],
                   ["orp" + rs, "v2" + rs, "XR0", "XR1", "XR2", "XR3", "XRd", "XR"], ["xw%d" % h, "XR"])
            tt((XRw, T.SO[:, s(8)]), T.SV[:, r * 256:r * 256 + L], T.SV[:, r * 256 + L:r * 256 + 256], ALU.add,
               ["so" + rs, "sv" + rs, "XR"], ["XR"])
        if r == RO - 2:
            arrive("Zb" + rs, ["zh0"])
        arrive("V" + rs, ["vl" + rs])
        arrive("da" + rs, ["da" + rs])
        stage[0] = rs + "4"
        if last:
            arrive("Z" + rs, ["zh1"])
            dma("Y", "yamt", T.Zh[:, ZW:ZW + L], ["zh1"], ["yamt"], 1500)
            win, wk = Xl, "X"
            z4, z4k, F4, F4k, zt4, zt4k = T.Zh[:, 0:L], "zh0", T.Zh[:, L:L + 1], "zh0", T.Zh[:, ZT:ZR], "zh0"
            cap4, cap4b, cap4k = T.capf[:, 2:3], T.capf[:, 0:1], ["capo", "capb"]
        else:
            arrive("Z" + rs, ["zt" + ns])
            arrive("zF" + rs, ["zc" + ns])
            win, wk = XRl, "XR"
            z4, z4k, F4, F4k, zt4, zt4k = zc, zck, Fc, Fck, zt, ztk
            cap4, cap4b, cap4k = T.capf[:, 3:4], T.capf[:, 4:5], ["capH", "capJ"]
        S4, V4 = STEP4[last]
        v4 = V4[-1][1]
        spread(zt4, zt4k, S4)
        act(T.t3[:, L:2 * L], z4, ID, [z4k] + cap4k, ["t4"], bias=cap4, scale=-1.0)
        pieces(T.th[:, W:W + v4], T.t3[:, L:L + v4 // 16], "t4", TH4, G4[r])
        act(T.fc[:, 4:5], F4, ID, [F4k], ["fc4"], bias=16.0, scale=-1.0)
        act(T.off[:], T.onS[:, L * last:L * last + L], ID, ["onS", "fc4"], ["off"], scale=T.fc[:, 4:5])
        for a, b in V4:
            tt(T.bb[:, a:b], (win, T.Vl[:, r * L + a // 16:r * L + b // 16]), T.th[:, W + a:W + b], ALU.is_gt,
               [wk, "vl" + rs] + TH4, cols("bb", a, b))
        for n, (a, b) in enumerate(S4):
            o = T.PT[:, 512 * n:512 * n + b - a]
            act(T.xs[:, a:b], (win, T.Vl[:, r * L + a // 16:r * L + b // 16]), ID, [wk, "vl" + rs] + cap4k, cols("xs", a, b), bias=cap4b)
            mm(o, T.idb[:], T.xs[:, a:b], ["idb"] + cols("xs", a, b), "B%d" % n)
            act(T.bb[:, a:b], o, SIGN, ["B%d" % n], cols("bb", a, b), bias=-0.5)
        for h in range(2):
            pk, bk, c = (T.P6, T.P7)[h][:, 0:64], "B%d" % (6 + h), slice(128 * h, 128 * h + 128)
            if [1 for a, b in S4 if a // 1024 == h]:
                mm(pk, T.idb[:], T.off[:, 64 * h:64 * h + 64], ["idb", "off"], bk)
            for k in range(16):
                mm(pk, wband(T.WB, k), T.bb[:, 1024 * h + k:1024 * h + 1024:16], ["WB"] + cols("bb", 1024 * h, 1024 * h + 1024), bk)
            ts(T.TK[:, 128 * h + 1:128 * h + 128:2], pk, F4, ALU.is_lt, [bk, F4k, "TK%d" % h], ["TK%d" % h])
            n0, tnk = (r + 1) * 256 + 128 * h, "Tn%d%d" % (r + 1, h)
            scan(T.Tn[:, n0:n0 + 128], T.TK[:, c], T.DA[:, r * 256 + 128 * h:r * 256 + 128 * h + 128], ALU.mult, ALU.add,
                 ["TK%d" % h, "da" + rs], [tnk])
            if last:
                cp(T.To[:, 64 * h:64 * h + 64], T.Tn[:, n0 + 1:n0 + 128:2], [tnk], ["To%d" % h])
            else:
                c0 = (r + 1) * L + 64 * h
                cp(T.Tc[:, c0:c0 + 64], (T.Tn[:, n0:n0 + 128], T.cP1[:, 0:4]), [tnk, "cP1"], ["tc%d%d" % (r + 1, h)])
    dma("Y", "ytraj", T.To[:], ["To0", "To1"], ["ytraj"], LOAD)
    op("Y", None, ["ysect", "yamt", "ytraj"], ())
    for r in range(RO):
        for q, lines in list(CHAINS.items()) + (list(CHAINS0.items()) if r == 0 else []):
            for words in lines:
                chain(r, q, words)
    return ops, eng, total["sent"]


def rank_program(g, core, T, topo):
    if T.rank_of(core) is None:
        helper_program(g, core, T, topo)
        return
    ops, eng, sent = record(g, core, T, topo)
    order = lay_out(ops)

    def token(i):
        o = ops[i]
        return o["ext"] if o["ext"] else ("q" + o["q"], o["n"])

    known = {q: {} for q in eng}
    rankof, plan, place, ends = {q: 0 for q in eng}, [], {}, {}
    for n, i in enumerate(order):
        o = ops[i]
        place[i] = n
        if o["q"] == "X":
            o["know"] = {}
            continue
        if o["group"] is not None:
            ends[o["group"]] = (ends.get(o["group"], (i, i))[0], i)
        if not o["ext"]:
            rankof[o["q"]] += 1
            o["n"] = rankof[o["q"]]
        kn, need = known[o["q"]], []
        for d in sorted(o["deps"], key=lambda x: -place[x]):
            sem, n = token(d)
            if sem == "-" or kn.get(sem, 0) >= n:
                continue
            need.append(d)
            kn[sem] = n
            for k2, v2 in ops[d]["know"].items():
                if kn.get(k2, 0) < v2:
                    kn[k2] = v2
        o["know"] = dict(kn)
        plan.append((i, need))
    wanted = set(d for _, need in plan for d in need)
    count, val = {q: 0 for q in eng}, {}
    for i, need in plan:
        o = ops[i]
        for d in need:
            if ops[d]["ext"]:
                eng[o["q"]].wait_ge(T.sem[ops[d]["ext"][0]], ops[d]["ext"][1])
            else:
                eng[o["q"]].wait_ge(T.sem["q" + ops[d]["q"]], val[d])
        if o["fn"] is None:
            continue
        ins = o["fn"]() if o["group"] is None else o["fn"](ends[o["group"]][0] == i, ends[o["group"]][1] == i)
        if o["ext"]:
            if o["ext"][0] != "-":
                ins.then_inc(T.sem[o["ext"][0]], o["ext"][1])
        elif i in wanted:
            count[o["q"]] += 1
            val[i] = count[o["q"]]
            ins.then_inc(T.sem["q" + o["q"]], 1)
    g.wait_ge(T.sem.sent, sent)
